import numpy as np
import ml_dtypes


def mxq(x, axis, fmt="e4m3"):
    dtype, down = {"e4m3": (ml_dtypes.float8_e4m3fn, 7), "e5m2": (ml_dtypes.float8_e5m2, 14)}[fmt]
    v = np.moveaxis(np.asarray(x, np.float32).astype(ml_dtypes.bfloat16).astype(np.float64), axis, -1)
    blocks = v.reshape(v.shape[:-1] + (-1, 32))
    amax = np.abs(blocks).max(-1, keepdims=True)
    byte = np.maximum(np.where(amax > 0, np.frexp(amax)[1] - 1 + 127, 0) - down, 1)
    scale = np.exp2(byte - 127.0)
    codes = (blocks / scale).astype(np.float32).astype(dtype).astype(np.float64)
    return np.moveaxis((codes * scale).reshape(v.shape), -1, axis)


WIDE = False


def mx_kscale(k):
    if not WIDE:
        return np.ones(k)
    levels = np.array([10, -10, 5, -5, 0])
    if k % 512:
        return np.exp2(np.random.permutation(np.resize(levels, k // 32))).repeat(32)
    a = np.empty((k // 512, 16))
    for p in range(k // 512):
        a[p, :8] = np.random.permutation(np.resize(levels, 8))
        for g in range(8):
            far = levels[np.abs(levels - a[p, g]) >= 10]
            a[p, g + 8] = far[np.random.randint(len(far))]
    return np.exp2(a.ravel()).repeat(32)


def f64(x):
    return np.asarray(x).astype(np.float64)


def striped(idx):
    return np.tile(np.asarray(idx).reshape(-1, 16).T, (8, 1)).astype(np.uint16)


def unstriped(offs):
    return offs[:16].T.reshape(-1).astype(np.int64)


E2M1 = np.array([0.0, 0.5, 1.0, 1.5, 2.0, 3.0, 4.0, 6.0, -0.0, -0.5, -1.0, -1.5, -2.0, -3.0, -4.0, -6.0])


def pack_weight(w, fmt):
    k, n = w.shape
    w = f64(np.asarray(w, np.float32).astype(ml_dtypes.bfloat16)).reshape(k // 32, 32, n)
    amax = np.abs(w).max(1)
    if fmt == "e4m3":
        byte = np.frexp(amax)[1] - 1 + 127 - 7
    else:
        mant, ex = np.frexp(amax / 6.0)
        byte = np.where(mant > 0.5, ex, ex - 1) + 127
    byte = np.clip(np.where(amax > 0, byte, 1), 1, 254)
    scaled = (w * np.exp2(127.0 - byte)[:, None, :]).reshape(k, n).astype(np.float32)
    by_word = np.ascontiguousarray(scaled.reshape(k // 512, 128, 4, n).transpose(0, 1, 3, 2))
    if fmt == "e4m3":
        words = by_word.astype(ml_dtypes.float8_e4m3fn).view(np.uint8)
    else:
        c = by_word.astype(ml_dtypes.float4_e2m1fn).view(np.uint8) & 0xF
        words = (c[..., 0::2] | (c[..., 1::2] << 4)).reshape(k // 512, 128, 2 * n)
    return np.ascontiguousarray(words), np.ascontiguousarray(byte.astype(np.uint8).reshape(k // 512, 16, n))


def unpack_weight(words, scales, fmt):
    g, _, n = scales.shape
    words = np.ascontiguousarray(words).reshape(g, 128, n, -1)
    if fmt == "e4m3":
        vals = words.view(ml_dtypes.float8_e4m3fn).astype(np.float64)
    else:
        nib = np.empty((g, 128, n, 4), np.uint8)
        nib[..., 0::2] = words & 0xF
        nib[..., 1::2] = words >> 4
        vals = E2M1[nib]
    vals = vals * np.repeat(np.exp2(scales.astype(np.float64) - 127.0), 8, axis=1)[..., None]
    return vals.transpose(0, 1, 3, 2).reshape(g * 512, n)


B, N, T, D, DV, NQ = 1, 1024, 2048, 1024, 256, 128
PAGE = 32


def setup_inputs():
    n = np.random.standard_normal
    pages = np.random.permutation(T // PAGE)[:B * N // PAGE]
    idx = (pages[:, None] * PAGE + np.arange(PAGE)[None, :]).reshape(-1)
    s = mx_kscale(D)[:, None]
    u = np.ones(T)
    u[idx] = mx_kscale(B * N)
    r = np.random.uniform(0.5, 2.0, T)
    k = n((D, T)) / s
    v = n((DV, T)) / (u * r)
    kp = pack_weight(k, "e2m1")
    return {
        "qT": (n((B, D, NQ)) * s * (0.80 / np.sqrt(D))).astype(np.float32),
        "k_words": np.ascontiguousarray(kp[0].reshape(D // 1024, 2, 128, T, 2).transpose(0, 2, 3, 1, 4)).reshape(D // 1024, 128, T, 4),
        "k_scales": kp[1],
        "vT": v.astype(np.float32),
        "vs": np.tile(u * r, (128, 1)).astype(np.float32),
        "kb": np.tile(n(T), (128, 1)).astype(np.float32),
        "offs": striped(idx),
    }


def reference(qT, k_words, k_scales, vT, vs, kb, offs):
    idx = unstriped(offs)
    k = unpack_weight(k_words.reshape(D // 1024, 128, T, 2, 2).transpose(0, 3, 1, 2, 4).reshape(D // 512, 128, 2 * T), k_scales, "e2m1")
    v = f64(vT)
    pick = lambda x: x[:, idx].reshape(x.shape[0], B, N).transpose(1, 0, 2)
    q = f64(qT)
    score = mxq(q, 1, "e4m3").transpose(0, 2, 1) @ pick(k)
    score = score + pick(f64(kb))[:, :1, :]
    m = score.max(-1, keepdims=True)
    p = np.exp(score - m)
    total = p.sum(-1, keepdims=True)
    w = p * pick(f64(vs))[:, :1, :]
    y = mxq(w, 2, "e4m3") @ mxq(pick(v).transpose(0, 2, 1), 1, "e4m3")
    y = y / total
    return y

@@ -1,0 +1,220 @@
+from contextlib import ExitStack
+
+import concourse.mybir as mybir
+from concourse.masks import make_identity
+
+F32 = mybir.dt.float32
+BF16 = mybir.dt.bfloat16
+I32 = mybir.dt.int32
+U32 = mybir.dt.uint32
+U16 = mybir.dt.uint16
+U8 = mybir.dt.uint8
+FP8X4 = mybir.dt.float8_e4m3fn_x4
+FP4X4 = mybir.dt.float4_e2m1fn_x4
+ACT = mybir.ActivationFunctionType
+ALU = mybir.AluOpType
+
+P = 128
+N, T, D, DV, NQ = 1024, 2048, 1024, 256, 128
+PASS = 512
+G = N // PASS
+LIVE = P - 1
+
+FLOPS = 2 * NQ * N * (D + DV)
+BYTES = 4 * D * NQ + 4 * P * T + 32 * T + 4 * DV * T + 2 * 4 * T + 2 * N + 4 * NQ * DV
+
+
+def tile_attend_bias_kernel(tc, qT, k_words, k_scales, vT, vs, kb, offs, out):
+    nc = tc.nc
+    with ExitStack() as ctx:
+        sb = ctx.enter_context(tc.tile_pool(name="sb", bufs=1))
+        ps = ctx.enter_context(tc.psum_pool(name="ps", bufs=1))
+
+        def bank(tag, name):
+            return ps.tile([P, 4, P], F32, tag=tag, name=name)
+
+        offsets = sb.tile([P, N // 16], U16, name="offsets")
+        nc.sync.dma_start(offsets[:], offs)
+
+        def listed(g):
+            return offsets[:, g * (PASS // 16) : (g + 1) * (PASS // 16)]
+
+        ks_pool = sb.tile([P, T], U8, name="ks_pool", align_bytes=64)
+        nc.vector.memset(ks_pool[:].bitcast(I32), 0)
+        kb_pool = sb.tile([P, T], F32, name="kb_pool")
+        vs_pool = sb.tile([P, T], F32, name="vs_pool")
+        nc.sync.dma_start(kb_pool[LIVE:P, :], kb[0:1, :])
+        nc.sync.dma_start(vs_pool[LIVE:P, :], vs[0:1, :])
+        for quad in range(4):
+            nc.sync.dma_start(
+                ks_pool[32 * quad : 32 * quad + 8, :].bitcast(I32),
+                k_scales[:, 4 * quad : 4 * quad + 4, :].bitcast(I32),
+            )
+        kw_pool = sb.tile([P, T], I32, name="kw_pool")
+        nc.sync.dma_start(kw_pool[:], k_words[0].rearrange("p t b -> p (t b)").bitcast(I32))
+        q_raw = sb.tile([P, 2, 4, NQ], F32, name="q_raw")
+        nc.sync.dma_start(q_raw[:], qT[0].rearrange("(o p j) w -> p o j w", o=2, j=4))
+        v_pool = [sb.tile([P, T], F32, name=f"v_pool{h}") for h in range(2)]
+        for h in range(2):
+            nc.sync.dma_start(v_pool[h][:], vT[h * P : (h + 1) * P, :])
+
+        warm = sb.tile([P, 1], F32, name="warm")
+        ident = sb.tile([P, P], F32, name="ident")
+        make_identity(nc, ident[:])
+        nc.scalar.activation(warm[:], ident[:, 0:1], ACT.Exp)
+
+        nc.vector.memset(kb_pool[0:LIVE, :], 0.0)
+        nc.vector.memset(vs_pool[0:LIVE, :], 0.0)
+        ks1 = sb.tile([P, N], U8, name="ks1", align_bytes=64)
+        nc.vector.memset(ks1[:].bitcast(I32), 0)
+
+        ks0 = sb.tile([P, N], U8, name="ks0", align_bytes=64)
+        nc.vector.tensor_copy(ks0[:], ks_pool[:].indirect(offsets[:]))
+        nc.sync.dma_start(ks1[0:112, :].bitcast(I32), ks0[4:116, :].bitcast(I32))
+        k_sc = [ks0, ks1]
+
+        kb_g = sb.tile([P, N], F32, name="kb_g")
+        nc.vector.tensor_copy(kb_g[:], kb_pool[:].indirect(offsets[:]))
+        kb_col = sb.tile([P, G, 4], F32, name="kb_col")
+        for g in range(G):
+            turned = bank(f"a{g}", f"kb_turned{g}")
+            for b in range(4):
+                c0 = g * PASS + b * P
+                nc.tensor.transpose(turned[:, b, :], kb_g[:, c0 : c0 + P], ident[:])
+            nc.scalar.copy(kb_col[:, g, :], turned[:, :, LIVE])
+
+        kw_g = [sb.tile([P, PASS], I32, name=f"kw_g{g}") for g in range(G)]
+        k_codes = [sb.tile([P, 2, 2 * PASS], U8, name=f"k_codes{g}", align_bytes=64) for g in range(G)]
+        for g in range(G):
+            nc.vector.tensor_copy(kw_g[g][:].bitcast(U32), kw_pool[:].bitcast(U32).indirect(listed(g)))
+
+        q_bf = sb.tile([P, 2, NQ, 4], BF16, name="q_bf", align_bytes=64)
+        nc.scalar.activation(q_bf[:], q_raw[:].rearrange("p o j w -> p o w j"), ACT.Copy)
+        q_codes = sb.tile([P, 2 * NQ], U32, name="q_codes", align_bytes=64)
+        q_sc = sb.tile([P, 2 * NQ], U8, name="q_sc", align_bytes=64)
+
+        def part_words(g):
+            nc.vector.tensor_copy(
+                k_codes[g][:].bitcast(U16), kw_g[g][:].bitcast(U16).rearrange("p (n o) -> p o n", o=2)
+            )
+
+        part_words(0)
+        nc.vector.quantize_mx(
+            out=q_codes[:].bitcast(FP8X4), scales=q_sc[:], in_=q_bf[:].rearrange("p o w j -> p (o w j)")
+        )
+        part_words(1)
+
+        s_t = sb.tile([P, G, 4, NQ], F32, name="s_t")
+        neg_s = sb.tile([P, G, 4, P], F32, name="neg_s")
+        neg_m = [sb.tile([P, 1], F32, name=f"neg_m{g}") for g in range(G)]
+        raw = []
+        for g in range(G):
+            raw.append(bank(f"b{g}", f"raw{g}"))
+            for b in range(4):
+                for o in range(2):
+                    c0 = g * PASS + b * P
+                    nc.tensor.matmul_mx(
+                        out=raw[g][:, b, :],
+                        lhsT=k_codes[g][:, o, 2 * b * P : 2 * (b + 1) * P].bitcast(FP4X4),
+                        lhsT_scale=k_sc[o][:, c0 : c0 + P],
+                        rhs=q_codes[:, o * NQ : (o + 1) * NQ].bitcast(FP8X4),
+                        rhs_scale=q_sc[:, o * NQ : (o + 1) * NQ],
+                        start=(o == 0),
+                        stop=(o == 1),
+                    )
+        for g in range(G):
+            for b in range(4):
+                nc.scalar.activation(s_t[:, g, b, :], raw[g][:, b, :], ACT.Identity, bias=kb_col[:, g, b : b + 1])
+
+        vs_g = sb.tile([P, N], F32, name="vs_g")
+        nc.vector.tensor_copy(vs_g[:], vs_pool[:].indirect(offsets[:]))
+
+        for g in range(G):
+            scores = bank(f"a{g}", f"scores{g}")
+            for b in range(4):
+                nc.tensor.transpose(scores[:, b, :], s_t[:, g, b, :], ident[:])
+            nc.vector.tensor_scalar(
+                neg_s[:, g, :, :],
+                scores[:].rearrange("q b c -> q (b c)").rearrange("q (p t) -> q t p", t=4),
+                -1.0,
+                neg_m[0][:] if g else None,
+                ALU.mult,
+                ALU.min,
+                accum_out=neg_m[g][:],
+            )
+
+        vs_col = sb.tile([P, G, 4], F32, name="vs_col")
+        for g in range(G):
+            turned = bank(f"c{g}", f"vs_turned{g}")
+            for t in range(4):
+                nc.tensor.transpose(turned[:, t, :], vs_g[:, g * PASS + t : (g + 1) * PASS : 4], ident[:])
+            nc.scalar.copy(vs_col[:, g, :], turned[:, :, LIVE])
+
+        p_sb = sb.tile([P, G, 4, P], F32, name="p_sb")
+        l_part = [sb.tile([P, 1], F32, name=f"l_part{g}") for g in range(G)]
+        for g in range(G):
+            nc.scalar.activation(
+                p_sb[:, g, :, :], neg_s[:, g, :, :], ACT.Exp, bias=neg_m[G - 1][:], scale=-1.0, accum_out=l_part[g][:]
+            )
+
+        v_bf = sb.tile([P, T], BF16, name="v_bf")
+        nc.scalar.activation(v_bf[:], v_pool[0][:], ACT.Copy)
+        v_g = [sb.tile([P, G, 2, P, 2], BF16, name=f"v_g{h}") for h in range(2)]
+        for g in range(G):
+            nc.scalar.activation(v_g[0][:, g].rearrange("e u p i -> e p u i"), v_bf[:].indirect(listed(g)), ACT.Copy)
+        for g in range(G):
+            nc.vector.tensor_copy(v_g[1][:, g].rearrange("e u p i -> e p u i"), v_pool[1][:].indirect(listed(g)))
+
+        v_il = sb.tile([P, G, DV, 4], BF16, name="v_il", align_bytes=64)
+        v_codes = sb.tile([P, G, DV], U32, name="v_codes", align_bytes=64)
+        v_sc = sb.tile([P, G, DV], U8, name="v_sc", align_bytes=64)
+        for g in range(G):
+            turned = bank(f"c{g}", f"v_turned{g}")
+            for h in range(2):
+                words = v_g[h][:, g].rearrange("e u p i -> e u (p i)").bitcast(F32)
+                for u in range(2):
+                    nc.tensor.transpose(turned[:, 2 * h + u, :], words[:, u, :], ident[:])
+            nc.scalar.copy(
+                v_il[:, g].bitcast(F32).rearrange("p (h e) u -> p h e u", h=2),
+                turned[:].rearrange("p (h u) e -> p h e u", h=2),
+            )
+            nc.vector.quantize_mx(
+                out=v_codes[:, g, :].bitcast(FP8X4), scales=v_sc[:, g, :], in_=v_il[:, g].rearrange("p e t -> p (e t)")
+            )
+
+        w_il = sb.tile([P, G, NQ, 4], BF16, name="w_il", align_bytes=64)
+        w_codes = sb.tile([P, G, NQ], U32, name="w_codes", align_bytes=64)
+        w_sc = sb.tile([P, G, NQ], U8, name="w_sc", align_bytes=64)
+        for g in range(G):
+            turned = bank(f"b{g}", f"p_turned{g}")
+            for t in range(4):
+                nc.tensor.transpose(turned[:, t, :], p_sb[:, g, t, :], ident[:])
+            nc.vector.tensor_tensor(
+                w_il[:, g],
+                turned[:].rearrange("p t q -> p q t"),
+                vs_col[:, g, :].unsqueeze(1).to_broadcast([P, NQ, 4]),
+                ALU.mult,
+            )
+        l_sum = sb.tile([P, 1], F32, name="l_sum")
+        l_inv = sb.tile([P, 1], F32, name="l_inv")
+        nc.vector.tensor_tensor(l_sum[:], l_part[0][:], l_part[1][:], ALU.add)
+        for g in range(G):
+            nc.vector.quantize_mx(
+                out=w_codes[:, g, :].bitcast(FP8X4), scales=w_sc[:, g, :], in_=w_il[:, g].rearrange("p q t -> p (q t)")
+            )
+        nc.vector.reciprocal(l_inv[:], l_sum[:])
+
+        y_ps = ps.tile([P, DV], F32, tag="d", name="y_ps")
+        for g in range(G):
+            nc.tensor.matmul_mx(
+                out=y_ps[:],
+                lhsT=w_codes[:, g, :].bitcast(FP8X4),
+                lhsT_scale=w_sc[:, g, :],
+                rhs=v_codes[:, g, :].bitcast(FP8X4),
+                rhs_scale=v_sc[:, g, :],
+                start=(g == 0),
+                stop=(g == G - 1),
+            )
+        y_sb = sb.tile([P, DV], F32, name="y_sb")
+        nc.scalar.activation(y_sb[:], y_ps[:], ACT.Copy, scale=l_inv[:])
+        nc.sync.dma_start(out[0], y_sb[:])

@@ -40,130 +40,162 @@ def tile_attend_bias_kernel(tc, qT, k_words, k_scales, vT, vs, kb, offs, out):
             return offsets[:, g * (PASS // 16) : (g + 1) * (PASS // 16)]
 
         ks_pool = sb.tile([P, T], U8, name="ks_pool", align_bytes=64)
-        nc.vector.memset(ks_pool[:].bitcast(I32), 0)
+        nc.gpsimd.memset(ks_pool[:].bitcast(I32), 0)
         kb_pool = sb.tile([P, T], F32, name="kb_pool")
-        vs_pool = sb.tile([P, T], F32, name="vs_pool")
-        nc.sync.dma_start(kb_pool[LIVE:P, :], kb[0:1, :])
-        nc.sync.dma_start(vs_pool[LIVE:P, :], vs[0:1, :])
         for quad in range(4):
             nc.sync.dma_start(
                 ks_pool[32 * quad : 32 * quad + 8, :].bitcast(I32),
                 k_scales[:, 4 * quad : 4 * quad + 4, :].bitcast(I32),
             )
-        kw_pool = sb.tile([P, T], I32, name="kw_pool")
-        nc.sync.dma_start(kw_pool[:], k_words[0].rearrange("p t b -> p (t b)").bitcast(I32))
+        vs_pool = sb.tile([P, T], F32, name="vs_pool")
+        nc.sync.dma_start(vs_pool[LIVE:P, :], vs[0:1, :])
+        nc.sync.dma_start(kb_pool[LIVE:P, :], kb[0:1, :])
+        v_raw = [[sb.tile([P, T // 2], F32, name=f"v_raw{h}{c}", tag=f"stage{h}{c}") for c in range(2)] for h in range(2)]
+
+        def load_values(h):
+            for c in range(2):
+                nc.sync.dma_start(v_raw[h][c][:], vT[h * P : (h + 1) * P, c * (T // 2) : (c + 1) * (T // 2)])
+
+        load_values(0)
         q_raw = sb.tile([P, 2, 4, NQ], F32, name="q_raw")
         nc.sync.dma_start(q_raw[:], qT[0].rearrange("(o p j) w -> p o j w", o=2, j=4))
-        v_pool = [sb.tile([P, T], F32, name=f"v_pool{h}") for h in range(2)]
-        for h in range(2):
-            nc.sync.dma_start(v_pool[h][:], vT[h * P : (h + 1) * P, :])
+        kw_pool = sb.tile([P, T], I32, name="kw_pool")
+        nc.sync.dma_start(kw_pool[:], k_words[0].rearrange("p t b -> p (t b)").bitcast(I32))
 
         warm = sb.tile([P, 1], F32, name="warm")
         ident = sb.tile([P, P], F32, name="ident")
+        nc.gpsimd.memset(kb_pool[0:LIVE, :], 0.0)
         make_identity(nc, ident[:])
-        nc.scalar.activation(warm[:], ident[:, 0:1], ACT.Exp)
+        nc.vector.memset(warm[:], 0.0)
+        nc.scalar.activation(warm[:], warm[:], ACT.Exp)
 
-        nc.vector.memset(kb_pool[0:LIVE, :], 0.0)
-        nc.vector.memset(vs_pool[0:LIVE, :], 0.0)
         ks1 = sb.tile([P, N], U8, name="ks1", align_bytes=64)
-        nc.vector.memset(ks1[:].bitcast(I32), 0)
+        nc.gpsimd.memset(ks1[:].bitcast(I32), 0)
+        nc.vector.memset(vs_pool[0:LIVE, 0 : T // 2 - 1], 0.0)
+        nc.vector.memset(vs_pool[0:LIVE, T // 2 - 1 : T], 0.0)
 
         ks0 = sb.tile([P, N], U8, name="ks0", align_bytes=64)
         nc.vector.tensor_copy(ks0[:], ks_pool[:].indirect(offsets[:]))
         nc.sync.dma_start(ks1[0:112, :].bitcast(I32), ks0[4:116, :].bitcast(I32))
+        load_values(1)
         k_sc = [ks0, ks1]
 
         kb_g = sb.tile([P, N], F32, name="kb_g")
         nc.vector.tensor_copy(kb_g[:], kb_pool[:].indirect(offsets[:]))
-        kb_col = sb.tile([P, G, 4], F32, name="kb_col")
+        v_bf = [sb.tile([P, T], BF16, name=f"v_bf{h}", tag=f"v_bf{h}") for h in range(2)]
+        v_g = [[None] * G for h in range(2)]
+
+        def cast_values(h):
+            for c in range(2):
+                nc.scalar.activation(v_bf[h][:, c * (T // 2) : (c + 1) * (T // 2)], v_raw[h][c][:], ACT.Copy)
+
+        def gather_values(h, g, tag):
+            v_g[h][g] = sb.tile([P, 2, P, 2], BF16, name=f"v_g{h}{g}", tag=tag)
+            nc.scalar.activation(
+                v_g[h][g][:].rearrange("e u p i -> e p u i"), v_bf[h][:].indirect(listed(g)), ACT.Copy
+            )
+
+        q_bf = sb.tile([P, 2, NQ, 4], BF16, name="q_bf", align_bytes=64)
+        cast_values(0)
+        nc.scalar.activation(q_bf[:], q_raw[:].rearrange("p o j w -> p o w j"), ACT.Copy)
+        for g in range(G):
+            gather_values(0, g, f"v_g0{g}")
+
+        kb_col = sb.tile([P, G, 4], F32, name="kb_col", tag="v_bf0")
         for g in range(G):
             turned = bank(f"a{g}", f"kb_turned{g}")
             for b in range(4):
                 c0 = g * PASS + b * P
                 nc.tensor.transpose(turned[:, b, :], kb_g[:, c0 : c0 + P], ident[:])
             nc.scalar.copy(kb_col[:, g, :], turned[:, :, LIVE])
+        cast_values(1)
 
-        kw_g = [sb.tile([P, PASS], I32, name=f"kw_g{g}") for g in range(G)]
-        k_codes = [sb.tile([P, 2, 2 * PASS], U8, name=f"k_codes{g}", align_bytes=64) for g in range(G)]
-        for g in range(G):
-            nc.vector.tensor_copy(kw_g[g][:].bitcast(U32), kw_pool[:].bitcast(U32).indirect(listed(g)))
+        chunks = [(0, 512), (512, 256), (768, 256)]
 
-        q_bf = sb.tile([P, 2, NQ, 4], BF16, name="q_bf", align_bytes=64)
-        nc.scalar.activation(q_bf[:], q_raw[:].rearrange("p o j w -> p o w j"), ACT.Copy)
+        def listed_range(start, count):
+            return offsets[:, start // 16 : (start + count) // 16]
+
+        kw_g = [sb.tile([P, n], I32, name=f"kw_g{c}", tag=f"gathered{c}") for c, (s0, n) in enumerate(chunks)]
+        k_codes = [sb.tile([P, 2, 2 * n], U8, name=f"k_codes{c}", align_bytes=64) for c, (s0, n) in enumerate(chunks)]
+
+        def gather_words(c):
+            nc.vector.tensor_copy(kw_g[c][:].bitcast(U32), kw_pool[:].bitcast(U32).indirect(listed_range(*chunks[c])))
+
+        def part_words(c):
+            nc.vector.tensor_copy(
+                k_codes[c][:].bitcast(U16), kw_g[c][:].bitcast(U16).rearrange("p (n o) -> p o n", o=2)
+            )
+
         q_codes = sb.tile([P, 2 * NQ], U32, name="q_codes", align_bytes=64)
         q_sc = sb.tile([P, 2 * NQ], U8, name="q_sc", align_bytes=64)
 
-        def part_words(g):
-            nc.vector.tensor_copy(
-                k_codes[g][:].bitcast(U16), kw_g[g][:].bitcast(U16).rearrange("p (n o) -> p o n", o=2)
-            )
-
+        gather_words(0)
+        gather_words(1)
         part_words(0)
         nc.vector.quantize_mx(
             out=q_codes[:].bitcast(FP8X4), scales=q_sc[:], in_=q_bf[:].rearrange("p o w j -> p (o w j)")
         )
+        gather_words(2)
         part_words(1)
+        part_words(2)
 
-        s_t = sb.tile([P, G, 4, NQ], F32, name="s_t")
+        s_t = sb.tile([P, N // P, NQ], F32, name="s_t", tag="stage11")
         neg_s = sb.tile([P, G, 4, P], F32, name="neg_s")
-        neg_m = [sb.tile([P, 1], F32, name=f"neg_m{g}") for g in range(G)]
-        raw = []
-        for g in range(G):
-            raw.append(bank(f"b{g}", f"raw{g}"))
-            for b in range(4):
+        neg_m = [sb.tile([P, 1], F32, name=f"neg_m{c}") for c in range(len(chunks))]
+        raw_tag = ["b0", "b1", "d"]
+        score_tag = ["a0", "a1", "e"]
+        for c, (start, count) in enumerate(chunks):
+            raw = bank(raw_tag[c], f"raw{c}")
+            for b in range(count // P):
+                c0 = start + b * P
                 for o in range(2):
-                    c0 = g * PASS + b * P
                     nc.tensor.matmul_mx(
-                        out=raw[g][:, b, :],
-                        lhsT=k_codes[g][:, o, 2 * b * P : 2 * (b + 1) * P].bitcast(FP4X4),
+                        out=raw[:, b, :],
+                        lhsT=k_codes[c][:, o, 2 * b * P : 2 * (b + 1) * P].bitcast(FP4X4),
                         lhsT_scale=k_sc[o][:, c0 : c0 + P],
                         rhs=q_codes[:, o * NQ : (o + 1) * NQ].bitcast(FP8X4),
                         rhs_scale=q_sc[:, o * NQ : (o + 1) * NQ],
                         start=(o == 0),
                         stop=(o == 1),
                     )
-        for g in range(G):
-            for b in range(4):
-                nc.scalar.activation(s_t[:, g, b, :], raw[g][:, b, :], ACT.Identity, bias=kb_col[:, g, b : b + 1])
-
-        vs_g = sb.tile([P, N], F32, name="vs_g")
-        nc.vector.tensor_copy(vs_g[:], vs_pool[:].indirect(offsets[:]))
-
-        for g in range(G):
-            scores = bank(f"a{g}", f"scores{g}")
-            for b in range(4):
-                nc.tensor.transpose(scores[:, b, :], s_t[:, g, b, :], ident[:])
+            for b in range(count // P):
+                blk = start // P + b
+                nc.scalar.activation(
+                    s_t[:, blk, :], raw[:, b, :], ACT.Identity, bias=kb_col[:, blk // 4, blk % 4 : blk % 4 + 1]
+                )
+        for c, (start, count) in enumerate(chunks):
+            scores = bank(score_tag[c], f"scores{c}")
+            for b in range(count // P):
+                nc.tensor.transpose(scores[:, b, :], s_t[:, start // P + b, :], ident[:])
+            p0 = (start % PASS) // 4
             nc.vector.tensor_scalar(
-                neg_s[:, g, :, :],
-                scores[:].rearrange("q b c -> q (b c)").rearrange("q (p t) -> q t p", t=4),
+                neg_s[:, start // PASS, :, p0 : p0 + count // 4],
+                scores[:, 0 : count // P, :].rearrange("q b c -> q (b c)").rearrange("q (p t) -> q t p", t=4),
                 -1.0,
-                neg_m[0][:] if g else None,
+                neg_m[c - 1][:] if c else None,
                 ALU.mult,
                 ALU.min,
-                accum_out=neg_m[g][:],
+                accum_out=neg_m[c][:],
             )
 
-        vs_col = sb.tile([P, G, 4], F32, name="vs_col")
+        vs_col = [sb.tile([P, 4], F32, name=f"vs_col{g}") for g in range(G)]
         for g in range(G):
-            turned = bank(f"c{g}", f"vs_turned{g}")
+            vs_g = sb.tile([P, PASS], F32, name=f"vs_g{g}", tag=["gathered0", "stage11"][g])
+            nc.vector.tensor_copy(vs_g[:], vs_pool[:].indirect(listed(g)))
+            turned = bank(f"a{g}", f"vs_turned{g}")
             for t in range(4):
-                nc.tensor.transpose(turned[:, t, :], vs_g[:, g * PASS + t : (g + 1) * PASS : 4], ident[:])
-            nc.scalar.copy(vs_col[:, g, :], turned[:, :, LIVE])
+                nc.tensor.transpose(turned[:, t, :], vs_g[:, t:PASS:4], ident[:])
+            nc.vector.tensor_copy(vs_col[g][:], turned[:, :, LIVE])
 
         p_sb = sb.tile([P, G, 4, P], F32, name="p_sb")
         l_part = [sb.tile([P, 1], F32, name=f"l_part{g}") for g in range(G)]
         for g in range(G):
             nc.scalar.activation(
-                p_sb[:, g, :, :], neg_s[:, g, :, :], ACT.Exp, bias=neg_m[G - 1][:], scale=-1.0, accum_out=l_part[g][:]
+                p_sb[:, g, :, :], neg_s[:, g, :, :], ACT.Exp, bias=neg_m[-1][:], scale=-1.0, accum_out=l_part[g][:]
             )
 
-        v_bf = sb.tile([P, T], BF16, name="v_bf")
-        nc.scalar.activation(v_bf[:], v_pool[0][:], ACT.Copy)
-        v_g = [sb.tile([P, G, 2, P, 2], BF16, name=f"v_g{h}") for h in range(2)]
-        for g in range(G):
-            nc.scalar.activation(v_g[0][:, g].rearrange("e u p i -> e p u i"), v_bf[:].indirect(listed(g)), ACT.Copy)
-        for g in range(G):
-            nc.vector.tensor_copy(v_g[1][:, g].rearrange("e u p i -> e p u i"), v_pool[1][:].indirect(listed(g)))
+        gather_values(1, 0, "v_g10")
+        gather_values(1, 1, "v_g11")
 
         v_il = sb.tile([P, G, DV, 4], BF16, name="v_il", align_bytes=64)
         v_codes = sb.tile([P, G, DV], U32, name="v_codes", align_bytes=64)
@@ -171,10 +203,11 @@ def tile_attend_bias_kernel(tc, qT, k_words, k_scales, vT, vs, kb, offs, out):
         for g in range(G):
             turned = bank(f"c{g}", f"v_turned{g}")
             for h in range(2):
-                words = v_g[h][:, g].rearrange("e u p i -> e u (p i)").bitcast(F32)
+                words = v_g[h][g][:].rearrange("e u p i -> e u (p i)").bitcast(F32)
                 for u in range(2):
                     nc.tensor.transpose(turned[:, 2 * h + u, :], words[:, u, :], ident[:])
-            nc.scalar.copy(
+            copy_out = nc.scalar.copy if g else nc.vector.tensor_copy
+            copy_out(
                 v_il[:, g].bitcast(F32).rearrange("p (h e) u -> p h e u", h=2),
                 turned[:].rearrange("p (h u) e -> p h e u", h=2),
             )
@@ -192,7 +225,7 @@ def tile_attend_bias_kernel(tc, qT, k_words, k_scales, vT, vs, kb, offs, out):
             nc.vector.tensor_tensor(
                 w_il[:, g],
                 turned[:].rearrange("p t q -> p q t"),
-                vs_col[:, g, :].unsqueeze(1).to_broadcast([P, NQ, 4]),
+                vs_col[g][:].unsqueeze(1).to_broadcast([P, NQ, 4]),
                 ALU.mult,
             )
         l_sum = sb.tile([P, 1], F32, name="l_sum")

@@ -41,7 +41,6 @@ def tile_attend_bias_kernel(tc, qT, k_words, k_scales, vT, vs, kb, offs, out):
 
         ks_pool = sb.tile([P, T], U8, name="ks_pool", align_bytes=64)
         nc.gpsimd.memset(ks_pool[:].bitcast(I32), 0)
-        kb_pool = sb.tile([P, T], F32, name="kb_pool")
         for quad in range(4):
             nc.sync.dma_start(
                 ks_pool[32 * quad : 32 * quad + 8, :].bitcast(I32),
@@ -49,26 +48,32 @@ def tile_attend_bias_kernel(tc, qT, k_words, k_scales, vT, vs, kb, offs, out):
             )
         vs_pool = sb.tile([P, T], F32, name="vs_pool")
         nc.sync.dma_start(vs_pool[LIVE:P, :], vs[0:1, :])
+        kb_pool = sb.tile([P, T], F32, name="kb_pool")
         nc.sync.dma_start(kb_pool[LIVE:P, :], kb[0:1, :])
-        v_raw = [[sb.tile([P, T // 2], F32, name=f"v_raw{h}{c}", tag=f"stage{h}{c}") for c in range(2)] for h in range(2)]
+        v_raw = [
+            [sb.tile([P, T // 2], F32, name=f"v_raw{h}{c}", tag=f"v_raw{h}{c}", align_bytes=64) for c in range(2)]
+            for h in range(2)
+        ]
 
-        def load_values(h):
-            for c in range(2):
-                nc.sync.dma_start(v_raw[h][c][:], vT[h * P : (h + 1) * P, c * (T // 2) : (c + 1) * (T // 2)])
+        def columns(c):
+            return slice(c * T // 2, (c + 1) * T // 2)
 
-        load_values(0)
+        def load_values(h, c):
+            nc.sync.dma_start(v_raw[h][c][:], vT[h * P : (h + 1) * P, columns(c)])
+
+        load_values(0, 0)
         q_raw = sb.tile([P, 2, 4, NQ], F32, name="q_raw")
         nc.sync.dma_start(q_raw[:], qT[0].rearrange("(o p j) w -> p o j w", o=2, j=4))
+        load_values(0, 1)
         kw_pool = sb.tile([P, T], I32, name="kw_pool")
         nc.sync.dma_start(kw_pool[:], k_words[0].rearrange("p t b -> p (t b)").bitcast(I32))
 
         warm = sb.tile([P, 1], F32, name="warm")
         ident = sb.tile([P, P], F32, name="ident")
-        nc.gpsimd.memset(kb_pool[0:LIVE, :], 0.0)
-        make_identity(nc, ident[:])
         nc.vector.memset(warm[:], 0.0)
         nc.scalar.activation(warm[:], warm[:], ACT.Exp)
-
+        make_identity(nc, ident[:])
+        nc.gpsimd.memset(kb_pool[0:LIVE, :], 0.0)
         ks1 = sb.tile([P, N], U8, name="ks1", align_bytes=64)
         nc.gpsimd.memset(ks1[:].bitcast(I32), 0)
         nc.vector.memset(vs_pool[0:LIVE, 0 : T // 2 - 1], 0.0)
@@ -77,37 +82,34 @@ def tile_attend_bias_kernel(tc, qT, k_words, k_scales, vT, vs, kb, offs, out):
         ks0 = sb.tile([P, N], U8, name="ks0", align_bytes=64)
         nc.vector.tensor_copy(ks0[:], ks_pool[:].indirect(offsets[:]))
         nc.sync.dma_start(ks1[0:112, :].bitcast(I32), ks0[4:116, :].bitcast(I32))
-        load_values(1)
         k_sc = [ks0, ks1]
-
+        load_values(1, 0)
+        load_values(1, 1)
         kb_g = sb.tile([P, N], F32, name="kb_g")
         nc.vector.tensor_copy(kb_g[:], kb_pool[:].indirect(offsets[:]))
-        v_bf = [sb.tile([P, T], BF16, name=f"v_bf{h}", tag=f"v_bf{h}") for h in range(2)]
-        v_g = [[None] * G for h in range(2)]
+
+        v_bf = [sb.tile([P, T], BF16, name=f"v_bf{h}", tag=f"v_bf{h}", align_bytes=64) for h in range(2)]
+        v_g = [sb.tile([P, G, PASS + 16], BF16, name=f"v_g{h}") for h in range(2)]
 
         def cast_values(h):
             for c in range(2):
-                nc.scalar.activation(v_bf[h][:, c * (T // 2) : (c + 1) * (T // 2)], v_raw[h][c][:], ACT.Copy)
+                nc.scalar.activation(v_bf[h][:, columns(c)], v_raw[h][c][:], ACT.Copy)
 
-        def gather_values(h, g, tag):
-            v_g[h][g] = sb.tile([P, 2, P, 2], BF16, name=f"v_g{h}{g}", tag=tag)
-            nc.scalar.activation(
-                v_g[h][g][:].rearrange("e u p i -> e p u i"), v_bf[h][:].indirect(listed(g)), ACT.Copy
-            )
+        def gather_values(h):
+            nc.scalar.activation(v_g[h][:, :, 0:PASS], v_bf[h][:].indirect(offsets[:]), ACT.Copy)
 
-        q_bf = sb.tile([P, 2, NQ, 4], BF16, name="q_bf", align_bytes=64)
         cast_values(0)
+        q_bf = sb.tile([P, 2, NQ, 4], BF16, name="q_bf", align_bytes=64)
         nc.scalar.activation(q_bf[:], q_raw[:].rearrange("p o j w -> p o w j"), ACT.Copy)
-        for g in range(G):
-            gather_values(0, g, f"v_g0{g}")
+        gather_values(0)
 
-        kb_col = sb.tile([P, G, 4], F32, name="kb_col", tag="v_bf0")
+        kb_col = sb.tile([P, N // P], F32, name="kb_col", tag="v_bf0", align_bytes=64)
         for g in range(G):
             turned = bank(f"a{g}", f"kb_turned{g}")
             for b in range(4):
                 c0 = g * PASS + b * P
                 nc.tensor.transpose(turned[:, b, :], kb_g[:, c0 : c0 + P], ident[:])
-            nc.scalar.copy(kb_col[:, g, :], turned[:, :, LIVE])
+            nc.scalar.copy(kb_col[:, 4 * g : 4 * g + 4], turned[:, :, LIVE])
         cast_values(1)
 
         chunks = [(0, 512), (512, 256), (768, 256)]
@@ -115,7 +117,7 @@ def tile_attend_bias_kernel(tc, qT, k_words, k_scales, vT, vs, kb, offs, out):
         def listed_range(start, count):
             return offsets[:, start // 16 : (start + count) // 16]
 
-        kw_g = [sb.tile([P, n], I32, name=f"kw_g{c}", tag=f"gathered{c}") for c, (s0, n) in enumerate(chunks)]
+        kw_g = [sb.tile([P, n], I32, name=f"kw_g{c}", tag=f"gathered{c}", align_bytes=64) for c, (s0, n) in enumerate(chunks)]
         k_codes = [sb.tile([P, 2, 2 * n], U8, name=f"k_codes{c}", align_bytes=64) for c, (s0, n) in enumerate(chunks)]
 
         def gather_words(c):
@@ -139,7 +141,7 @@ def tile_attend_bias_kernel(tc, qT, k_words, k_scales, vT, vs, kb, offs, out):
         part_words(1)
         part_words(2)
 
-        s_t = sb.tile([P, N // P, NQ], F32, name="s_t", tag="stage11")
+        s_t = sb.tile([P, N // P, NQ], F32, name="s_t", tag="s_t", align_bytes=32)
         neg_s = sb.tile([P, G, 4, P], F32, name="neg_s")
         neg_m = [sb.tile([P, 1], F32, name=f"neg_m{c}") for c in range(len(chunks))]
         raw_tag = ["b0", "b1", "d"]
@@ -158,11 +160,13 @@ def tile_attend_bias_kernel(tc, qT, k_words, k_scales, vT, vs, kb, offs, out):
                         start=(o == 0),
                         stop=(o == 1),
                     )
-            for b in range(count // P):
-                blk = start // P + b
-                nc.scalar.activation(
-                    s_t[:, blk, :], raw[:, b, :], ACT.Identity, bias=kb_col[:, blk // 4, blk % 4 : blk % 4 + 1]
-                )
+            b0, nb = start // P, count // P
+            nc.vector.tensor_tensor(
+                s_t[:, b0 : b0 + nb, :],
+                raw[:, 0:nb, :],
+                kb_col[:, b0 : b0 + nb].unsqueeze(2).to_broadcast([P, nb, NQ]),
+                ALU.add,
+            )
         for c, (start, count) in enumerate(chunks):
             scores = bank(score_tag[c], f"scores{c}")
             for b in range(count // P):
@@ -180,39 +184,19 @@ def tile_attend_bias_kernel(tc, qT, k_words, k_scales, vT, vs, kb, offs, out):
 
         vs_col = [sb.tile([P, 4], F32, name=f"vs_col{g}") for g in range(G)]
         for g in range(G):
-            vs_g = sb.tile([P, PASS], F32, name=f"vs_g{g}", tag=["gathered0", "stage11"][g])
+            vs_g = sb.tile([P, PASS], F32, name=f"vs_g{g}", tag=["gathered0", "s_t"][g], align_bytes=[64, 32][g])
             nc.vector.tensor_copy(vs_g[:], vs_pool[:].indirect(listed(g)))
-            turned = bank(f"a{g}", f"vs_turned{g}")
+            turned = bank(["d", "a1"][g], f"vs_turned{g}")
             for t in range(4):
                 nc.tensor.transpose(turned[:, t, :], vs_g[:, t:PASS:4], ident[:])
             nc.vector.tensor_copy(vs_col[g][:], turned[:, :, LIVE])
 
-        p_sb = sb.tile([P, G, 4, P], F32, name="p_sb")
+        gather_values(1)
+        p_sb = sb.tile([P, G, 4, P], F32, name="p_sb", tag="v_bf1", align_bytes=64)
         l_part = [sb.tile([P, 1], F32, name=f"l_part{g}") for g in range(G)]
         for g in range(G):
             nc.scalar.activation(
                 p_sb[:, g, :, :], neg_s[:, g, :, :], ACT.Exp, bias=neg_m[-1][:], scale=-1.0, accum_out=l_part[g][:]
-            )
-
-        gather_values(1, 0, "v_g10")
-        gather_values(1, 1, "v_g11")
-
-        v_il = sb.tile([P, G, DV, 4], BF16, name="v_il", align_bytes=64)
-        v_codes = sb.tile([P, G, DV], U32, name="v_codes", align_bytes=64)
-        v_sc = sb.tile([P, G, DV], U8, name="v_sc", align_bytes=64)
-        for g in range(G):
-            turned = bank(f"c{g}", f"v_turned{g}")
-            for h in range(2):
-                words = v_g[h][g][:].rearrange("e u p i -> e u (p i)").bitcast(F32)
-                for u in range(2):
-                    nc.tensor.transpose(turned[:, 2 * h + u, :], words[:, u, :], ident[:])
-            copy_out = nc.scalar.copy if g else nc.vector.tensor_copy
-            copy_out(
-                v_il[:, g].bitcast(F32).rearrange("p (h e) u -> p h e u", h=2),
-                turned[:].rearrange("p (h u) e -> p h e u", h=2),
-            )
-            nc.vector.quantize_mx(
-                out=v_codes[:, g, :].bitcast(FP8X4), scales=v_sc[:, g, :], in_=v_il[:, g].rearrange("p e t -> p (e t)")
             )
 
         w_il = sb.tile([P, G, NQ, 4], BF16, name="w_il", align_bytes=64)
@@ -228,13 +212,30 @@ def tile_attend_bias_kernel(tc, qT, k_words, k_scales, vT, vs, kb, offs, out):
                 vs_col[g][:].unsqueeze(1).to_broadcast([P, NQ, 4]),
                 ALU.mult,
             )
-        l_sum = sb.tile([P, 1], F32, name="l_sum")
-        l_inv = sb.tile([P, 1], F32, name="l_inv")
-        nc.vector.tensor_tensor(l_sum[:], l_part[0][:], l_part[1][:], ALU.add)
         for g in range(G):
             nc.vector.quantize_mx(
                 out=w_codes[:, g, :].bitcast(FP8X4), scales=w_sc[:, g, :], in_=w_il[:, g].rearrange("p q t -> p (q t)")
             )
+        v_il = sb.tile([P, G, 2, P, 4], BF16, name="v_il", tag="v_raw11", align_bytes=64)
+        v_codes = sb.tile([P, G, DV], U32, name="v_codes", align_bytes=64)
+        v_sc = sb.tile([P, G, DV], U8, name="v_sc", align_bytes=64)
+        for h in range(2):
+            turned = bank(f"c{h}", f"v_turned{h}")
+            for g in range(G):
+                words = v_g[h][:, g, 0:PASS].bitcast(F32)
+                for u in range(2):
+                    nc.tensor.transpose(turned[:, 2 * g + u, :], words[:, u : PASS // 2 : 2], ident[:])
+            nc.scalar.copy(v_il[:, :, h].bitcast(F32), turned[:].rearrange("p (g u) e -> p g e u", g=G))
+            for g in range(G):
+                nc.vector.quantize_mx(
+                    out=v_codes[:, g, h * P : (h + 1) * P].bitcast(FP8X4),
+                    scales=v_sc[:, g, h * P : (h + 1) * P],
+                    in_=v_il[:, g, h].rearrange("p e t -> p (e t)"),
+                )
+
+        l_sum = sb.tile([P, 1], F32, name="l_sum")
+        l_inv = sb.tile([P, 1], F32, name="l_inv")
+        nc.vector.tensor_tensor(l_sum[:], l_part[0][:], l_part[1][:], ALU.add)
         nc.vector.reciprocal(l_inv[:], l_sum[:])
 
         y_ps = ps.tile([P, DV], F32, tag="d", name="y_ps")

@@ -36,11 +36,8 @@ def tile_attend_bias_kernel(tc, qT, k_words, k_scales, vT, vs, kb, offs, out):
         offsets = sb.tile([P, N // 16], U16, name="offsets")
         nc.sync.dma_start(offsets[:], offs)
 
-        def listed(g):
-            return offsets[:, g * (PASS // 16) : (g + 1) * (PASS // 16)]
-
         ks_pool = sb.tile([P, T], U8, name="ks_pool", align_bytes=64)
-        nc.gpsimd.memset(ks_pool[:].bitcast(I32), 0)
+        nc.vector.memset(ks_pool[:].bitcast(I32), 0)
         for quad in range(4):
             nc.sync.dma_start(
                 ks_pool[32 * quad : 32 * quad + 8, :].bitcast(I32),
@@ -70,14 +67,12 @@ def tile_attend_bias_kernel(tc, qT, k_words, k_scales, vT, vs, kb, offs, out):
 
         warm = sb.tile([P, 1], F32, name="warm")
         ident = sb.tile([P, P], F32, name="ident")
-        nc.vector.memset(warm[:], 0.0)
-        nc.scalar.activation(warm[:], warm[:], ACT.Exp)
         make_identity(nc, ident[:])
-        nc.gpsimd.memset(kb_pool[0:LIVE, :], 0.0)
+        nc.scalar.activation(warm[:], ident[:, 0:1], ACT.Exp)
+        nc.vector.memset(kb_pool[0:LIVE, :], 0.0)
         ks1 = sb.tile([P, N], U8, name="ks1", align_bytes=64)
-        nc.gpsimd.memset(ks1[:].bitcast(I32), 0)
-        nc.vector.memset(vs_pool[0:LIVE, 0 : T // 2 - 1], 0.0)
-        nc.vector.memset(vs_pool[0:LIVE, T // 2 - 1 : T], 0.0)
+        nc.vector.memset(ks1[:].bitcast(I32), 0)
+        nc.vector.memset(vs_pool[0:LIVE, :], 0.0)
 
         ks0 = sb.tile([P, N], U8, name="ks0", align_bytes=64)
         nc.vector.tensor_copy(ks0[:], ks_pool[:].indirect(offsets[:]))
@@ -141,7 +136,7 @@ def tile_attend_bias_kernel(tc, qT, k_words, k_scales, vT, vs, kb, offs, out):
         part_words(1)
         part_words(2)
 
-        s_t = sb.tile([P, N // P, NQ], F32, name="s_t", tag="s_t", align_bytes=32)
+        s_t = sb.tile([P, N // P, NQ], F32, name="s_t", tag="v_raw11", align_bytes=64)
         neg_s = sb.tile([P, G, 4, P], F32, name="neg_s")
         neg_m = [sb.tile([P, 1], F32, name=f"neg_m{c}") for c in range(len(chunks))]
         raw_tag = ["b0", "b1", "d"]
@@ -160,13 +155,9 @@ def tile_attend_bias_kernel(tc, qT, k_words, k_scales, vT, vs, kb, offs, out):
                         start=(o == 0),
                         stop=(o == 1),
                     )
-            b0, nb = start // P, count // P
-            nc.vector.tensor_tensor(
-                s_t[:, b0 : b0 + nb, :],
-                raw[:, 0:nb, :],
-                kb_col[:, b0 : b0 + nb].unsqueeze(2).to_broadcast([P, nb, NQ]),
-                ALU.add,
-            )
+            for b in range(count // P):
+                blk = start // P + b
+                nc.scalar.activation(s_t[:, blk, :], raw[:, b, :], ACT.Identity, bias=kb_col[:, blk : blk + 1])
         for c, (start, count) in enumerate(chunks):
             scores = bank(score_tag[c], f"scores{c}")
             for b in range(count // P):
@@ -183,12 +174,12 @@ def tile_attend_bias_kernel(tc, qT, k_words, k_scales, vT, vs, kb, offs, out):
             )
 
         vs_col = [sb.tile([P, 4], F32, name=f"vs_col{g}") for g in range(G)]
+        vs_g = sb.tile([P, N], F32, name="vs_g", tag="gathered0", align_bytes=64)
+        nc.vector.tensor_copy(vs_g[:], vs_pool[:].indirect(offsets[:]))
         for g in range(G):
-            vs_g = sb.tile([P, PASS], F32, name=f"vs_g{g}", tag=["gathered0", "s_t"][g], align_bytes=[64, 32][g])
-            nc.vector.tensor_copy(vs_g[:], vs_pool[:].indirect(listed(g)))
-            turned = bank(["d", "a1"][g], f"vs_turned{g}")
+            turned = bank(["b0", "d"][g], f"vs_turned{g}")
             for t in range(4):
-                nc.tensor.transpose(turned[:, t, :], vs_g[:, t:PASS:4], ident[:])
+                nc.tensor.transpose(turned[:, t, :], vs_g[:, g * PASS + t : (g + 1) * PASS : 4], ident[:])
             nc.vector.tensor_copy(vs_col[g][:], turned[:, :, LIVE])
 
         gather_values(1)
@@ -225,7 +216,7 @@ def tile_attend_bias_kernel(tc, qT, k_words, k_scales, vT, vs, kb, offs, out):
                 words = v_g[h][:, g, 0:PASS].bitcast(F32)
                 for u in range(2):
                     nc.tensor.transpose(turned[:, 2 * g + u, :], words[:, u : PASS // 2 : 2], ident[:])
-            nc.scalar.copy(v_il[:, :, h].bitcast(F32), turned[:].rearrange("p (g u) e -> p g e u", g=G))
+            nc.vector.tensor_copy(v_il[:, :, h].bitcast(F32), turned[:].rearrange("p (g u) e -> p g e u", g=G))
             for g in range(G):
                 nc.vector.quantize_mx(
                     out=v_codes[:, g, h * P : (h + 1) * P].bitcast(FP8X4),

@@ -65,10 +65,8 @@ def tile_attend_bias_kernel(tc, qT, k_words, k_scales, vT, vs, kb, offs, out):
         kw_pool = sb.tile([P, T], I32, name="kw_pool")
         nc.sync.dma_start(kw_pool[:], k_words[0].rearrange("p t b -> p (t b)").bitcast(I32))
 
-        warm = sb.tile([P, 1], F32, name="warm")
         ident = sb.tile([P, P], F32, name="ident")
         make_identity(nc, ident[:])
-        nc.scalar.activation(warm[:], ident[:, 0:1], ACT.Exp)
         nc.vector.memset(kb_pool[0:LIVE, :], 0.0)
         ks1 = sb.tile([P, N], U8, name="ks1", align_bytes=64)
         nc.vector.memset(ks1[:].bitcast(I32), 0)

@@ -37,16 +37,10 @@ def tile_attend_bias_kernel(tc, qT, k_words, k_scales, vT, vs, kb, offs, out):
         nc.sync.dma_start(offsets[:], offs)
 
         ks_pool = sb.tile([P, T], U8, name="ks_pool", align_bytes=64)
-        nc.vector.memset(ks_pool[:].bitcast(I32), 0)
-        for quad in range(4):
-            nc.sync.dma_start(
-                ks_pool[32 * quad : 32 * quad + 8, :].bitcast(I32),
-                k_scales[:, 4 * quad : 4 * quad + 4, :].bitcast(I32),
-            )
-        vs_pool = sb.tile([P, T], F32, name="vs_pool")
-        nc.sync.dma_start(vs_pool[LIVE:P, :], vs[0:1, :])
+        nc.sync.dma_start(ks_pool[96:P, :].bitcast(I32), k_scales.bitcast(I32).rearrange("o r w -> r o w"))
+        nc.vector.memset(ks_pool[0:96, :].bitcast(I32), 0)
         kb_pool = sb.tile([P, T], F32, name="kb_pool")
-        nc.sync.dma_start(kb_pool[LIVE:P, :], kb[0:1, :])
+        nc.scalar.dma_start(kb_pool[LIVE:P, :], kb[0:1, :])
         v_raw = [
             [sb.tile([P, T // 2], F32, name=f"v_raw{h}{c}", tag=f"v_raw{h}{c}", align_bytes=64) for c in range(2)]
             for h in range(2)
@@ -65,36 +59,41 @@ def tile_attend_bias_kernel(tc, qT, k_words, k_scales, vT, vs, kb, offs, out):
         kw_pool = sb.tile([P, T], I32, name="kw_pool")
         nc.sync.dma_start(kw_pool[:], k_words[0].rearrange("p t b -> p (t b)").bitcast(I32))
 
+        vs_pool = sb.tile([P, T], F32, name="vs_pool")
+        nc.scalar.dma_start(vs_pool[LIVE:P, :], vs[0:1, :])
+
         ident = sb.tile([P, P], F32, name="ident")
         make_identity(nc, ident[:])
+        k_sc = sb.tile([P, 2, N], U8, name="k_sc", align_bytes=64)
+        nc.vector.memset(k_sc[:].bitcast(I32), 0)
         nc.vector.memset(kb_pool[0:LIVE, :], 0.0)
-        ks1 = sb.tile([P, N], U8, name="ks1", align_bytes=64)
-        nc.vector.memset(ks1[:].bitcast(I32), 0)
-        nc.vector.memset(vs_pool[0:LIVE, :], 0.0)
+        nc.gpsimd.memset(vs_pool[0:LIVE, :], 0.0)
 
         ks0 = sb.tile([P, N], U8, name="ks0", align_bytes=64)
         nc.vector.tensor_copy(ks0[:], ks_pool[:].indirect(offsets[:]))
-        nc.sync.dma_start(ks1[0:112, :].bitcast(I32), ks0[4:116, :].bitcast(I32))
-        k_sc = [ks0, ks1]
+        for quad in range(4):
+            nc.sync.dma_start(
+                k_sc[32 * quad : 32 * quad + 4].bitcast(I32), ks0[96 + 8 * quad : 104 + 8 * quad, :].bitcast(I32)
+            )
         load_values(1, 0)
         load_values(1, 1)
         kb_g = sb.tile([P, N], F32, name="kb_g")
         nc.vector.tensor_copy(kb_g[:], kb_pool[:].indirect(offsets[:]))
 
         v_bf = [sb.tile([P, T], BF16, name=f"v_bf{h}", tag=f"v_bf{h}", align_bytes=64) for h in range(2)]
-        v_g = [sb.tile([P, G, PASS + 16], BF16, name=f"v_g{h}") for h in range(2)]
+        v_g0 = sb.tile([P, N], BF16, name="v_g0")
 
         def cast_values(h):
             for c in range(2):
                 nc.scalar.activation(v_bf[h][:, columns(c)], v_raw[h][c][:], ACT.Copy)
 
-        def gather_values(h):
-            nc.scalar.activation(v_g[h][:, :, 0:PASS], v_bf[h][:].indirect(offsets[:]), ACT.Copy)
+        def listed_range(start, count):
+            return offsets[:, start // 16 : (start + count) // 16]
 
         cast_values(0)
         q_bf = sb.tile([P, 2, NQ, 4], BF16, name="q_bf", align_bytes=64)
         nc.scalar.activation(q_bf[:], q_raw[:].rearrange("p o j w -> p o w j"), ACT.Copy)
-        gather_values(0)
+        nc.scalar.activation(v_g0[:], v_bf[0][:].indirect(offsets[:]), ACT.Copy)
 
         kb_col = sb.tile([P, N // P], F32, name="kb_col", tag="v_bf0", align_bytes=64)
         for g in range(G):
@@ -106,9 +105,6 @@ def tile_attend_bias_kernel(tc, qT, k_words, k_scales, vT, vs, kb, offs, out):
         cast_values(1)
 
         chunks = [(0, 512), (512, 256), (768, 256)]
-
-        def listed_range(start, count):
-            return offsets[:, start // 16 : (start + count) // 16]
 
         kw_g = [sb.tile([P, n], I32, name=f"kw_g{c}", tag=f"gathered{c}", align_bytes=64) for c, (s0, n) in enumerate(chunks)]
         k_codes = [sb.tile([P, 2, 2 * n], U8, name=f"k_codes{c}", align_bytes=64) for c, (s0, n) in enumerate(chunks)]
@@ -135,7 +131,7 @@ def tile_attend_bias_kernel(tc, qT, k_words, k_scales, vT, vs, kb, offs, out):
         part_words(2)
 
         s_t = sb.tile([P, N // P, NQ], F32, name="s_t", tag="v_raw11", align_bytes=64)
-        neg_s = sb.tile([P, G, 4, P], F32, name="neg_s")
+        neg_s = sb.tile([P, G, 4, P], F32, name="neg_s", tag="neg_s")
         neg_m = [sb.tile([P, 1], F32, name=f"neg_m{c}") for c in range(len(chunks))]
         raw_tag = ["b0", "b1", "d"]
         score_tag = ["a0", "a1", "e"]
@@ -147,7 +143,7 @@ def tile_attend_bias_kernel(tc, qT, k_words, k_scales, vT, vs, kb, offs, out):
                     nc.tensor.matmul_mx(
                         out=raw[:, b, :],
                         lhsT=k_codes[c][:, o, 2 * b * P : 2 * (b + 1) * P].bitcast(FP4X4),
-                        lhsT_scale=k_sc[o][:, c0 : c0 + P],
+                        lhsT_scale=k_sc[:, o, c0 : c0 + P],
                         rhs=q_codes[:, o * NQ : (o + 1) * NQ].bitcast(FP8X4),
                         rhs_scale=q_sc[:, o * NQ : (o + 1) * NQ],
                         start=(o == 0),
@@ -172,21 +168,22 @@ def tile_attend_bias_kernel(tc, qT, k_words, k_scales, vT, vs, kb, offs, out):
             )
 
         vs_col = [sb.tile([P, 4], F32, name=f"vs_col{g}") for g in range(G)]
-        vs_g = sb.tile([P, N], F32, name="vs_g", tag="gathered0", align_bytes=64)
+        vs_g = sb.tile([P, N], F32, name="vs_g", tag="gathered2", align_bytes=64)
         nc.vector.tensor_copy(vs_g[:], vs_pool[:].indirect(offsets[:]))
         for g in range(G):
-            turned = bank(["b0", "d"][g], f"vs_turned{g}")
-            for t in range(4):
-                nc.tensor.transpose(turned[:, t, :], vs_g[:, g * PASS + t : (g + 1) * PASS : 4], ident[:])
-            nc.vector.tensor_copy(vs_col[g][:], turned[:, :, LIVE])
+            nc.sync.dma_start(vs_col[g][:], vs_g[LIVE:P, g * PASS : (g + 1) * PASS])
 
-        gather_values(1)
-        p_sb = sb.tile([P, G, 4, P], F32, name="p_sb", tag="v_bf1", align_bytes=64)
+        v_g10 = sb.tile([P, PASS], BF16, name="v_g10")
+        nc.scalar.activation(v_g10[:], v_bf[1][:].indirect(listed_range(0, PASS)), ACT.Copy)
+        p_sb = sb.tile([P, G, 4, P], F32, name="p_sb")
         l_part = [sb.tile([P, 1], F32, name=f"l_part{g}") for g in range(G)]
         for g in range(G):
             nc.scalar.activation(
                 p_sb[:, g, :, :], neg_s[:, g, :, :], ACT.Exp, bias=neg_m[-1][:], scale=-1.0, accum_out=l_part[g][:]
             )
+
+        v_g11 = sb.tile([P, PASS], BF16, name="v_g11", tag="neg_s")
+        nc.scalar.activation(v_g11[:], v_bf[1][:].indirect(listed_range(PASS, PASS)), ACT.Copy)
 
         w_il = sb.tile([P, G, NQ, 4], BF16, name="w_il", align_bytes=64)
         w_codes = sb.tile([P, G, NQ], U32, name="w_codes", align_bytes=64)
@@ -208,14 +205,22 @@ def tile_attend_bias_kernel(tc, qT, k_words, k_scales, vT, vs, kb, offs, out):
         v_il = sb.tile([P, G, 2, P, 4], BF16, name="v_il", tag="v_raw11", align_bytes=64)
         v_codes = sb.tile([P, G, DV], U32, name="v_codes", align_bytes=64)
         v_sc = sb.tile([P, G, DV], U8, name="v_sc", align_bytes=64)
-        for h in range(2):
-            turned = bank(f"c{h}", f"v_turned{h}")
-            for g in range(G):
-                words = v_g[h][:, g, 0:PASS].bitcast(F32)
+        pieces = [
+            (0, [0, 1], "c0", [v_g0[:, 0:PASS], v_g0[:, PASS:N]]),
+            (1, [0], "c1", [v_g10[:]]),
+            (1, [1], "a0", [v_g11[:]]),
+        ]
+        for h, gs, tag, sources in pieces:
+            turned = bank(tag, f"v_turned{h}{gs[0]}")
+            for i, source in enumerate(sources):
+                words = source.bitcast(F32)
                 for u in range(2):
-                    nc.tensor.transpose(turned[:, 2 * g + u, :], words[:, u : PASS // 2 : 2], ident[:])
-            nc.vector.tensor_copy(v_il[:, :, h].bitcast(F32), turned[:].rearrange("p (g u) e -> p g e u", g=G))
-            for g in range(G):
+                    nc.tensor.transpose(turned[:, 2 * i + u, :], words[:, u : PASS // 2 : 2], ident[:])
+            nc.vector.tensor_copy(
+                v_il[:, gs[0] : gs[-1] + 1, h].bitcast(F32),
+                turned[:, 0 : 2 * len(gs), :].rearrange("p (g u) e -> p g e u", u=2),
+            )
+            for g in gs:
                 nc.vector.quantize_mx(
                     out=v_codes[:, g, h * P : (h + 1) * P].bitcast(FP8X4),
                     scales=v_sc[:, g, h * P : (h + 1) * P],

@@ -41,21 +41,19 @@ def tile_attend_bias_kernel(tc, qT, k_words, k_scales, vT, vs, kb, offs, out):
         nc.vector.memset(ks_pool[0:96, :].bitcast(I32), 0)
         kb_pool = sb.tile([P, T], F32, name="kb_pool")
         nc.scalar.dma_start(kb_pool[LIVE:P, :], kb[0:1, :])
-        v_raw = [
-            [sb.tile([P, T // 2], F32, name=f"v_raw{h}{c}", tag=f"v_raw{h}{c}", align_bytes=64) for c in range(2)]
-            for h in range(2)
-        ]
+        v_raw0 = [sb.tile([P, T // 2], F32, name=f"v_raw0{c}") for c in range(2)]
+        v_raw1 = sb.tile([P, T], F32, name="v_raw1")
 
         def columns(c):
             return slice(c * T // 2, (c + 1) * T // 2)
 
-        def load_values(h, c):
-            nc.sync.dma_start(v_raw[h][c][:], vT[h * P : (h + 1) * P, columns(c)])
+        def load_values(c):
+            nc.sync.dma_start(v_raw0[c][:], vT[0:P, columns(c)])
 
-        load_values(0, 0)
+        load_values(0)
         q_raw = sb.tile([P, 2, 4, NQ], F32, name="q_raw")
         nc.sync.dma_start(q_raw[:], qT[0].rearrange("(o p j) w -> p o j w", o=2, j=4))
-        load_values(0, 1)
+        load_values(1)
         kw_pool = sb.tile([P, T], I32, name="kw_pool")
         nc.sync.dma_start(kw_pool[:], k_words[0].rearrange("p t b -> p (t b)").bitcast(I32))
 
@@ -75,25 +73,21 @@ def tile_attend_bias_kernel(tc, qT, k_words, k_scales, vT, vs, kb, offs, out):
             nc.sync.dma_start(
                 k_sc[32 * quad : 32 * quad + 4].bitcast(I32), ks0[96 + 8 * quad : 104 + 8 * quad, :].bitcast(I32)
             )
-        load_values(1, 0)
-        load_values(1, 1)
+        nc.sync.dma_start(v_raw1[:], vT[P:DV, :])
         kb_g = sb.tile([P, N], F32, name="kb_g")
         nc.vector.tensor_copy(kb_g[:], kb_pool[:].indirect(offsets[:]))
 
-        v_bf = [sb.tile([P, T], BF16, name=f"v_bf{h}", tag=f"v_bf{h}", align_bytes=64) for h in range(2)]
+        v_bf0 = sb.tile([P, T], BF16, name="v_bf0", tag="v_bf0", align_bytes=64)
         v_g0 = sb.tile([P, N], BF16, name="v_g0")
-
-        def cast_values(h):
-            for c in range(2):
-                nc.scalar.activation(v_bf[h][:, columns(c)], v_raw[h][c][:], ACT.Copy)
 
         def listed_range(start, count):
             return offsets[:, start // 16 : (start + count) // 16]
 
-        cast_values(0)
+        for c in range(2):
+            nc.scalar.activation(v_bf0[:, columns(c)], v_raw0[c][:], ACT.Copy)
         q_bf = sb.tile([P, 2, NQ, 4], BF16, name="q_bf", align_bytes=64)
         nc.scalar.activation(q_bf[:], q_raw[:].rearrange("p o j w -> p o w j"), ACT.Copy)
-        nc.scalar.activation(v_g0[:], v_bf[0][:].indirect(offsets[:]), ACT.Copy)
+        nc.scalar.activation(v_g0[:], v_bf0[:].indirect(offsets[:]), ACT.Copy)
 
         kb_col = sb.tile([P, N // P], F32, name="kb_col", tag="v_bf0", align_bytes=64)
         for g in range(G):
@@ -102,7 +96,6 @@ def tile_attend_bias_kernel(tc, qT, k_words, k_scales, vT, vs, kb, offs, out):
                 c0 = g * PASS + b * P
                 nc.tensor.transpose(turned[:, b, :], kb_g[:, c0 : c0 + P], ident[:])
             nc.scalar.copy(kb_col[:, 4 * g : 4 * g + 4], turned[:, :, LIVE])
-        cast_values(1)
 
         chunks = [(0, 512), (512, 256), (768, 256)]
 
@@ -130,9 +123,9 @@ def tile_attend_bias_kernel(tc, qT, k_words, k_scales, vT, vs, kb, offs, out):
         part_words(1)
         part_words(2)
 
-        s_t = sb.tile([P, N // P, NQ], F32, name="s_t", tag="v_raw11", align_bytes=64)
+        s_t = sb.tile([P, N // P, NQ], F32, name="s_t")
         neg_s = sb.tile([P, G, 4, P], F32, name="neg_s", tag="neg_s")
-        neg_m = [sb.tile([P, 1], F32, name=f"neg_m{c}") for c in range(len(chunks))]
+        neg_m = [sb.tile([P, 1], F32, name=f"neg_m{c}", tag=f"neg_m{c}") for c in range(len(chunks))]
         raw_tag = ["b0", "b1", "d"]
         score_tag = ["a0", "a1", "e"]
         for c, (start, count) in enumerate(chunks):
@@ -173,17 +166,15 @@ def tile_attend_bias_kernel(tc, qT, k_words, k_scales, vT, vs, kb, offs, out):
         for g in range(G):
             nc.sync.dma_start(vs_col[g][:], vs_g[LIVE:P, g * PASS : (g + 1) * PASS])
 
-        v_g10 = sb.tile([P, PASS], BF16, name="v_g10")
-        nc.scalar.activation(v_g10[:], v_bf[1][:].indirect(listed_range(0, PASS)), ACT.Copy)
+        v_g1 = sb.tile([P, G, PASS], BF16, name="v_g1", tag="neg_m1")
+        for g in range(G):
+            nc.vector.tensor_copy(v_g1[:, g, :], v_raw1[:].indirect(listed_range(g * PASS, PASS)))
         p_sb = sb.tile([P, G, 4, P], F32, name="p_sb")
         l_part = [sb.tile([P, 1], F32, name=f"l_part{g}") for g in range(G)]
         for g in range(G):
             nc.scalar.activation(
                 p_sb[:, g, :, :], neg_s[:, g, :, :], ACT.Exp, bias=neg_m[-1][:], scale=-1.0, accum_out=l_part[g][:]
             )
-
-        v_g11 = sb.tile([P, PASS], BF16, name="v_g11", tag="neg_s")
-        nc.scalar.activation(v_g11[:], v_bf[1][:].indirect(listed_range(PASS, PASS)), ACT.Copy)
 
         w_il = sb.tile([P, G, NQ, 4], BF16, name="w_il", align_bytes=64)
         w_codes = sb.tile([P, G, NQ], U32, name="w_codes", align_bytes=64)
@@ -202,13 +193,13 @@ def tile_attend_bias_kernel(tc, qT, k_words, k_scales, vT, vs, kb, offs, out):
             nc.vector.quantize_mx(
                 out=w_codes[:, g, :].bitcast(FP8X4), scales=w_sc[:, g, :], in_=w_il[:, g].rearrange("p q t -> p (q t)")
             )
-        v_il = sb.tile([P, G, 2, P, 4], BF16, name="v_il", tag="v_raw11", align_bytes=64)
+        v_il = sb.tile([P, G, 2, P, 4], BF16, name="v_il", align_bytes=64)
         v_codes = sb.tile([P, G, DV], U32, name="v_codes", align_bytes=64)
         v_sc = sb.tile([P, G, DV], U8, name="v_sc", align_bytes=64)
         pieces = [
             (0, [0, 1], "c0", [v_g0[:, 0:PASS], v_g0[:, PASS:N]]),
-            (1, [0], "c1", [v_g10[:]]),
-            (1, [1], "a0", [v_g11[:]]),
+            (1, [0], "c1", [v_g1[:, 0, :]]),
+            (1, [1], "a0", [v_g1[:, 1, :]]),
         ]
         for h, gs, tag, sources in pieces:
             turned = bank(tag, f"v_turned{h}{gs[0]}")
@@ -216,7 +207,7 @@ def tile_attend_bias_kernel(tc, qT, k_words, k_scales, vT, vs, kb, offs, out):
                 words = source.bitcast(F32)
                 for u in range(2):
                     nc.tensor.transpose(turned[:, 2 * i + u, :], words[:, u : PASS // 2 : 2], ident[:])
-            nc.vector.tensor_copy(
+            nc.scalar.copy(
                 v_il[:, gs[0] : gs[-1] + 1, h].bitcast(F32),
                 turned[:, 0 : 2 * len(gs), :].rearrange("p (g u) e -> p g e u", u=2),
             )

@@ -50,12 +50,11 @@ def tile_attend_bias_kernel(tc, qT, k_words, k_scales, vT, vs, kb, offs, out):
         def load_values(c):
             nc.sync.dma_start(v_raw0[c][:], vT[0:P, columns(c)])
 
-        load_values(0)
         q_raw = sb.tile([P, 2, 4, NQ], F32, name="q_raw")
         nc.sync.dma_start(q_raw[:], qT[0].rearrange("(o p j) w -> p o j w", o=2, j=4))
-        load_values(1)
         kw_pool = sb.tile([P, T], I32, name="kw_pool")
         nc.sync.dma_start(kw_pool[:], k_words[0].rearrange("p t b -> p (t b)").bitcast(I32))
+        load_values(0)
 
         vs_pool = sb.tile([P, T], F32, name="vs_pool")
         nc.scalar.dma_start(vs_pool[LIVE:P, :], vs[0:1, :])
@@ -73,6 +72,7 @@ def tile_attend_bias_kernel(tc, qT, k_words, k_scales, vT, vs, kb, offs, out):
             nc.sync.dma_start(
                 k_sc[32 * quad : 32 * quad + 4].bitcast(I32), ks0[96 + 8 * quad : 104 + 8 * quad, :].bitcast(I32)
             )
+        load_values(1)
         nc.sync.dma_start(v_raw1[:], vT[P:DV, :])
         kb_g = sb.tile([P, N], F32, name="kb_g")
         nc.vector.tensor_copy(kb_g[:], kb_pool[:].indirect(offsets[:]))

@@ -36,12 +36,12 @@ def tile_attend_bias_kernel(tc, qT, k_words, k_scales, vT, vs, kb, offs, out):
         offsets = sb.tile([P, N // 16], U16, name="offsets")
         nc.sync.dma_start(offsets[:], offs)
 
-        ks_pool = sb.tile([P, T], U8, name="ks_pool", align_bytes=64)
+        ks_pool = sb.tile([P, T], U8, name="ks_pool", tag="ks_pool", align_bytes=64)
         nc.sync.dma_start(ks_pool[96:P, :].bitcast(I32), k_scales.bitcast(I32).rearrange("o r w -> r o w"))
         nc.vector.memset(ks_pool[0:96, :].bitcast(I32), 0)
-        kb_pool = sb.tile([P, T], F32, name="kb_pool")
+        kb_pool = sb.tile([P, T], F32, name="kb_pool", tag="gathered0", align_bytes=64)
         nc.scalar.dma_start(kb_pool[LIVE:P, :], kb[0:1, :])
-        v_raw0 = [sb.tile([P, T // 2], F32, name=f"v_raw0{c}") for c in range(2)]
+        v_raw0 = [sb.tile([P, T // 2], F32, name=f"v_raw0{c}", tag=f"v_raw0{c}") for c in range(2)]
         v_raw1 = sb.tile([P, T], F32, name="v_raw1")
 
         def columns(c):
@@ -50,54 +50,54 @@ def tile_attend_bias_kernel(tc, qT, k_words, k_scales, vT, vs, kb, offs, out):
         def load_values(c):
             nc.sync.dma_start(v_raw0[c][:], vT[0:P, columns(c)])
 
-        q_raw = sb.tile([P, 2, 4, NQ], F32, name="q_raw")
+        q_raw = sb.tile([P, 2, 4, NQ], F32, name="q_raw", tag="q_raw", align_bytes=64)
         nc.sync.dma_start(q_raw[:], qT[0].rearrange("(o p j) w -> p o j w", o=2, j=4))
         kw_pool = sb.tile([P, T], I32, name="kw_pool")
         nc.sync.dma_start(kw_pool[:], k_words[0].rearrange("p t b -> p (t b)").bitcast(I32))
         load_values(0)
-
-        vs_pool = sb.tile([P, T], F32, name="vs_pool")
-        nc.scalar.dma_start(vs_pool[LIVE:P, :], vs[0:1, :])
+        load_values(1)
+        nc.sync.dma_start(v_raw1[:], vT[P:DV, :])
 
         ident = sb.tile([P, P], F32, name="ident")
         make_identity(nc, ident[:])
-        k_sc = sb.tile([P, 2, N], U8, name="k_sc", align_bytes=64)
-        nc.vector.memset(k_sc[:].bitcast(I32), 0)
         nc.vector.memset(kb_pool[0:LIVE, :], 0.0)
-        nc.gpsimd.memset(vs_pool[0:LIVE, :], 0.0)
+
+        q_bf = sb.tile([P, 2, NQ, 4], BF16, name="q_bf", align_bytes=64)
+        nc.scalar.activation(q_bf[:], q_raw[:].rearrange("p o j w -> p o w j"), ACT.Copy)
+        k_sc = sb.tile([P, 2, N], U8, name="k_sc", tag="q_raw", align_bytes=64)
+        nc.gpsimd.memset(k_sc[:].bitcast(I32), 0)
 
         ks0 = sb.tile([P, N], U8, name="ks0", align_bytes=64)
         nc.vector.tensor_copy(ks0[:], ks_pool[:].indirect(offsets[:]))
         for quad in range(4):
-            nc.sync.dma_start(
+            nc.scalar.dma_start(
                 k_sc[32 * quad : 32 * quad + 4].bitcast(I32), ks0[96 + 8 * quad : 104 + 8 * quad, :].bitcast(I32)
             )
-        load_values(1)
-        nc.sync.dma_start(v_raw1[:], vT[P:DV, :])
+        vs_pool = sb.tile([P, T], F32, name="vs_pool", tag="ks_pool", align_bytes=64)
+        nc.sync.dma_start(vs_pool[LIVE:P, :], vs[0:1, :])
+        nc.gpsimd.memset(vs_pool[0:LIVE, :], 0.0)
         kb_g = sb.tile([P, N], F32, name="kb_g")
         nc.vector.tensor_copy(kb_g[:], kb_pool[:].indirect(offsets[:]))
 
         v_bf0 = sb.tile([P, T], BF16, name="v_bf0", tag="v_bf0", align_bytes=64)
-        v_g0 = sb.tile([P, N], BF16, name="v_g0")
+        v_g00 = sb.tile([P, PASS], BF16, name="v_g00")
 
         def listed_range(start, count):
             return offsets[:, start // 16 : (start + count) // 16]
 
         for c in range(2):
             nc.scalar.activation(v_bf0[:, columns(c)], v_raw0[c][:], ACT.Copy)
-        q_bf = sb.tile([P, 2, NQ, 4], BF16, name="q_bf", align_bytes=64)
-        nc.scalar.activation(q_bf[:], q_raw[:].rearrange("p o j w -> p o w j"), ACT.Copy)
-        nc.scalar.activation(v_g0[:], v_bf0[:].indirect(offsets[:]), ACT.Copy)
 
-        kb_col = sb.tile([P, N // P], F32, name="kb_col", tag="v_bf0", align_bytes=64)
+        kb_col = sb.tile([P, N // P], F32, name="kb_col", tag="v_raw01")
         for g in range(G):
             turned = bank(f"a{g}", f"kb_turned{g}")
             for b in range(4):
                 c0 = g * PASS + b * P
                 nc.tensor.transpose(turned[:, b, :], kb_g[:, c0 : c0 + P], ident[:])
             nc.scalar.copy(kb_col[:, 4 * g : 4 * g + 4], turned[:, :, LIVE])
+        nc.scalar.activation(v_g00[:], v_bf0[:].indirect(listed_range(0, PASS)), ACT.Copy)
 
-        chunks = [(0, 512), (512, 256), (768, 256)]
+        chunks = [(0, 512), (512, 512)]
 
         kw_g = [sb.tile([P, n], I32, name=f"kw_g{c}", tag=f"gathered{c}", align_bytes=64) for c, (s0, n) in enumerate(chunks)]
         k_codes = [sb.tile([P, 2, 2 * n], U8, name=f"k_codes{c}", align_bytes=64) for c, (s0, n) in enumerate(chunks)]
@@ -113,21 +113,28 @@ def tile_attend_bias_kernel(tc, qT, k_words, k_scales, vT, vs, kb, offs, out):
         q_codes = sb.tile([P, 2 * NQ], U32, name="q_codes", align_bytes=64)
         q_sc = sb.tile([P, 2 * NQ], U8, name="q_sc", align_bytes=64)
 
-        gather_words(0)
-        gather_words(1)
-        part_words(0)
         nc.vector.quantize_mx(
             out=q_codes[:].bitcast(FP8X4), scales=q_sc[:], in_=q_bf[:].rearrange("p o w j -> p (o w j)")
         )
-        gather_words(2)
+        gather_words(0)
+        gather_words(1)
+        part_words(0)
         part_words(1)
-        part_words(2)
+
+        vs_col = [sb.tile([P, 4], F32, name=f"vs_col{g}") for g in range(G)]
+        vs_g = sb.tile([P, N], F32, name="vs_g", tag="gathered0", align_bytes=64)
+        nc.vector.tensor_copy(vs_g[:], vs_pool[:].indirect(offsets[:]))
+        for g in range(G):
+            nc.sync.dma_start(vs_col[g][:], vs_g[LIVE:P, g * PASS : (g + 1) * PASS])
+
+        v_g10 = sb.tile([P, PASS], BF16, name="v_g10", tag="gathered1", align_bytes=64)
+        nc.vector.tensor_copy(v_g10[:], v_raw1[:].indirect(listed_range(0, PASS)))
 
         s_t = sb.tile([P, N // P, NQ], F32, name="s_t")
-        neg_s = sb.tile([P, G, 4, P], F32, name="neg_s", tag="neg_s")
-        neg_m = [sb.tile([P, 1], F32, name=f"neg_m{c}", tag=f"neg_m{c}") for c in range(len(chunks))]
-        raw_tag = ["b0", "b1", "d"]
-        score_tag = ["a0", "a1", "e"]
+        neg_s = sb.tile([P, G, 4, P], F32, name="neg_s", tag="ks_pool", align_bytes=64)
+        neg_m = [sb.tile([P, 1], F32, name=f"neg_m{c}", tag=f"neg_m{c}", align_bytes=64) for c in range(len(chunks))]
+        raw_tag = ["b0", "b1"]
+        score_tag = ["a0", "a1"]
         for c, (start, count) in enumerate(chunks):
             raw = bank(raw_tag[c], f"raw{c}")
             for b in range(count // P):
@@ -160,21 +167,44 @@ def tile_attend_bias_kernel(tc, qT, k_words, k_scales, vT, vs, kb, offs, out):
                 accum_out=neg_m[c][:],
             )
 
-        vs_col = [sb.tile([P, 4], F32, name=f"vs_col{g}") for g in range(G)]
-        vs_g = sb.tile([P, N], F32, name="vs_g", tag="gathered2", align_bytes=64)
-        nc.vector.tensor_copy(vs_g[:], vs_pool[:].indirect(offsets[:]))
-        for g in range(G):
-            nc.sync.dma_start(vs_col[g][:], vs_g[LIVE:P, g * PASS : (g + 1) * PASS])
-
-        v_g1 = sb.tile([P, G, PASS], BF16, name="v_g1", tag="neg_m1")
-        for g in range(G):
-            nc.vector.tensor_copy(v_g1[:, g, :], v_raw1[:].indirect(listed_range(g * PASS, PASS)))
+        v_g01 = sb.tile([P, PASS], BF16, name="v_g01", tag="v_raw01")
+        nc.scalar.activation(v_g01[:], v_bf0[:].indirect(listed_range(PASS, PASS)), ACT.Copy)
         p_sb = sb.tile([P, G, 4, P], F32, name="p_sb")
         l_part = [sb.tile([P, 1], F32, name=f"l_part{g}") for g in range(G)]
         for g in range(G):
             nc.scalar.activation(
                 p_sb[:, g, :, :], neg_s[:, g, :, :], ACT.Exp, bias=neg_m[-1][:], scale=-1.0, accum_out=l_part[g][:]
             )
+
+        l_sum = sb.tile([P, 1], F32, name="l_sum")
+        nc.scalar.activation(l_sum[:], l_part[0][:], ACT.Identity, bias=l_part[1][:])
+
+        v_codes = sb.tile([P, G, DV], U32, name="v_codes", align_bytes=64)
+        v_sc = sb.tile([P, G, DV], U8, name="v_sc", tag="neg_m0", align_bytes=64)
+
+        def turn_values(h, g, tag, slot, source):
+            turned = bank(tag, f"v_turned{h}{g}")
+            words = source.bitcast(F32)
+            for u in range(2):
+                nc.tensor.transpose(turned[:, u, :], words[:, u : PASS // 2 : 2], ident[:])
+            v_il = sb.tile([P, P, 4], BF16, name=f"v_il{h}{g}", tag=slot, align_bytes=64)
+            nc.scalar.copy(v_il[:].bitcast(F32), turned[:, 0:2, :].rearrange("p u e -> p e u"))
+            return v_il
+
+        def quantize_values(h, g, v_il):
+            nc.vector.quantize_mx(
+                out=v_codes[:, g, h * P : (h + 1) * P].bitcast(FP8X4),
+                scales=v_sc[:, g, h * P : (h + 1) * P],
+                in_=v_il[:].rearrange("p e t -> p (e t)"),
+            )
+
+        v_il00 = turn_values(0, 0, "c0", "v_il00", v_g00[:])
+        v_il10 = turn_values(1, 0, "b1", "neg_m1", v_g10[:])
+        v_il01 = turn_values(0, 1, "e", "v_il01", v_g01[:])
+        quantize_values(0, 0, v_il00)
+        v_g11 = sb.tile([P, PASS], BF16, name="v_g11", tag="v_il00", align_bytes=64)
+        nc.vector.tensor_copy(v_g11[:], v_raw1[:].indirect(listed_range(PASS, PASS)))
+        quantize_values(0, 1, v_il01)
 
         w_il = sb.tile([P, G, NQ, 4], BF16, name="w_il", align_bytes=64)
         w_codes = sb.tile([P, G, NQ], U32, name="w_codes", align_bytes=64)
@@ -189,39 +219,15 @@ def tile_attend_bias_kernel(tc, qT, k_words, k_scales, vT, vs, kb, offs, out):
                 vs_col[g][:].unsqueeze(1).to_broadcast([P, NQ, 4]),
                 ALU.mult,
             )
+        v_il11 = turn_values(1, 1, "b0", "v_il11", v_g11[:])
         for g in range(G):
             nc.vector.quantize_mx(
                 out=w_codes[:, g, :].bitcast(FP8X4), scales=w_sc[:, g, :], in_=w_il[:, g].rearrange("p q t -> p (q t)")
             )
-        v_il = sb.tile([P, G, 2, P, 4], BF16, name="v_il", align_bytes=64)
-        v_codes = sb.tile([P, G, DV], U32, name="v_codes", align_bytes=64)
-        v_sc = sb.tile([P, G, DV], U8, name="v_sc", align_bytes=64)
-        pieces = [
-            (0, [0, 1], "c0", [v_g0[:, 0:PASS], v_g0[:, PASS:N]]),
-            (1, [0], "c1", [v_g1[:, 0, :]]),
-            (1, [1], "a0", [v_g1[:, 1, :]]),
-        ]
-        for h, gs, tag, sources in pieces:
-            turned = bank(tag, f"v_turned{h}{gs[0]}")
-            for i, source in enumerate(sources):
-                words = source.bitcast(F32)
-                for u in range(2):
-                    nc.tensor.transpose(turned[:, 2 * i + u, :], words[:, u : PASS // 2 : 2], ident[:])
-            nc.scalar.copy(
-                v_il[:, gs[0] : gs[-1] + 1, h].bitcast(F32),
-                turned[:, 0 : 2 * len(gs), :].rearrange("p (g u) e -> p g e u", u=2),
-            )
-            for g in gs:
-                nc.vector.quantize_mx(
-                    out=v_codes[:, g, h * P : (h + 1) * P].bitcast(FP8X4),
-                    scales=v_sc[:, g, h * P : (h + 1) * P],
-                    in_=v_il[:, g, h].rearrange("p e t -> p (e t)"),
-                )
-
-        l_sum = sb.tile([P, 1], F32, name="l_sum")
+        quantize_values(1, 0, v_il10)
         l_inv = sb.tile([P, 1], F32, name="l_inv")
-        nc.vector.tensor_tensor(l_sum[:], l_part[0][:], l_part[1][:], ALU.add)
         nc.vector.reciprocal(l_inv[:], l_sum[:])
+        quantize_values(1, 1, v_il11)
 
         y_ps = ps.tile([P, DV], F32, tag="d", name="y_ps")
         for g in range(G):

@@ -41,61 +41,65 @@ def tile_attend_bias_kernel(tc, qT, k_words, k_scales, vT, vs, kb, offs, out):
         nc.vector.memset(ks_pool[0:96, :].bitcast(I32), 0)
         kb_pool = sb.tile([P, T], F32, name="kb_pool", tag="gathered0", align_bytes=64)
         nc.scalar.dma_start(kb_pool[LIVE:P, :], kb[0:1, :])
-        v_raw0 = [sb.tile([P, T // 2], F32, name=f"v_raw0{c}", tag=f"v_raw0{c}") for c in range(2)]
-        v_raw1 = sb.tile([P, T], F32, name="v_raw1")
+        v_raw = [
+            [sb.tile([P, T // 2], F32, name=f"v_raw{h}{c}", tag=f"v_raw{h}{c}") for c in range(2)] for h in range(2)
+        ]
 
         def columns(c):
             return slice(c * T // 2, (c + 1) * T // 2)
 
-        def load_values(c):
-            nc.sync.dma_start(v_raw0[c][:], vT[0:P, columns(c)])
+        def load_values(h):
+            for c in range(2):
+                nc.sync.dma_start(v_raw[h][c][:], vT[h * P : (h + 1) * P, columns(c)])
 
         q_raw = sb.tile([P, 2, 4, NQ], F32, name="q_raw", tag="q_raw", align_bytes=64)
         nc.sync.dma_start(q_raw[:], qT[0].rearrange("(o p j) w -> p o j w", o=2, j=4))
+        load_values(0)
         kw_pool = sb.tile([P, T], I32, name="kw_pool")
         nc.sync.dma_start(kw_pool[:], k_words[0].rearrange("p t b -> p (t b)").bitcast(I32))
-        load_values(0)
-        load_values(1)
-        nc.sync.dma_start(v_raw1[:], vT[P:DV, :])
 
         ident = sb.tile([P, P], F32, name="ident")
         make_identity(nc, ident[:])
         nc.vector.memset(kb_pool[0:LIVE, :], 0.0)
+        k_sc = sb.tile([P, 2, N], U8, name="k_sc", align_bytes=64)
+        nc.vector.memset(k_sc[:].bitcast(I32), 0)
 
         q_bf = sb.tile([P, 2, NQ, 4], BF16, name="q_bf", align_bytes=64)
         nc.scalar.activation(q_bf[:], q_raw[:].rearrange("p o j w -> p o w j"), ACT.Copy)
-        k_sc = sb.tile([P, 2, N], U8, name="k_sc", tag="q_raw", align_bytes=64)
-        nc.gpsimd.memset(k_sc[:].bitcast(I32), 0)
 
         ks0 = sb.tile([P, N], U8, name="ks0", align_bytes=64)
         nc.vector.tensor_copy(ks0[:], ks_pool[:].indirect(offsets[:]))
         for quad in range(4):
-            nc.scalar.dma_start(
+            nc.sync.dma_start(
                 k_sc[32 * quad : 32 * quad + 4].bitcast(I32), ks0[96 + 8 * quad : 104 + 8 * quad, :].bitcast(I32)
             )
         vs_pool = sb.tile([P, T], F32, name="vs_pool", tag="ks_pool", align_bytes=64)
         nc.sync.dma_start(vs_pool[LIVE:P, :], vs[0:1, :])
         nc.gpsimd.memset(vs_pool[0:LIVE, :], 0.0)
+        load_values(1)
         kb_g = sb.tile([P, N], F32, name="kb_g")
         nc.vector.tensor_copy(kb_g[:], kb_pool[:].indirect(offsets[:]))
 
         v_bf0 = sb.tile([P, T], BF16, name="v_bf0", tag="v_bf0", align_bytes=64)
-        v_g00 = sb.tile([P, PASS], BF16, name="v_g00")
+        v_bf1 = sb.tile([P, T], BF16, name="v_bf1")
+        v_g0 = sb.tile([P, N], BF16, name="v_g0")
 
         def listed_range(start, count):
             return offsets[:, start // 16 : (start + count) // 16]
 
         for c in range(2):
-            nc.scalar.activation(v_bf0[:, columns(c)], v_raw0[c][:], ACT.Copy)
+            nc.scalar.activation(v_bf0[:, columns(c)], v_raw[0][c][:], ACT.Copy)
+        nc.scalar.activation(v_g0[:], v_bf0[:].indirect(offsets[:]), ACT.Copy)
 
-        kb_col = sb.tile([P, N // P], F32, name="kb_col", tag="v_raw01")
+        kb_col = sb.tile([P, N // P], F32, name="kb_col", tag="v_bf0", align_bytes=64)
         for g in range(G):
             turned = bank(f"a{g}", f"kb_turned{g}")
             for b in range(4):
                 c0 = g * PASS + b * P
                 nc.tensor.transpose(turned[:, b, :], kb_g[:, c0 : c0 + P], ident[:])
             nc.scalar.copy(kb_col[:, 4 * g : 4 * g + 4], turned[:, :, LIVE])
-        nc.scalar.activation(v_g00[:], v_bf0[:].indirect(listed_range(0, PASS)), ACT.Copy)
+        for c in range(2):
+            nc.scalar.activation(v_bf1[:, columns(c)], v_raw[1][c][:], ACT.Copy)
 
         chunks = [(0, 512), (512, 512)]
 
@@ -127,10 +131,7 @@ def tile_attend_bias_kernel(tc, qT, k_words, k_scales, vT, vs, kb, offs, out):
         for g in range(G):
             nc.sync.dma_start(vs_col[g][:], vs_g[LIVE:P, g * PASS : (g + 1) * PASS])
 
-        v_g10 = sb.tile([P, PASS], BF16, name="v_g10", tag="gathered1", align_bytes=64)
-        nc.vector.tensor_copy(v_g10[:], v_raw1[:].indirect(listed_range(0, PASS)))
-
-        s_t = sb.tile([P, N // P, NQ], F32, name="s_t")
+        s_t = sb.tile([P, N // P, NQ], F32, name="s_t", tag="v_raw11")
         neg_s = sb.tile([P, G, 4, P], F32, name="neg_s", tag="ks_pool", align_bytes=64)
         neg_m = [sb.tile([P, 1], F32, name=f"neg_m{c}", tag=f"neg_m{c}", align_bytes=64) for c in range(len(chunks))]
         raw_tag = ["b0", "b1"]
@@ -156,10 +157,9 @@ def tile_attend_bias_kernel(tc, qT, k_words, k_scales, vT, vs, kb, offs, out):
             scores = bank(score_tag[c], f"scores{c}")
             for b in range(count // P):
                 nc.tensor.transpose(scores[:, b, :], s_t[:, start // P + b, :], ident[:])
-            p0 = (start % PASS) // 4
             nc.vector.tensor_scalar(
-                neg_s[:, start // PASS, :, p0 : p0 + count // 4],
-                scores[:, 0 : count // P, :].rearrange("q b c -> q (b c)").rearrange("q (p t) -> q t p", t=4),
+                neg_s[:, c].rearrange("q t p -> q p t"),
+                scores[:].rearrange("q b c -> q (b c)").rearrange("q (p t) -> q p t", t=4),
                 -1.0,
                 neg_m[c - 1][:] if c else None,
                 ALU.mult,
@@ -167,8 +167,8 @@ def tile_attend_bias_kernel(tc, qT, k_words, k_scales, vT, vs, kb, offs, out):
                 accum_out=neg_m[c][:],
             )
 
-        v_g01 = sb.tile([P, PASS], BF16, name="v_g01", tag="v_raw01")
-        nc.scalar.activation(v_g01[:], v_bf0[:].indirect(listed_range(PASS, PASS)), ACT.Copy)
+        v_g10 = sb.tile([P, PASS], BF16, name="v_g10")
+        nc.scalar.activation(v_g10[:], v_bf1[:].indirect(listed_range(0, PASS)), ACT.Copy)
         p_sb = sb.tile([P, G, 4, P], F32, name="p_sb")
         l_part = [sb.tile([P, 1], F32, name=f"l_part{g}") for g in range(G)]
         for g in range(G):
@@ -179,32 +179,34 @@ def tile_attend_bias_kernel(tc, qT, k_words, k_scales, vT, vs, kb, offs, out):
         l_sum = sb.tile([P, 1], F32, name="l_sum")
         nc.scalar.activation(l_sum[:], l_part[0][:], ACT.Identity, bias=l_part[1][:])
 
-        v_codes = sb.tile([P, G, DV], U32, name="v_codes", align_bytes=64)
-        v_sc = sb.tile([P, G, DV], U8, name="v_sc", tag="neg_m0", align_bytes=64)
+        v_codes = sb.tile([P, 2, G, P], U32, name="v_codes", align_bytes=64)
+        v_sc = sb.tile([P, 2, G, P], U8, name="v_sc", tag="neg_m0", align_bytes=64)
 
-        def turn_values(h, g, tag, slot, source):
-            turned = bank(tag, f"v_turned{h}{g}")
+        def turn_values(name, tag, slot, source):
+            passes = source.shape[1] // PASS
+            turned = bank(tag, f"v_turned{name}")
             words = source.bitcast(F32)
-            for u in range(2):
-                nc.tensor.transpose(turned[:, u, :], words[:, u : PASS // 2 : 2], ident[:])
-            v_il = sb.tile([P, P, 4], BF16, name=f"v_il{h}{g}", tag=slot, align_bytes=64)
-            nc.scalar.copy(v_il[:].bitcast(F32), turned[:, 0:2, :].rearrange("p u e -> p e u"))
+            for g in range(passes):
+                for u in range(2):
+                    first = g * PASS // 2
+                    nc.tensor.transpose(turned[:, 2 * g + u, :], words[:, first + u : first + PASS // 2 : 2], ident[:])
+            v_il = sb.tile([P, passes, P, 4], BF16, name=f"v_il{name}", tag=slot, align_bytes=64)
+            nc.scalar.copy(v_il[:].bitcast(F32), turned[:, 0 : 2 * passes, :].rearrange("p (g u) e -> p g e u", u=2))
             return v_il
 
-        def quantize_values(h, g, v_il):
+        def quantize_values(h, g0, v_il):
+            gs = slice(g0, g0 + v_il.shape[1])
             nc.vector.quantize_mx(
-                out=v_codes[:, g, h * P : (h + 1) * P].bitcast(FP8X4),
-                scales=v_sc[:, g, h * P : (h + 1) * P],
-                in_=v_il[:].rearrange("p e t -> p (e t)"),
+                out=v_codes[:, h, gs, :].rearrange("p g e -> p (g e)").bitcast(FP8X4),
+                scales=v_sc[:, h, gs, :].rearrange("p g e -> p (g e)"),
+                in_=v_il[:].rearrange("p g e t -> p (g e t)"),
             )
 
-        v_il00 = turn_values(0, 0, "c0", "v_il00", v_g00[:])
-        v_il10 = turn_values(1, 0, "b1", "neg_m1", v_g10[:])
-        v_il01 = turn_values(0, 1, "e", "v_il01", v_g01[:])
-        quantize_values(0, 0, v_il00)
-        v_g11 = sb.tile([P, PASS], BF16, name="v_g11", tag="v_il00", align_bytes=64)
-        nc.vector.tensor_copy(v_g11[:], v_raw1[:].indirect(listed_range(PASS, PASS)))
-        quantize_values(0, 1, v_il01)
+        v_il0 = turn_values("0", "c0", "v_bf0", v_g0[:])
+        v_il10 = turn_values("10", "c1", "neg_m1", v_g10[:])
+        quantize_values(0, 0, v_il0)
+        v_g11 = sb.tile([P, PASS], BF16, name="v_g11", tag="v_bf0", align_bytes=64)
+        nc.vector.tensor_copy(v_g11[:], v_bf1[:].indirect(listed_range(PASS, PASS)))
 
         w_il = sb.tile([P, G, NQ, 4], BF16, name="w_il", align_bytes=64)
         w_codes = sb.tile([P, G, NQ], U32, name="w_codes", align_bytes=64)
@@ -219,27 +221,28 @@ def tile_attend_bias_kernel(tc, qT, k_words, k_scales, vT, vs, kb, offs, out):
                 vs_col[g][:].unsqueeze(1).to_broadcast([P, NQ, 4]),
                 ALU.mult,
             )
-        v_il11 = turn_values(1, 1, "b0", "v_il11", v_g11[:])
+        v_il11 = turn_values("11", "b0", "v_il11", v_g11[:])
+        l_inv = sb.tile([P, 1], F32, name="l_inv")
+        nc.vector.reciprocal(l_inv[:], l_sum[:])
         for g in range(G):
             nc.vector.quantize_mx(
                 out=w_codes[:, g, :].bitcast(FP8X4), scales=w_sc[:, g, :], in_=w_il[:, g].rearrange("p q t -> p (q t)")
             )
         quantize_values(1, 0, v_il10)
-        l_inv = sb.tile([P, 1], F32, name="l_inv")
-        nc.vector.reciprocal(l_inv[:], l_sum[:])
         quantize_values(1, 1, v_il11)
 
-        y_ps = ps.tile([P, DV], F32, tag="d", name="y_ps")
-        for g in range(G):
-            nc.tensor.matmul_mx(
-                out=y_ps[:],
-                lhsT=w_codes[:, g, :].bitcast(FP8X4),
-                lhsT_scale=w_sc[:, g, :],
-                rhs=v_codes[:, g, :].bitcast(FP8X4),
-                rhs_scale=v_sc[:, g, :],
-                start=(g == 0),
-                stop=(g == G - 1),
-            )
-        y_sb = sb.tile([P, DV], F32, name="y_sb")
-        nc.scalar.activation(y_sb[:], y_ps[:], ACT.Copy, scale=l_inv[:])
-        nc.sync.dma_start(out[0], y_sb[:])
+        for h in range(2):
+            y_ps = ps.tile([P, P], F32, tag=["d", "e"][h], name=f"y_ps{h}")
+            for g in range(G):
+                nc.tensor.matmul_mx(
+                    out=y_ps[:],
+                    lhsT=w_codes[:, g, :].bitcast(FP8X4),
+                    lhsT_scale=w_sc[:, g, :],
+                    rhs=v_codes[:, h, g, :].bitcast(FP8X4),
+                    rhs_scale=v_sc[:, h, g, :],
+                    start=(g == 0),
+                    stop=(g == G - 1),
+                )
+            y_sb = sb.tile([P, P], F32, name=f"y_sb{h}")
+            nc.scalar.activation(y_sb[:], y_ps[:], ACT.Copy, scale=l_inv[:])
+            nc.sync.dma_start(out[0][:, h * P : (h + 1) * P], y_sb[:])

@@ -58,11 +58,11 @@ def tile_attend_bias_kernel(tc, qT, k_words, k_scales, vT, vs, kb, offs, out):
         kw_pool = sb.tile([P, T], I32, name="kw_pool")
         nc.sync.dma_start(kw_pool[:], k_words[0].rearrange("p t b -> p (t b)").bitcast(I32))
 
-        ident = sb.tile([P, P], F32, name="ident")
-        make_identity(nc, ident[:])
-        nc.vector.memset(kb_pool[0:LIVE, :], 0.0)
         k_sc = sb.tile([P, 2, N], U8, name="k_sc", align_bytes=64)
         nc.vector.memset(k_sc[:].bitcast(I32), 0)
+        ident = sb.tile([P, P], F32, name="ident")
+        make_identity(nc, ident[:])
+        nc.gpsimd.memset(kb_pool[0:LIVE, :], 0.0)
 
         q_bf = sb.tile([P, 2, NQ, 4], BF16, name="q_bf", align_bytes=64)
         nc.scalar.activation(q_bf[:], q_raw[:].rearrange("p o j w -> p o w j"), ACT.Copy)
@@ -81,7 +81,7 @@ def tile_attend_bias_kernel(tc, qT, k_words, k_scales, vT, vs, kb, offs, out):
         nc.vector.tensor_copy(kb_g[:], kb_pool[:].indirect(offsets[:]))
 
         v_bf0 = sb.tile([P, T], BF16, name="v_bf0", tag="v_bf0", align_bytes=64)
-        v_bf1 = sb.tile([P, T], BF16, name="v_bf1")
+        v_bf1 = sb.tile([P, T], BF16, name="v_bf1", tag="v_bf1", align_bytes=64)
         v_g0 = sb.tile([P, N], BF16, name="v_g0")
 
         def listed_range(start, count):
@@ -101,7 +101,7 @@ def tile_attend_bias_kernel(tc, qT, k_words, k_scales, vT, vs, kb, offs, out):
         for c in range(2):
             nc.scalar.activation(v_bf1[:, columns(c)], v_raw[1][c][:], ACT.Copy)
 
-        chunks = [(0, 512), (512, 512)]
+        chunks = [(c * 256, 256) for c in range(4)]
 
         kw_g = [sb.tile([P, n], I32, name=f"kw_g{c}", tag=f"gathered{c}", align_bytes=64) for c, (s0, n) in enumerate(chunks)]
         k_codes = [sb.tile([P, 2, 2 * n], U8, name=f"k_codes{c}", align_bytes=64) for c, (s0, n) in enumerate(chunks)]
@@ -121,21 +121,21 @@ def tile_attend_bias_kernel(tc, qT, k_words, k_scales, vT, vs, kb, offs, out):
             out=q_codes[:].bitcast(FP8X4), scales=q_sc[:], in_=q_bf[:].rearrange("p o w j -> p (o w j)")
         )
         gather_words(0)
-        gather_words(1)
-        part_words(0)
-        part_words(1)
+        for c in range(1, len(chunks)):
+            gather_words(c)
+            part_words(c - 1)
+        part_words(len(chunks) - 1)
 
         vs_col = [sb.tile([P, 4], F32, name=f"vs_col{g}") for g in range(G)]
-        vs_g = sb.tile([P, N], F32, name="vs_g", tag="gathered0", align_bytes=64)
+        vs_g = sb.tile([P, N], F32, name="vs_g", tag="gathered2", align_bytes=64)
         nc.vector.tensor_copy(vs_g[:], vs_pool[:].indirect(offsets[:]))
         for g in range(G):
             nc.sync.dma_start(vs_col[g][:], vs_g[LIVE:P, g * PASS : (g + 1) * PASS])
 
         s_t = sb.tile([P, N // P, NQ], F32, name="s_t", tag="v_raw11")
         neg_s = sb.tile([P, G, 4, P], F32, name="neg_s", tag="ks_pool", align_bytes=64)
-        neg_m = [sb.tile([P, 1], F32, name=f"neg_m{c}", tag=f"neg_m{c}", align_bytes=64) for c in range(len(chunks))]
-        raw_tag = ["b0", "b1"]
-        score_tag = ["a0", "a1"]
+        neg_m = [sb.tile([P, 1], F32, name=f"neg_m{c}", tag=f"neg_m{c}", align_bytes=64) for c in range(G)]
+        raw_tag = ["b0", "c1", "b1", "d"]
         for c, (start, count) in enumerate(chunks):
             raw = bank(raw_tag[c], f"raw{c}")
             for b in range(count // P):
@@ -153,10 +153,10 @@ def tile_attend_bias_kernel(tc, qT, k_words, k_scales, vT, vs, kb, offs, out):
             for b in range(count // P):
                 blk = start // P + b
                 nc.scalar.activation(s_t[:, blk, :], raw[:, b, :], ACT.Identity, bias=kb_col[:, blk : blk + 1])
-        for c, (start, count) in enumerate(chunks):
-            scores = bank(score_tag[c], f"scores{c}")
-            for b in range(count // P):
-                nc.tensor.transpose(scores[:, b, :], s_t[:, start // P + b, :], ident[:])
+        for c in range(G):
+            scores = bank(f"a{c}", f"scores{c}")
+            for b in range(4):
+                nc.tensor.transpose(scores[:, b, :], s_t[:, 4 * c + b, :], ident[:])
             nc.vector.tensor_scalar(
                 neg_s[:, c].rearrange("q t p -> q p t"),
                 scores[:].rearrange("q b c -> q (b c)").rearrange("q (p t) -> q p t", t=4),
@@ -167,20 +167,30 @@ def tile_attend_bias_kernel(tc, qT, k_words, k_scales, vT, vs, kb, offs, out):
                 accum_out=neg_m[c][:],
             )
 
-        v_g10 = sb.tile([P, PASS], BF16, name="v_g10")
+        v_g10 = sb.tile([P, PASS], BF16, name="v_g10", tag="v_bf0", align_bytes=64)
         nc.scalar.activation(v_g10[:], v_bf1[:].indirect(listed_range(0, PASS)), ACT.Copy)
         p_sb = sb.tile([P, G, 4, P], F32, name="p_sb")
-        l_part = [sb.tile([P, 1], F32, name=f"l_part{g}") for g in range(G)]
+        l_part = sb.tile([P, 2 * G], F32, name="l_part")
         for g in range(G):
-            nc.scalar.activation(
-                p_sb[:, g, :, :], neg_s[:, g, :, :], ACT.Exp, bias=neg_m[-1][:], scale=-1.0, accum_out=l_part[g][:]
-            )
+            for u in range(2):
+                nc.scalar.activation(
+                    p_sb[:, g, 2 * u : 2 * u + 2, :],
+                    neg_s[:, g, 2 * u : 2 * u + 2, :],
+                    ACT.Exp,
+                    bias=neg_m[-1][:],
+                    scale=-1.0,
+                    accum_out=l_part[:, 2 * g + u : 2 * g + u + 1],
+                )
 
+        l_copy = sb.tile([P, 2 * G], F32, name="l_copy")
         l_sum = sb.tile([P, 1], F32, name="l_sum")
-        nc.scalar.activation(l_sum[:], l_part[0][:], ACT.Identity, bias=l_part[1][:])
+        nc.scalar.activation(l_copy[:], l_part[:], ACT.Identity, accum_out=l_sum[:])
+
+        v_g11 = sb.tile([P, PASS], BF16, name="v_g11", tag="neg_m0", align_bytes=64)
+        nc.vector.tensor_copy(v_g11[:], v_bf1[:].indirect(listed_range(PASS, PASS)))
 
         v_codes = sb.tile([P, 2, G, P], U32, name="v_codes", align_bytes=64)
-        v_sc = sb.tile([P, 2, G, P], U8, name="v_sc", tag="neg_m0", align_bytes=64)
+        v_sc = sb.tile([P, 2, G, P], U8, name="v_sc", tag="v_bf1", align_bytes=64)
 
         def turn_values(name, tag, slot, source):
             passes = source.shape[1] // PASS
@@ -202,11 +212,8 @@ def tile_attend_bias_kernel(tc, qT, k_words, k_scales, vT, vs, kb, offs, out):
                 in_=v_il[:].rearrange("p g e t -> p (g e t)"),
             )
 
-        v_il0 = turn_values("0", "c0", "v_bf0", v_g0[:])
+        v_il0 = turn_values("0", "c0", "ks_pool", v_g0[:])
         v_il10 = turn_values("10", "c1", "neg_m1", v_g10[:])
-        quantize_values(0, 0, v_il0)
-        v_g11 = sb.tile([P, PASS], BF16, name="v_g11", tag="v_bf0", align_bytes=64)
-        nc.vector.tensor_copy(v_g11[:], v_bf1[:].indirect(listed_range(PASS, PASS)))
 
         w_il = sb.tile([P, G, NQ, 4], BF16, name="w_il", align_bytes=64)
         w_codes = sb.tile([P, G, NQ], U32, name="w_codes", align_bytes=64)
@@ -221,6 +228,7 @@ def tile_attend_bias_kernel(tc, qT, k_words, k_scales, vT, vs, kb, offs, out):
                 vs_col[g][:].unsqueeze(1).to_broadcast([P, NQ, 4]),
                 ALU.mult,
             )
+        quantize_values(0, 0, v_il0)
         v_il11 = turn_values("11", "b0", "v_il11", v_g11[:])
         l_inv = sb.tile([P, 1], F32, name="l_inv")
         nc.vector.reciprocal(l_inv[:], l_sum[:])

@@ -41,22 +41,18 @@ def tile_attend_bias_kernel(tc, qT, k_words, k_scales, vT, vs, kb, offs, out):
         nc.vector.memset(ks_pool[0:96, :].bitcast(I32), 0)
         kb_pool = sb.tile([P, T], F32, name="kb_pool", tag="gathered0", align_bytes=64)
         nc.scalar.dma_start(kb_pool[LIVE:P, :], kb[0:1, :])
-        v_raw = [
-            [sb.tile([P, T // 2], F32, name=f"v_raw{h}{c}", tag=f"v_raw{h}{c}") for c in range(2)] for h in range(2)
-        ]
+        v_raw0 = [sb.tile([P, T // 2], F32, name=f"v_raw0{c}", tag=f"v_raw0{c}", align_bytes=64) for c in range(2)]
+        v_raw1 = sb.tile([P, T], F32, name="v_raw1", tag="v_raw1", align_bytes=64)
 
         def columns(c):
             return slice(c * T // 2, (c + 1) * T // 2)
 
-        def load_values(h):
-            for c in range(2):
-                nc.sync.dma_start(v_raw[h][c][:], vT[h * P : (h + 1) * P, columns(c)])
-
         q_raw = sb.tile([P, 2, 4, NQ], F32, name="q_raw", tag="q_raw", align_bytes=64)
         nc.sync.dma_start(q_raw[:], qT[0].rearrange("(o p j) w -> p o j w", o=2, j=4))
-        load_values(0)
         kw_pool = sb.tile([P, T], I32, name="kw_pool")
         nc.sync.dma_start(kw_pool[:], k_words[0].rearrange("p t b -> p (t b)").bitcast(I32))
+        for c in range(2):
+            nc.sync.dma_start(v_raw0[c][:], vT[0:P, columns(c)])
 
         k_sc = sb.tile([P, 2, N], U8, name="k_sc", align_bytes=64)
         nc.vector.memset(k_sc[:].bitcast(I32), 0)
@@ -76,30 +72,27 @@ def tile_attend_bias_kernel(tc, qT, k_words, k_scales, vT, vs, kb, offs, out):
         vs_pool = sb.tile([P, T], F32, name="vs_pool", tag="ks_pool", align_bytes=64)
         nc.sync.dma_start(vs_pool[LIVE:P, :], vs[0:1, :])
         nc.gpsimd.memset(vs_pool[0:LIVE, :], 0.0)
-        load_values(1)
+        nc.sync.dma_start(v_raw1[:], vT[P:DV, :])
         kb_g = sb.tile([P, N], F32, name="kb_g")
         nc.vector.tensor_copy(kb_g[:], kb_pool[:].indirect(offsets[:]))
 
         v_bf0 = sb.tile([P, T], BF16, name="v_bf0", tag="v_bf0", align_bytes=64)
-        v_bf1 = sb.tile([P, T], BF16, name="v_bf1", tag="v_bf1", align_bytes=64)
-        v_g0 = sb.tile([P, N], BF16, name="v_g0")
+        v_g00 = sb.tile([P, PASS], BF16, name="v_g00")
 
         def listed_range(start, count):
             return offsets[:, start // 16 : (start + count) // 16]
 
         for c in range(2):
-            nc.scalar.activation(v_bf0[:, columns(c)], v_raw[0][c][:], ACT.Copy)
-        nc.scalar.activation(v_g0[:], v_bf0[:].indirect(offsets[:]), ACT.Copy)
+            nc.scalar.activation(v_bf0[:, columns(c)], v_raw0[c][:], ACT.Copy)
 
-        kb_col = sb.tile([P, N // P], F32, name="kb_col", tag="v_bf0", align_bytes=64)
+        kb_col = sb.tile([P, N // P], F32, name="kb_col", tag="v_raw01", align_bytes=64)
         for g in range(G):
             turned = bank(f"a{g}", f"kb_turned{g}")
             for b in range(4):
                 c0 = g * PASS + b * P
                 nc.tensor.transpose(turned[:, b, :], kb_g[:, c0 : c0 + P], ident[:])
             nc.scalar.copy(kb_col[:, 4 * g : 4 * g + 4], turned[:, :, LIVE])
-        for c in range(2):
-            nc.scalar.activation(v_bf1[:, columns(c)], v_raw[1][c][:], ACT.Copy)
+        nc.scalar.activation(v_g00[:], v_bf0[:].indirect(listed_range(0, PASS)), ACT.Copy)
 
         chunks = [(c * 256, 256) for c in range(4)]
 
@@ -132,7 +125,7 @@ def tile_attend_bias_kernel(tc, qT, k_words, k_scales, vT, vs, kb, offs, out):
         for g in range(G):
             nc.sync.dma_start(vs_col[g][:], vs_g[LIVE:P, g * PASS : (g + 1) * PASS])
 
-        s_t = sb.tile([P, N // P, NQ], F32, name="s_t", tag="v_raw11")
+        s_t = sb.tile([P, N // P, NQ], F32, name="s_t")
         neg_s = sb.tile([P, G, 4, P], F32, name="neg_s", tag="ks_pool", align_bytes=64)
         neg_m = [sb.tile([P, 1], F32, name=f"neg_m{c}", tag=f"neg_m{c}", align_bytes=64) for c in range(G)]
         raw_tag = ["b0", "c1", "b1", "d"]
@@ -167,8 +160,8 @@ def tile_attend_bias_kernel(tc, qT, k_words, k_scales, vT, vs, kb, offs, out):
                 accum_out=neg_m[c][:],
             )
 
-        v_g10 = sb.tile([P, PASS], BF16, name="v_g10", tag="v_bf0", align_bytes=64)
-        nc.scalar.activation(v_g10[:], v_bf1[:].indirect(listed_range(0, PASS)), ACT.Copy)
+        v_g01 = sb.tile([P, PASS], BF16, name="v_g01", tag="v_raw01", align_bytes=64)
+        nc.scalar.activation(v_g01[:], v_bf0[:].indirect(listed_range(PASS, PASS)), ACT.Copy)
         p_sb = sb.tile([P, G, 4, P], F32, name="p_sb")
         l_part = sb.tile([P, 2 * G], F32, name="l_part")
         for g in range(G):
@@ -182,38 +175,33 @@ def tile_attend_bias_kernel(tc, qT, k_words, k_scales, vT, vs, kb, offs, out):
                     accum_out=l_part[:, 2 * g + u : 2 * g + u + 1],
                 )
 
-        l_copy = sb.tile([P, 2 * G], F32, name="l_copy")
-        l_sum = sb.tile([P, 1], F32, name="l_sum")
-        nc.scalar.activation(l_copy[:], l_part[:], ACT.Identity, accum_out=l_sum[:])
-
-        v_g11 = sb.tile([P, PASS], BF16, name="v_g11", tag="neg_m0", align_bytes=64)
-        nc.vector.tensor_copy(v_g11[:], v_bf1[:].indirect(listed_range(PASS, PASS)))
+        v_g1 = sb.tile([P, N], BF16, name="v_g1", tag="neg_m0", align_bytes=64)
+        nc.vector.tensor_copy(v_g1[:], v_raw1[:].indirect(offsets[:]))
 
         v_codes = sb.tile([P, 2, G, P], U32, name="v_codes", align_bytes=64)
-        v_sc = sb.tile([P, 2, G, P], U8, name="v_sc", tag="v_bf1", align_bytes=64)
+        v_sc = sb.tile([P, 2, G, P], U8, name="v_sc", tag="v_raw1", align_bytes=64)
 
-        def turn_values(name, tag, slot, source):
-            passes = source.shape[1] // PASS
-            turned = bank(tag, f"v_turned{name}")
-            words = source.bitcast(F32)
-            for g in range(passes):
+        def turn_values(h, slot, sources):
+            turned = bank("c0", f"v_turned{h}")
+            for g in range(G):
+                words = sources[g].bitcast(F32)
                 for u in range(2):
-                    first = g * PASS // 2
-                    nc.tensor.transpose(turned[:, 2 * g + u, :], words[:, first + u : first + PASS // 2 : 2], ident[:])
-            v_il = sb.tile([P, passes, P, 4], BF16, name=f"v_il{name}", tag=slot, align_bytes=64)
-            nc.scalar.copy(v_il[:].bitcast(F32), turned[:, 0 : 2 * passes, :].rearrange("p (g u) e -> p g e u", u=2))
+                    nc.tensor.transpose(turned[:, 2 * g + u, :], words[:, u : PASS // 2 : 2], ident[:])
+            v_il = sb.tile([P, G, P, 4], BF16, name=f"v_il{h}", tag=slot, align_bytes=64)
+            nc.scalar.copy(v_il[:].bitcast(F32), turned[:].rearrange("p (g u) e -> p g e u", u=2))
             return v_il
 
-        def quantize_values(h, g0, v_il):
-            gs = slice(g0, g0 + v_il.shape[1])
+        def quantize_values(h, v_il):
             nc.vector.quantize_mx(
-                out=v_codes[:, h, gs, :].rearrange("p g e -> p (g e)").bitcast(FP8X4),
-                scales=v_sc[:, h, gs, :].rearrange("p g e -> p (g e)"),
+                out=v_codes[:, h].rearrange("p g e -> p (g e)").bitcast(FP8X4),
+                scales=v_sc[:, h].rearrange("p g e -> p (g e)"),
                 in_=v_il[:].rearrange("p g e t -> p (g e t)"),
             )
 
-        v_il0 = turn_values("0", "c0", "ks_pool", v_g0[:])
-        v_il10 = turn_values("10", "c1", "neg_m1", v_g10[:])
+        v_il0 = turn_values(0, "neg_m1", [v_g00[:], v_g01[:]])
+
+        l_sum = sb.tile([P, 1], F32, name="l_sum")
+        nc.scalar.activation(l_part[:], l_part[:], ACT.Identity, accum_out=l_sum[:])
 
         w_il = sb.tile([P, G, NQ, 4], BF16, name="w_il", align_bytes=64)
         w_codes = sb.tile([P, G, NQ], U32, name="w_codes", align_bytes=64)
@@ -228,16 +216,15 @@ def tile_attend_bias_kernel(tc, qT, k_words, k_scales, vT, vs, kb, offs, out):
                 vs_col[g][:].unsqueeze(1).to_broadcast([P, NQ, 4]),
                 ALU.mult,
             )
-        quantize_values(0, 0, v_il0)
-        v_il11 = turn_values("11", "b0", "v_il11", v_g11[:])
+        v_il1 = turn_values(1, "v_il1", [v_g1[:, 0:PASS], v_g1[:, PASS:N]])
         l_inv = sb.tile([P, 1], F32, name="l_inv")
         nc.vector.reciprocal(l_inv[:], l_sum[:])
         for g in range(G):
             nc.vector.quantize_mx(
                 out=w_codes[:, g, :].bitcast(FP8X4), scales=w_sc[:, g, :], in_=w_il[:, g].rearrange("p q t -> p (q t)")
             )
-        quantize_values(1, 0, v_il10)
-        quantize_values(1, 1, v_il11)
+        quantize_values(0, v_il0)
+        quantize_values(1, v_il1)
 
         for h in range(2):
             y_ps = ps.tile([P, P], F32, tag=["d", "e"][h], name=f"y_ps{h}")

@@ -77,7 +77,6 @@ def tile_attend_bias_kernel(tc, qT, k_words, k_scales, vT, vs, kb, offs, out):
         nc.vector.tensor_copy(kb_g[:], kb_pool[:].indirect(offsets[:]))
 
         v_bf0 = sb.tile([P, T], BF16, name="v_bf0", tag="v_bf0", align_bytes=64)
-        v_g00 = sb.tile([P, PASS], BF16, name="v_g00")
 
         def listed_range(start, count):
             return offsets[:, start // 16 : (start + count) // 16]
@@ -85,14 +84,13 @@ def tile_attend_bias_kernel(tc, qT, k_words, k_scales, vT, vs, kb, offs, out):
         for c in range(2):
             nc.scalar.activation(v_bf0[:, columns(c)], v_raw0[c][:], ACT.Copy)
 
-        kb_col = sb.tile([P, N // P], F32, name="kb_col", tag="v_raw01", align_bytes=64)
+        kb_col = [sb.tile([P, 4], F32, name=f"kb_col{g}", tag=f"v_raw0{g}", align_bytes=64) for g in range(G)]
         for g in range(G):
             turned = bank(f"a{g}", f"kb_turned{g}")
             for b in range(4):
                 c0 = g * PASS + b * P
                 nc.tensor.transpose(turned[:, b, :], kb_g[:, c0 : c0 + P], ident[:])
-            nc.scalar.copy(kb_col[:, 4 * g : 4 * g + 4], turned[:, :, LIVE])
-        nc.scalar.activation(v_g00[:], v_bf0[:].indirect(listed_range(0, PASS)), ACT.Copy)
+            nc.scalar.copy(kb_col[g][:], turned[:, :, LIVE])
 
         chunks = [(c * 256, 256) for c in range(4)]
 
@@ -145,7 +143,7 @@ def tile_attend_bias_kernel(tc, qT, k_words, k_scales, vT, vs, kb, offs, out):
                     )
             for b in range(count // P):
                 blk = start // P + b
-                nc.scalar.activation(s_t[:, blk, :], raw[:, b, :], ACT.Identity, bias=kb_col[:, blk : blk + 1])
+                nc.scalar.activation(s_t[:, blk, :], raw[:, b, :], ACT.Identity, bias=kb_col[blk // 4][:, blk % 4 : blk % 4 + 1])
         for c in range(G):
             scores = bank(f"a{c}", f"scores{c}")
             for b in range(4):
@@ -160,8 +158,9 @@ def tile_attend_bias_kernel(tc, qT, k_words, k_scales, vT, vs, kb, offs, out):
                 accum_out=neg_m[c][:],
             )
 
-        v_g01 = sb.tile([P, PASS], BF16, name="v_g01", tag="v_raw01", align_bytes=64)
-        nc.scalar.activation(v_g01[:], v_bf0[:].indirect(listed_range(PASS, PASS)), ACT.Copy)
+        v_g0 = [sb.tile([P, PASS], BF16, name=f"v_g0{g}", tag=f"v_raw0{g}", align_bytes=64) for g in range(G)]
+        for g in range(G):
+            nc.scalar.activation(v_g0[g][:], v_bf0[:].indirect(listed_range(g * PASS, PASS)), ACT.Copy)
         p_sb = sb.tile([P, G, 4, P], F32, name="p_sb")
         l_part = sb.tile([P, 2 * G], F32, name="l_part")
         for g in range(G):
@@ -198,7 +197,7 @@ def tile_attend_bias_kernel(tc, qT, k_words, k_scales, vT, vs, kb, offs, out):
                 in_=v_il[:].rearrange("p g e t -> p (g e t)"),
             )
 
-        v_il0 = turn_values(0, "neg_m1", [v_g00[:], v_g01[:]])
+        v_il0 = turn_values(0, "neg_m1", [v_g0[0][:], v_g0[1][:]])
 
         l_sum = sb.tile([P, 1], F32, name="l_sum")
         nc.scalar.activation(l_part[:], l_part[:], ACT.Identity, accum_out=l_sum[:])

@@ -181,21 +181,14 @@ def tile_attend_bias_kernel(tc, qT, k_words, k_scales, vT, vs, kb, offs, out):
         v_sc = sb.tile([P, 2, G, P], U8, name="v_sc", tag="v_raw1", align_bytes=64)
 
         def turn_values(h, slot, sources):
-            turned = bank("c0", f"v_turned{h}")
+            v_il = sb.tile([P, G, P, 4], BF16, name=f"v_il{h}", tag=slot, align_bytes=64)
             for g in range(G):
+                turned = bank(f"c{g}", f"v_turned{h}{g}")
                 words = sources[g].bitcast(F32)
                 for u in range(2):
-                    nc.tensor.transpose(turned[:, 2 * g + u, :], words[:, u : PASS // 2 : 2], ident[:])
-            v_il = sb.tile([P, G, P, 4], BF16, name=f"v_il{h}", tag=slot, align_bytes=64)
-            nc.scalar.copy(v_il[:].bitcast(F32), turned[:].rearrange("p (g u) e -> p g e u", u=2))
+                    nc.tensor.transpose(turned[:, u, :], words[:, u : PASS // 2 : 2], ident[:])
+                nc.scalar.copy(v_il[:, g].bitcast(F32), turned[:, 0:2, :].rearrange("p u e -> p e u"))
             return v_il
-
-        def quantize_values(h, v_il):
-            nc.vector.quantize_mx(
-                out=v_codes[:, h].rearrange("p g e -> p (g e)").bitcast(FP8X4),
-                scales=v_sc[:, h].rearrange("p g e -> p (g e)"),
-                in_=v_il[:].rearrange("p g e t -> p (g e t)"),
-            )
 
         v_il0 = turn_values(0, "neg_m1", [v_g0[0][:], v_g0[1][:]])
 
@@ -222,8 +215,17 @@ def tile_attend_bias_kernel(tc, qT, k_words, k_scales, vT, vs, kb, offs, out):
             nc.vector.quantize_mx(
                 out=w_codes[:, g, :].bitcast(FP8X4), scales=w_sc[:, g, :], in_=w_il[:, g].rearrange("p q t -> p (q t)")
             )
-        quantize_values(0, v_il0)
-        quantize_values(1, v_il1)
+        nc.vector.quantize_mx(
+            out=v_codes[:, 0].rearrange("p g e -> p (g e)").bitcast(FP8X4),
+            scales=v_sc[:, 0].rearrange("p g e -> p (g e)"),
+            in_=v_il0[:].rearrange("p g e t -> p (g e t)"),
+        )
+        for g in range(G):
+            nc.vector.quantize_mx(
+                out=v_codes[:, 1, g].bitcast(FP8X4),
+                scales=v_sc[:, 1, g],
+                in_=v_il1[:, g].rearrange("p e t -> p (e t)"),
+            )
 
         for h in range(2):
             y_ps = ps.tile([P, P], F32, tag=["d", "e"][h], name=f"y_ps{h}")

@@ -36,55 +36,45 @@ def tile_attend_bias_kernel(tc, qT, k_words, k_scales, vT, vs, kb, offs, out):
         offsets = sb.tile([P, N // 16], U16, name="offsets")
         nc.sync.dma_start(offsets[:], offs)
 
-        ks_pool = sb.tile([P, T], U8, name="ks_pool", tag="ks_pool", align_bytes=64)
-        nc.sync.dma_start(ks_pool[96:P, :].bitcast(I32), k_scales.bitcast(I32).rearrange("o r w -> r o w"))
+        ks_pool = sb.tile([P, T + 4], U8, name="ks_pool", align_bytes=64)
+        nc.sync.dma_start(ks_pool[96:P, 0:T].bitcast(I32), k_scales.bitcast(I32).rearrange("o r w -> r o w"))
         nc.vector.memset(ks_pool[0:96, :].bitcast(I32), 0)
         kb_pool = sb.tile([P, T], F32, name="kb_pool", tag="gathered0", align_bytes=64)
         nc.scalar.dma_start(kb_pool[LIVE:P, :], kb[0:1, :])
-        v_raw0 = [sb.tile([P, T // 2], F32, name=f"v_raw0{c}", tag=f"v_raw0{c}", align_bytes=64) for c in range(2)]
-        v_raw1 = sb.tile([P, T], F32, name="v_raw1", tag="v_raw1", align_bytes=64)
-
-        def columns(c):
-            return slice(c * T // 2, (c + 1) * T // 2)
+        vs_pool = sb.tile([P, T], F32, name="vs_pool")
+        nc.scalar.dma_start(vs_pool[LIVE:P, :], vs[0:1, :])
+        v_raw = [sb.tile([P, T], F32, name=f"v_raw{h}", tag=f"v_raw{h}", align_bytes=64) for h in range(2)]
 
         q_raw = sb.tile([P, 2, 4, NQ], F32, name="q_raw", tag="q_raw", align_bytes=64)
         nc.sync.dma_start(q_raw[:], qT[0].rearrange("(o p j) w -> p o j w", o=2, j=4))
         kw_pool = sb.tile([P, T], I32, name="kw_pool")
         nc.sync.dma_start(kw_pool[:], k_words[0].rearrange("p t b -> p (t b)").bitcast(I32))
-        for c in range(2):
-            nc.sync.dma_start(v_raw0[c][:], vT[0:P, columns(c)])
+        for h in range(2):
+            nc.sync.dma_start(v_raw[h][:], vT[h * P : (h + 1) * P, :])
 
-        k_sc = sb.tile([P, 2, N], U8, name="k_sc", align_bytes=64)
+        k_sc = sb.tile([P, 2 * N + 4], U8, name="k_sc", align_bytes=64)
         nc.vector.memset(k_sc[:].bitcast(I32), 0)
         ident = sb.tile([P, P], F32, name="ident")
         make_identity(nc, ident[:])
         nc.gpsimd.memset(kb_pool[0:LIVE, :], 0.0)
+        nc.gpsimd.memset(vs_pool[0:LIVE, :], 0.0)
 
         q_bf = sb.tile([P, 2, NQ, 4], BF16, name="q_bf", align_bytes=64)
         nc.scalar.activation(q_bf[:], q_raw[:].rearrange("p o j w -> p o w j"), ACT.Copy)
 
         ks0 = sb.tile([P, N], U8, name="ks0", align_bytes=64)
-        nc.vector.tensor_copy(ks0[:], ks_pool[:].indirect(offsets[:]))
+        nc.vector.tensor_copy(ks0[:], ks_pool[:, 0:T].indirect(offsets[:]))
         for quad in range(4):
-            nc.sync.dma_start(
-                k_sc[32 * quad : 32 * quad + 4].bitcast(I32), ks0[96 + 8 * quad : 104 + 8 * quad, :].bitcast(I32)
+            nc.scalar.dma_start(
+                k_sc[32 * quad : 32 * quad + 4, 0 : 2 * N].bitcast(I32), ks0[96 + 8 * quad : 104 + 8 * quad, :].bitcast(I32)
             )
-        vs_pool = sb.tile([P, T], F32, name="vs_pool", tag="ks_pool", align_bytes=64)
-        nc.sync.dma_start(vs_pool[LIVE:P, :], vs[0:1, :])
-        nc.gpsimd.memset(vs_pool[0:LIVE, :], 0.0)
-        nc.sync.dma_start(v_raw1[:], vT[P:DV, :])
         kb_g = sb.tile([P, N], F32, name="kb_g")
         nc.vector.tensor_copy(kb_g[:], kb_pool[:].indirect(offsets[:]))
-
-        v_bf0 = sb.tile([P, T], BF16, name="v_bf0", tag="v_bf0", align_bytes=64)
 
         def listed_range(start, count):
             return offsets[:, start // 16 : (start + count) // 16]
 
-        for c in range(2):
-            nc.scalar.activation(v_bf0[:, columns(c)], v_raw0[c][:], ACT.Copy)
-
-        kb_col = [sb.tile([P, 4], F32, name=f"kb_col{g}", tag=f"v_raw0{g}", align_bytes=64) for g in range(G)]
+        kb_col = [sb.tile([P, 4], F32, name=f"kb_col{g}") for g in range(G)]
         for g in range(G):
             turned = bank(f"a{g}", f"kb_turned{g}")
             for b in range(4):
@@ -123,10 +113,13 @@ def tile_attend_bias_kernel(tc, qT, k_words, k_scales, vT, vs, kb, offs, out):
         for g in range(G):
             nc.sync.dma_start(vs_col[g][:], vs_g[LIVE:P, g * PASS : (g + 1) * PASS])
 
+        v_g0 = sb.tile([P, N], BF16, name="v_g0", tag="gathered3", align_bytes=64)
+        nc.vector.tensor_copy(v_g0[:], v_raw[0][:].indirect(offsets[:]))
+
         s_t = sb.tile([P, N // P, NQ], F32, name="s_t")
-        neg_s = sb.tile([P, G, 4, P], F32, name="neg_s", tag="ks_pool", align_bytes=64)
+        neg_s = sb.tile([P, G, 4, P], F32, name="neg_s")
         neg_m = [sb.tile([P, 1], F32, name=f"neg_m{c}", tag=f"neg_m{c}", align_bytes=64) for c in range(G)]
-        raw_tag = ["b0", "c1", "b1", "d"]
+        raw_tag = ["b0", "c0", "b1", "d"]
         for c, (start, count) in enumerate(chunks):
             raw = bank(raw_tag[c], f"raw{c}")
             for b in range(count // P):
@@ -135,7 +128,7 @@ def tile_attend_bias_kernel(tc, qT, k_words, k_scales, vT, vs, kb, offs, out):
                     nc.tensor.matmul_mx(
                         out=raw[:, b, :],
                         lhsT=k_codes[c][:, o, 2 * b * P : 2 * (b + 1) * P].bitcast(FP4X4),
-                        lhsT_scale=k_sc[:, o, c0 : c0 + P],
+                        lhsT_scale=k_sc[:, o * N + c0 : o * N + c0 + P],
                         rhs=q_codes[:, o * NQ : (o + 1) * NQ].bitcast(FP8X4),
                         rhs_scale=q_sc[:, o * NQ : (o + 1) * NQ],
                         start=(o == 0),
@@ -158,9 +151,12 @@ def tile_attend_bias_kernel(tc, qT, k_words, k_scales, vT, vs, kb, offs, out):
                 accum_out=neg_m[c][:],
             )
 
-        v_g0 = [sb.tile([P, PASS], BF16, name=f"v_g0{g}", tag=f"v_raw0{g}", align_bytes=64) for g in range(G)]
+        v_turned0 = bank("d", "v_turned0")
         for g in range(G):
-            nc.scalar.activation(v_g0[g][:], v_bf0[:].indirect(listed_range(g * PASS, PASS)), ACT.Copy)
+            words = v_g0[:, g * PASS : (g + 1) * PASS].bitcast(F32)
+            for u in range(2):
+                nc.tensor.transpose(v_turned0[:, 2 * g + u, :], words[:, u : PASS // 2 : 2], ident[:])
+
         p_sb = sb.tile([P, G, 4, P], F32, name="p_sb")
         l_part = sb.tile([P, 2 * G], F32, name="l_part")
         for g in range(G):
@@ -175,7 +171,8 @@ def tile_attend_bias_kernel(tc, qT, k_words, k_scales, vT, vs, kb, offs, out):
                 )
 
         v_g1 = sb.tile([P, N], BF16, name="v_g1", tag="neg_m0", align_bytes=64)
-        nc.vector.tensor_copy(v_g1[:], v_raw1[:].indirect(offsets[:]))
+        for g in range(G):
+            nc.vector.tensor_copy(v_g1[:, g * PASS : (g + 1) * PASS], v_raw[1][:].indirect(listed_range(g * PASS, PASS)))
 
         v_codes = sb.tile([P, 2, G, P], U32, name="v_codes", align_bytes=64)
         v_sc = sb.tile([P, 2, G, P], U8, name="v_sc", tag="v_raw1", align_bytes=64)
@@ -190,7 +187,8 @@ def tile_attend_bias_kernel(tc, qT, k_words, k_scales, vT, vs, kb, offs, out):
                 nc.scalar.copy(v_il[:, g].bitcast(F32), turned[:, 0:2, :].rearrange("p u e -> p e u"))
             return v_il
 
-        v_il0 = turn_values(0, "neg_m1", [v_g0[0][:], v_g0[1][:]])
+        v_il0 = sb.tile([P, G, P, 4], BF16, name="v_il0", tag="neg_m1", align_bytes=64)
+        nc.scalar.copy(v_il0[:].bitcast(F32), v_turned0[:].rearrange("p (g u) e -> p g e u", u=2))
 
         l_sum = sb.tile([P, 1], F32, name="l_sum")
         nc.scalar.activation(l_part[:], l_part[:], ACT.Identity, accum_out=l_sum[:])
@@ -228,7 +226,7 @@ def tile_attend_bias_kernel(tc, qT, k_words, k_scales, vT, vs, kb, offs, out):
             )
 
         for h in range(2):
-            y_ps = ps.tile([P, P], F32, tag=["d", "e"][h], name=f"y_ps{h}")
+            y_ps = ps.tile([P, P], F32, tag=["e", "a0"][h], name=f"y_ps{h}")
             for g in range(G):
                 nc.tensor.matmul_mx(
                     out=y_ps[:],

@@ -28,6 +28,7 @@ def tile_attend_bias_kernel(tc, qT, k_words, k_scales, vT, vs, kb, offs, out):
     nc = tc.nc
     with ExitStack() as ctx:
         sb = ctx.enter_context(tc.tile_pool(name="sb", bufs=1))
+        shared = ctx.enter_context(tc.tile_pool(name="shared", bufs=1))
         ps = ctx.enter_context(tc.psum_pool(name="ps", bufs=1))
 
         def bank(tag, name):
@@ -39,25 +40,24 @@ def tile_attend_bias_kernel(tc, qT, k_words, k_scales, vT, vs, kb, offs, out):
         ks_pool = sb.tile([P, T + 4], U8, name="ks_pool", align_bytes=64)
         nc.sync.dma_start(ks_pool[96:P, 0:T].bitcast(I32), k_scales.bitcast(I32).rearrange("o r w -> r o w"))
         nc.vector.memset(ks_pool[0:96, :].bitcast(I32), 0)
-        kb_pool = sb.tile([P, T], F32, name="kb_pool", tag="gathered0", align_bytes=64)
+        kb_pool = sb.tile([P, T], F32, name="kb_pool")
         nc.scalar.dma_start(kb_pool[LIVE:P, :], kb[0:1, :])
-        vs_pool = sb.tile([P, T], F32, name="vs_pool")
-        nc.scalar.dma_start(vs_pool[LIVE:P, :], vs[0:1, :])
+        vs_pool = shared.tile([P, 8 + T], F32, name="vs_pool", offset=0, align_bytes=64)
+        nc.scalar.dma_start(vs_pool[LIVE:P, 8:], vs[0:1, :])
         v_raw = [sb.tile([P, T], F32, name=f"v_raw{h}", tag=f"v_raw{h}", align_bytes=64) for h in range(2)]
 
         q_raw = sb.tile([P, 2, 4, NQ], F32, name="q_raw", tag="q_raw", align_bytes=64)
         nc.sync.dma_start(q_raw[:], qT[0].rearrange("(o p j) w -> p o j w", o=2, j=4))
         kw_pool = sb.tile([P, T], I32, name="kw_pool")
         nc.sync.dma_start(kw_pool[:], k_words[0].rearrange("p t b -> p (t b)").bitcast(I32))
-        for h in range(2):
-            nc.sync.dma_start(v_raw[h][:], vT[h * P : (h + 1) * P, :])
 
+        nc.vector.memset(vs_pool[0:LIVE, 7:768], 0.0)
         k_sc = sb.tile([P, 2 * N + 4], U8, name="k_sc", align_bytes=64)
         nc.vector.memset(k_sc[:].bitcast(I32), 0)
         ident = sb.tile([P, P], F32, name="ident")
         make_identity(nc, ident[:])
         nc.gpsimd.memset(kb_pool[0:LIVE, :], 0.0)
-        nc.gpsimd.memset(vs_pool[0:LIVE, :], 0.0)
+        nc.gpsimd.memset(vs_pool[0:LIVE, 768:], 0.0)
 
         q_bf = sb.tile([P, 2, NQ, 4], BF16, name="q_bf", align_bytes=64)
         nc.scalar.activation(q_bf[:], q_raw[:].rearrange("p o j w -> p o w j"), ACT.Copy)
@@ -65,11 +65,18 @@ def tile_attend_bias_kernel(tc, qT, k_words, k_scales, vT, vs, kb, offs, out):
         ks0 = sb.tile([P, N], U8, name="ks0", align_bytes=64)
         nc.vector.tensor_copy(ks0[:], ks_pool[:, 0:T].indirect(offsets[:]))
         for quad in range(4):
-            nc.scalar.dma_start(
+            nc.sync.dma_start(
                 k_sc[32 * quad : 32 * quad + 4, 0 : 2 * N].bitcast(I32), ks0[96 + 8 * quad : 104 + 8 * quad, :].bitcast(I32)
             )
+        for h in range(2):
+            nc.sync.dma_start(v_raw[h][:], vT[h * P : (h + 1) * P, :])
         kb_g = sb.tile([P, N], F32, name="kb_g")
         nc.vector.tensor_copy(kb_g[:], kb_pool[:].indirect(offsets[:]))
+        vs_col = [sb.tile([P, 4], F32, name=f"vs_col{g}") for g in range(G)]
+        vs_g = sb.tile([P, N], F32, name="vs_g")
+        nc.vector.tensor_copy(vs_g[:], vs_pool[:, 8:].indirect(offsets[:]))
+        for g in range(G):
+            nc.sync.dma_start(vs_col[g][:], vs_g[LIVE:P, g * PASS : (g + 1) * PASS])
 
         def listed_range(start, count):
             return offsets[:, start // 16 : (start + count) // 16]
@@ -84,15 +91,17 @@ def tile_attend_bias_kernel(tc, qT, k_words, k_scales, vT, vs, kb, offs, out):
 
         chunks = [(c * 256, 256) for c in range(4)]
 
-        kw_g = [sb.tile([P, n], I32, name=f"kw_g{c}", tag=f"gathered{c}", align_bytes=64) for c, (s0, n) in enumerate(chunks)]
+        kw_g = [
+            shared.tile([P, n], I32, name=f"kw_g{c}", offset=4 * s0, align_bytes=64)[:] for c, (s0, n) in enumerate(chunks)
+        ]
         k_codes = [sb.tile([P, 2, 2 * n], U8, name=f"k_codes{c}", align_bytes=64) for c, (s0, n) in enumerate(chunks)]
 
         def gather_words(c):
-            nc.vector.tensor_copy(kw_g[c][:].bitcast(U32), kw_pool[:].bitcast(U32).indirect(listed_range(*chunks[c])))
+            nc.vector.tensor_copy(kw_g[c].bitcast(U32), kw_pool[:].bitcast(U32).indirect(listed_range(*chunks[c])))
 
         def part_words(c):
             nc.vector.tensor_copy(
-                k_codes[c][:].bitcast(U16), kw_g[c][:].bitcast(U16).rearrange("p (n o) -> p o n", o=2)
+                k_codes[c][:].bitcast(U16), kw_g[c].bitcast(U16).rearrange("p (n o) -> p o n", o=2)
             )
 
         q_codes = sb.tile([P, 2 * NQ], U32, name="q_codes", align_bytes=64)
@@ -107,17 +116,10 @@ def tile_attend_bias_kernel(tc, qT, k_words, k_scales, vT, vs, kb, offs, out):
             part_words(c - 1)
         part_words(len(chunks) - 1)
 
-        vs_col = [sb.tile([P, 4], F32, name=f"vs_col{g}") for g in range(G)]
-        vs_g = sb.tile([P, N], F32, name="vs_g", tag="gathered2", align_bytes=64)
-        nc.vector.tensor_copy(vs_g[:], vs_pool[:].indirect(offsets[:]))
-        for g in range(G):
-            nc.sync.dma_start(vs_col[g][:], vs_g[LIVE:P, g * PASS : (g + 1) * PASS])
-
-        v_g0 = sb.tile([P, N], BF16, name="v_g0", tag="gathered3", align_bytes=64)
-        nc.vector.tensor_copy(v_g0[:], v_raw[0][:].indirect(offsets[:]))
-
-        s_t = sb.tile([P, N // P, NQ], F32, name="s_t")
-        neg_s = sb.tile([P, G, 4, P], F32, name="neg_s")
+        v_g0 = [shared.tile([P, PASS], BF16, name="v_g00", offset=4 * chunks[2][0], align_bytes=64)]
+        nc.vector.tensor_copy(v_g0[0][:], v_raw[0][:].indirect(listed_range(0, PASS)))
+        s_t = [sb.tile([P, 4, NQ], F32, name=f"s_t{g}", tag=f"s_t{g}", align_bytes=64) for g in range(G)]
+        neg_s = [sb.tile([P, 4, P], F32, name=f"neg_s{g}", tag=["neg_s0", "v_raw0"][g], align_bytes=64) for g in range(G)]
         neg_m = [sb.tile([P, 1], F32, name=f"neg_m{c}", tag=f"neg_m{c}", align_bytes=64) for c in range(G)]
         raw_tag = ["b0", "c0", "b1", "d"]
         for c, (start, count) in enumerate(chunks):
@@ -136,13 +138,13 @@ def tile_attend_bias_kernel(tc, qT, k_words, k_scales, vT, vs, kb, offs, out):
                     )
             for b in range(count // P):
                 blk = start // P + b
-                nc.scalar.activation(s_t[:, blk, :], raw[:, b, :], ACT.Identity, bias=kb_col[blk // 4][:, blk % 4 : blk % 4 + 1])
+                nc.scalar.activation(s_t[blk // 4][:, blk % 4, :], raw[:, b, :], ACT.Identity, bias=kb_col[blk // 4][:, blk % 4 : blk % 4 + 1])
         for c in range(G):
             scores = bank(f"a{c}", f"scores{c}")
             for b in range(4):
-                nc.tensor.transpose(scores[:, b, :], s_t[:, 4 * c + b, :], ident[:])
+                nc.tensor.transpose(scores[:, b, :], s_t[c][:, b, :], ident[:])
             nc.vector.tensor_scalar(
-                neg_s[:, c].rearrange("q t p -> q p t"),
+                neg_s[c][:].rearrange("q t p -> q p t"),
                 scores[:].rearrange("q b c -> q (b c)").rearrange("q (p t) -> q p t", t=4),
                 -1.0,
                 neg_m[c - 1][:] if c else None,
@@ -150,10 +152,13 @@ def tile_attend_bias_kernel(tc, qT, k_words, k_scales, vT, vs, kb, offs, out):
                 ALU.min,
                 accum_out=neg_m[c][:],
             )
+            if c == 0:
+                v_g0.append(sb.tile([P, PASS], BF16, name="v_g01", tag="s_t0", align_bytes=64))
+                nc.vector.tensor_copy(v_g0[1][:], v_raw[0][:].indirect(listed_range(PASS, PASS)))
 
         v_turned0 = bank("d", "v_turned0")
         for g in range(G):
-            words = v_g0[:, g * PASS : (g + 1) * PASS].bitcast(F32)
+            words = v_g0[g][:].bitcast(F32)
             for u in range(2):
                 nc.tensor.transpose(v_turned0[:, 2 * g + u, :], words[:, u : PASS // 2 : 2], ident[:])
 
@@ -163,7 +168,7 @@ def tile_attend_bias_kernel(tc, qT, k_words, k_scales, vT, vs, kb, offs, out):
             for u in range(2):
                 nc.scalar.activation(
                     p_sb[:, g, 2 * u : 2 * u + 2, :],
-                    neg_s[:, g, 2 * u : 2 * u + 2, :],
+                    neg_s[g][:, 2 * u : 2 * u + 2, :],
                     ACT.Exp,
                     bias=neg_m[-1][:],
                     scale=-1.0,

@@ -119,7 +119,7 @@ def tile_attend_bias_kernel(tc, qT, k_words, k_scales, vT, vs, kb, offs, out):
         v_g0 = [shared.tile([P, PASS], BF16, name="v_g00", offset=4 * chunks[2][0], align_bytes=64)]
         nc.vector.tensor_copy(v_g0[0][:], v_raw[0][:].indirect(listed_range(0, PASS)))
         s_t = [sb.tile([P, 4, NQ], F32, name=f"s_t{g}", tag=f"s_t{g}", align_bytes=64) for g in range(G)]
-        neg_s = [sb.tile([P, 4, P], F32, name=f"neg_s{g}", tag=["neg_s0", "v_raw0"][g], align_bytes=64) for g in range(G)]
+        neg_s = [sb.tile([P, PASS], F32, name=f"neg_s{g}", tag=["neg_s0", "v_raw0"][g], align_bytes=64) for g in range(G)]
         neg_m = [sb.tile([P, 1], F32, name=f"neg_m{c}", tag=f"neg_m{c}", align_bytes=64) for c in range(G)]
         raw_tag = ["b0", "c0", "b1", "d"]
         for c, (start, count) in enumerate(chunks):
@@ -144,8 +144,8 @@ def tile_attend_bias_kernel(tc, qT, k_words, k_scales, vT, vs, kb, offs, out):
             for b in range(4):
                 nc.tensor.transpose(scores[:, b, :], s_t[c][:, b, :], ident[:])
             nc.vector.tensor_scalar(
-                neg_s[c][:].rearrange("q t p -> q p t"),
-                scores[:].rearrange("q b c -> q (b c)").rearrange("q (p t) -> q p t", t=4),
+                neg_s[c][:],
+                scores[:].rearrange("q b c -> q (b c)"),
                 -1.0,
                 neg_m[c - 1][:] if c else None,
                 ALU.mult,
@@ -167,8 +167,8 @@ def tile_attend_bias_kernel(tc, qT, k_words, k_scales, vT, vs, kb, offs, out):
         for g in range(G):
             for u in range(2):
                 nc.scalar.activation(
-                    p_sb[:, g, 2 * u : 2 * u + 2, :],
-                    neg_s[g][:, 2 * u : 2 * u + 2, :],
+                    p_sb[:, g, 2 * u : 2 * u + 2, :].rearrange("q e p -> q p e"),
+                    neg_s[g][:].rearrange("q (p t) -> q p t", t=4)[:, :, 2 * u : 2 * u + 2],
                     ACT.Exp,
                     bias=neg_m[-1][:],
                     scale=-1.0,

@@ -81,7 +81,7 @@ def tile_attend_bias_kernel(tc, qT, k_words, k_scales, vT, vs, kb, offs, out):
         def listed_range(start, count):
             return offsets[:, start // 16 : (start + count) // 16]
 
-        kb_col = [sb.tile([P, 4], F32, name=f"kb_col{g}") for g in range(G)]
+        kb_col = [sb.tile([P, 4], F32, name=f"kb_col{g}", tag=f"kb_col{g}", align_bytes=64) for g in range(G)]
         for g in range(G):
             turned = bank(f"a{g}", f"kb_turned{g}")
             for b in range(4):
@@ -119,7 +119,8 @@ def tile_attend_bias_kernel(tc, qT, k_words, k_scales, vT, vs, kb, offs, out):
         v_g0 = [shared.tile([P, PASS], BF16, name="v_g00", offset=4 * chunks[2][0], align_bytes=64)]
         nc.vector.tensor_copy(v_g0[0][:], v_raw[0][:].indirect(listed_range(0, PASS)))
         s_t = [sb.tile([P, 4, NQ], F32, name=f"s_t{g}", tag=f"s_t{g}", align_bytes=64) for g in range(G)]
-        neg_s = [sb.tile([P, PASS], F32, name=f"neg_s{g}", tag=["neg_s0", "v_raw0"][g], align_bytes=64) for g in range(G)]
+        unused = sb.tile([P, PASS], BF16, name="unused")
+        scores = []
         neg_m = [sb.tile([P, 1], F32, name=f"neg_m{c}", tag=f"neg_m{c}", align_bytes=64) for c in range(G)]
         raw_tag = ["b0", "c0", "b1", "d"]
         for c, (start, count) in enumerate(chunks):
@@ -140,20 +141,18 @@ def tile_attend_bias_kernel(tc, qT, k_words, k_scales, vT, vs, kb, offs, out):
                 blk = start // P + b
                 nc.scalar.activation(s_t[blk // 4][:, blk % 4, :], raw[:, b, :], ACT.Identity, bias=kb_col[blk // 4][:, blk % 4 : blk % 4 + 1])
         for c in range(G):
-            scores = bank(f"a{c}", f"scores{c}")
+            turned = bank(f"a{c}", f"scores{c}")
             for b in range(4):
-                nc.tensor.transpose(scores[:, b, :], s_t[c][:, b, :], ident[:])
-            nc.vector.tensor_scalar(
-                neg_s[c][:],
-                scores[:].rearrange("q b c -> q (b c)"),
-                -1.0,
-                neg_m[c - 1][:] if c else None,
-                ALU.mult,
-                ALU.min,
-                accum_out=neg_m[c][:],
-            )
+                nc.tensor.transpose(turned[:, b, :], s_t[c][:, b, :], ident[:])
+            scores.append(turned[:].rearrange("q b c -> q (b c)"))
             if c == 0:
-                v_g0.append(sb.tile([P, PASS], BF16, name="v_g01", tag="s_t0", align_bytes=64))
+                nc.vector.tensor_reduce(neg_m[0][:], scores[0], mybir.AxisListType.X, ALU.max, negate=True)
+            else:
+                nc.vector.tensor_scalar(
+                    unused[:], scores[1], -1.0, neg_m[0][:], ALU.mult, ALU.min, accum_out=neg_m[1][:]
+                )
+            if c == 0:
+                v_g0.append(sb.tile([P, PASS], BF16, name="v_g01", tag="kb_col1", align_bytes=64))
                 nc.vector.tensor_copy(v_g0[1][:], v_raw[0][:].indirect(listed_range(PASS, PASS)))
 
         v_turned0 = bank("d", "v_turned0")
@@ -168,14 +167,13 @@ def tile_attend_bias_kernel(tc, qT, k_words, k_scales, vT, vs, kb, offs, out):
             for u in range(2):
                 nc.scalar.activation(
                     p_sb[:, g, 2 * u : 2 * u + 2, :].rearrange("q e p -> q p e"),
-                    neg_s[g][:].rearrange("q (p t) -> q p t", t=4)[:, :, 2 * u : 2 * u + 2],
+                    scores[g].rearrange("q (p t) -> q p t", t=4)[:, :, 2 * u : 2 * u + 2],
                     ACT.Exp,
                     bias=neg_m[-1][:],
-                    scale=-1.0,
                     accum_out=l_part[:, 2 * g + u : 2 * g + u + 1],
                 )
 
-        v_g1 = sb.tile([P, N], BF16, name="v_g1", tag="neg_m0", align_bytes=64)
+        v_g1 = shared.tile([P, N], BF16, name="v_g1", offset=4 * chunks[2][0], align_bytes=64)
         for g in range(G):
             nc.vector.tensor_copy(v_g1[:, g * PASS : (g + 1) * PASS], v_raw[1][:].indirect(listed_range(g * PASS, PASS)))
 
@@ -185,7 +183,7 @@ def tile_attend_bias_kernel(tc, qT, k_words, k_scales, vT, vs, kb, offs, out):
         def turn_values(h, slot, sources):
             v_il = sb.tile([P, G, P, 4], BF16, name=f"v_il{h}", tag=slot, align_bytes=64)
             for g in range(G):
-                turned = bank(f"c{g}", f"v_turned{h}{g}")
+                turned = bank(f"a{g}", f"v_turned{h}{g}")
                 words = sources[g].bitcast(F32)
                 for u in range(2):
                     nc.tensor.transpose(turned[:, u, :], words[:, u : PASS // 2 : 2], ident[:])
@@ -212,8 +210,6 @@ def tile_attend_bias_kernel(tc, qT, k_words, k_scales, vT, vs, kb, offs, out):
                 ALU.mult,
             )
         v_il1 = turn_values(1, "v_il1", [v_g1[:, 0:PASS], v_g1[:, PASS:N]])
-        l_inv = sb.tile([P, 1], F32, name="l_inv")
-        nc.vector.reciprocal(l_inv[:], l_sum[:])
         for g in range(G):
             nc.vector.quantize_mx(
                 out=w_codes[:, g, :].bitcast(FP8X4), scales=w_sc[:, g, :], in_=w_il[:, g].rearrange("p q t -> p (q t)")
@@ -230,8 +226,11 @@ def tile_attend_bias_kernel(tc, qT, k_words, k_scales, vT, vs, kb, offs, out):
                 in_=v_il1[:, g].rearrange("p e t -> p (e t)"),
             )
 
+        l_inv = sb.tile([P, 1], F32, name="l_inv", tag="neg_m1", align_bytes=64)
+        nc.vector.reciprocal(l_inv[:], l_sum[:])
+
         for h in range(2):
-            y_ps = ps.tile([P, P], F32, tag=["e", "a0"][h], name=f"y_ps{h}")
+            y_ps = ps.tile([P, P], F32, tag=["e", "c1"][h], name=f"y_ps{h}")
             for g in range(G):
                 nc.tensor.matmul_mx(
                     out=y_ps[:],

@@ -37,13 +37,13 @@ def tile_attend_bias_kernel(tc, qT, k_words, k_scales, vT, vs, kb, offs, out):
         offsets = sb.tile([P, N // 16], U16, name="offsets")
         nc.sync.dma_start(offsets[:], offs)
 
-        ks_pool = sb.tile([P, T + 4], U8, name="ks_pool", align_bytes=64)
-        nc.sync.dma_start(ks_pool[96:P, 0:T].bitcast(I32), k_scales.bitcast(I32).rearrange("o r w -> r o w"))
+        ks_pool = sb.tile([P, T], U8, name="ks_pool", align_bytes=64)
+        nc.sync.dma_start(ks_pool[96:P, :].bitcast(I32), k_scales.bitcast(I32).rearrange("o r w -> r o w"))
         nc.vector.memset(ks_pool[0:96, :].bitcast(I32), 0)
         kb_pool = sb.tile([P, T], F32, name="kb_pool")
         nc.scalar.dma_start(kb_pool[LIVE:P, :], kb[0:1, :])
-        vs_pool = shared.tile([P, 8 + T], F32, name="vs_pool", offset=0, align_bytes=64)
-        nc.scalar.dma_start(vs_pool[LIVE:P, 8:], vs[0:1, :])
+        vs_pool = shared.tile([P, T], F32, name="vs_pool", offset=0, align_bytes=64)
+        nc.scalar.dma_start(vs_pool[LIVE:P, :], vs[0:1, :])
         v_raw = [sb.tile([P, T], F32, name=f"v_raw{h}", tag=f"v_raw{h}", align_bytes=64) for h in range(2)]
 
         q_raw = sb.tile([P, 2, 4, NQ], F32, name="q_raw", tag="q_raw", align_bytes=64)
@@ -51,19 +51,19 @@ def tile_attend_bias_kernel(tc, qT, k_words, k_scales, vT, vs, kb, offs, out):
         kw_pool = sb.tile([P, T], I32, name="kw_pool")
         nc.sync.dma_start(kw_pool[:], k_words[0].rearrange("p t b -> p (t b)").bitcast(I32))
 
-        nc.vector.memset(vs_pool[0:LIVE, 7:768], 0.0)
-        k_sc = sb.tile([P, 2 * N + 4], U8, name="k_sc", align_bytes=64)
+        nc.vector.memset(kb_pool[0:LIVE, :], 0.0)
+        k_sc = sb.tile([P, 2 * N], U8, name="k_sc", align_bytes=64)
         nc.vector.memset(k_sc[:].bitcast(I32), 0)
+        nc.vector.memset(vs_pool[0:LIVE, 0:768], 0.0)
+        nc.gpsimd.memset(vs_pool[0:LIVE, 764:], 0.0)
         ident = sb.tile([P, P], F32, name="ident")
         make_identity(nc, ident[:])
-        nc.gpsimd.memset(kb_pool[0:LIVE, :], 0.0)
-        nc.gpsimd.memset(vs_pool[0:LIVE, 768:], 0.0)
 
         q_bf = sb.tile([P, 2, NQ, 4], BF16, name="q_bf", align_bytes=64)
         nc.scalar.activation(q_bf[:], q_raw[:].rearrange("p o j w -> p o w j"), ACT.Copy)
 
         ks0 = sb.tile([P, N], U8, name="ks0", align_bytes=64)
-        nc.vector.tensor_copy(ks0[:], ks_pool[:, 0:T].indirect(offsets[:]))
+        nc.vector.tensor_copy(ks0[:], ks_pool[:].indirect(offsets[:]))
         for quad in range(4):
             nc.sync.dma_start(
                 k_sc[32 * quad : 32 * quad + 4, 0 : 2 * N].bitcast(I32), ks0[96 + 8 * quad : 104 + 8 * quad, :].bitcast(I32)
@@ -74,7 +74,7 @@ def tile_attend_bias_kernel(tc, qT, k_words, k_scales, vT, vs, kb, offs, out):
         nc.vector.tensor_copy(kb_g[:], kb_pool[:].indirect(offsets[:]))
         vs_col = [sb.tile([P, 4], F32, name=f"vs_col{g}") for g in range(G)]
         vs_g = sb.tile([P, N], F32, name="vs_g")
-        nc.vector.tensor_copy(vs_g[:], vs_pool[:, 8:].indirect(offsets[:]))
+        nc.vector.tensor_copy(vs_g[:], vs_pool[:].indirect(offsets[:]))
         for g in range(G):
             nc.sync.dma_start(vs_col[g][:], vs_g[LIVE:P, g * PASS : (g + 1) * PASS])
 

@@ -81,7 +81,7 @@ def tile_attend_bias_kernel(tc, qT, k_words, k_scales, vT, vs, kb, offs, out):
         def listed_range(start, count):
             return offsets[:, start // 16 : (start + count) // 16]
 
-        kb_col = [sb.tile([P, 4], F32, name=f"kb_col{g}", tag=f"kb_col{g}", align_bytes=64) for g in range(G)]
+        kb_col = [sb.tile([P, 4], F32, name=f"kb_col{g}") for g in range(G)]
         for g in range(G):
             turned = bank(f"a{g}", f"kb_turned{g}")
             for b in range(4):
@@ -116,10 +116,10 @@ def tile_attend_bias_kernel(tc, qT, k_words, k_scales, vT, vs, kb, offs, out):
             part_words(c - 1)
         part_words(len(chunks) - 1)
 
-        v_g0 = [shared.tile([P, PASS], BF16, name="v_g00", offset=4 * chunks[2][0], align_bytes=64)]
-        nc.vector.tensor_copy(v_g0[0][:], v_raw[0][:].indirect(listed_range(0, PASS)))
+        v_g0 = shared.tile([P, N], BF16, name="v_g0", offset=4 * chunks[1][0], align_bytes=64)
+        nc.vector.tensor_copy(v_g0[:], v_raw[0][:].indirect(offsets[:]))
         s_t = [sb.tile([P, 4, NQ], F32, name=f"s_t{g}", tag=f"s_t{g}", align_bytes=64) for g in range(G)]
-        unused = sb.tile([P, PASS], BF16, name="unused")
+        neg_s1 = sb.tile([P, PASS], F32, name="neg_s1")
         scores = []
         neg_m = [sb.tile([P, 1], F32, name=f"neg_m{c}", tag=f"neg_m{c}", align_bytes=64) for c in range(G)]
         raw_tag = ["b0", "c0", "b1", "d"]
@@ -149,15 +149,12 @@ def tile_attend_bias_kernel(tc, qT, k_words, k_scales, vT, vs, kb, offs, out):
                 nc.vector.tensor_reduce(neg_m[0][:], scores[0], mybir.AxisListType.X, ALU.max, negate=True)
             else:
                 nc.vector.tensor_scalar(
-                    unused[:], scores[1], -1.0, neg_m[0][:], ALU.mult, ALU.min, accum_out=neg_m[1][:]
+                    neg_s1[:], scores[1], -1.0, neg_m[0][:], ALU.mult, ALU.min, accum_out=neg_m[1][:]
                 )
-            if c == 0:
-                v_g0.append(sb.tile([P, PASS], BF16, name="v_g01", tag="kb_col1", align_bytes=64))
-                nc.vector.tensor_copy(v_g0[1][:], v_raw[0][:].indirect(listed_range(PASS, PASS)))
 
-        v_turned0 = bank("d", "v_turned0")
+        v_turned0 = bank("a1", "v_turned0")
         for g in range(G):
-            words = v_g0[g][:].bitcast(F32)
+            words = v_g0[:, g * PASS : (g + 1) * PASS].bitcast(F32)
             for u in range(2):
                 nc.tensor.transpose(v_turned0[:, 2 * g + u, :], words[:, u : PASS // 2 : 2], ident[:])
 
@@ -167,13 +164,14 @@ def tile_attend_bias_kernel(tc, qT, k_words, k_scales, vT, vs, kb, offs, out):
             for u in range(2):
                 nc.scalar.activation(
                     p_sb[:, g, 2 * u : 2 * u + 2, :].rearrange("q e p -> q p e"),
-                    scores[g].rearrange("q (p t) -> q p t", t=4)[:, :, 2 * u : 2 * u + 2],
+                    [scores[0], neg_s1[:]][g].rearrange("q (p t) -> q p t", t=4)[:, :, 2 * u : 2 * u + 2],
                     ACT.Exp,
                     bias=neg_m[-1][:],
+                    scale=[1.0, -1.0][g],
                     accum_out=l_part[:, 2 * g + u : 2 * g + u + 1],
                 )
 
-        v_g1 = shared.tile([P, N], BF16, name="v_g1", offset=4 * chunks[2][0], align_bytes=64)
+        v_g1 = sb.tile([P, N], BF16, name="v_g1", tag="neg_m0", align_bytes=64)
         for g in range(G):
             nc.vector.tensor_copy(v_g1[:, g * PASS : (g + 1) * PASS], v_raw[1][:].indirect(listed_range(g * PASS, PASS)))
 

@@ -75,9 +75,6 @@ def tile_attend_bias_kernel(tc, qT, k_words, k_scales, vT, vs, kb, offs, out):
         vs_col = [sb.tile([P, 4], F32, name=f"vs_col{g}") for g in range(G)]
         vs_g = sb.tile([P, N], F32, name="vs_g")
         nc.vector.tensor_copy(vs_g[:], vs_pool[:].indirect(offsets[:]))
-        for g in range(G):
-            nc.sync.dma_start(vs_col[g][:], vs_g[LIVE:P, g * PASS : (g + 1) * PASS])
-
         def listed_range(start, count):
             return offsets[:, start // 16 : (start + count) // 16]
 
@@ -88,6 +85,14 @@ def tile_attend_bias_kernel(tc, qT, k_words, k_scales, vT, vs, kb, offs, out):
                 c0 = g * PASS + b * P
                 nc.tensor.transpose(turned[:, b, :], kb_g[:, c0 : c0 + P], ident[:])
             nc.scalar.copy(kb_col[g][:], turned[:, :, LIVE])
+
+        vs_dealt = sb.tile([P, N], F32, name="vs_dealt")
+        nc.scalar.copy(
+            vs_dealt[:].rearrange("p (b m u i) -> p b m u i", m=8, u=2, i=2),
+            vs_g[:].rearrange("p (b u m i) -> p b m u i", u=2, m=8, i=2),
+        )
+        for g in range(G):
+            nc.sync.dma_start(vs_col[g][:], vs_dealt[LIVE:P, g * PASS : (g + 1) * PASS])
 
         chunks = [(c * 256, 256) for c in range(4)]
 
@@ -117,7 +122,7 @@ def tile_attend_bias_kernel(tc, qT, k_words, k_scales, vT, vs, kb, offs, out):
         part_words(len(chunks) - 1)
 
         v_g0 = shared.tile([P, N], BF16, name="v_g0", offset=4 * chunks[1][0], align_bytes=64)
-        nc.vector.tensor_copy(v_g0[:], v_raw[0][:].indirect(offsets[:]))
+        nc.vector.tensor_copy(v_g0[:].rearrange("p (u b x) -> p b u x", u=2, x=16), v_raw[0][:].indirect(offsets[:]))
         s_t = [sb.tile([P, 4, NQ], F32, name=f"s_t{g}", tag=f"s_t{g}", align_bytes=64) for g in range(G)]
         neg_s1 = sb.tile([P, PASS], F32, name="neg_s1")
         scores = []
@@ -154,17 +159,17 @@ def tile_attend_bias_kernel(tc, qT, k_words, k_scales, vT, vs, kb, offs, out):
 
         v_turned0 = bank("a1", "v_turned0")
         for g in range(G):
-            words = v_g0[:, g * PASS : (g + 1) * PASS].bitcast(F32)
             for u in range(2):
-                nc.tensor.transpose(v_turned0[:, 2 * g + u, :], words[:, u : PASS // 2 : 2], ident[:])
+                words = v_g0[:, u * PASS + g * 256 : u * PASS + (g + 1) * 256].bitcast(F32)
+                nc.tensor.transpose(v_turned0[:, 2 * g + u, :], words, ident[:])
 
         p_sb = sb.tile([P, G, 4, P], F32, name="p_sb")
         l_part = sb.tile([P, 2 * G], F32, name="l_part")
         for g in range(G):
             for u in range(2):
                 nc.scalar.activation(
-                    p_sb[:, g, 2 * u : 2 * u + 2, :].rearrange("q e p -> q p e"),
-                    [scores[0], neg_s1[:]][g].rearrange("q (p t) -> q p t", t=4)[:, :, 2 * u : 2 * u + 2],
+                    p_sb[:, g, 2 * u : 2 * u + 2, :].rearrange("q i (b m) -> q b m i", m=8),
+                    [scores[0], neg_s1[:]][g].rearrange("q (b u m i) -> q u b m i", u=2, m=8, i=2)[:, u],
                     ACT.Exp,
                     bias=neg_m[-1][:],
                     scale=[1.0, -1.0][g],
@@ -173,7 +178,10 @@ def tile_attend_bias_kernel(tc, qT, k_words, k_scales, vT, vs, kb, offs, out):
 
         v_g1 = sb.tile([P, N], BF16, name="v_g1", tag="neg_m0", align_bytes=64)
         for g in range(G):
-            nc.vector.tensor_copy(v_g1[:, g * PASS : (g + 1) * PASS], v_raw[1][:].indirect(listed_range(g * PASS, PASS)))
+            nc.vector.tensor_copy(
+                v_g1[:, g * PASS : (g + 1) * PASS].rearrange("p (u b x) -> p b u x", u=2, x=16),
+                v_raw[1][:].indirect(listed_range(g * PASS, PASS)),
+            )
 
         v_codes = sb.tile([P, 2, G, P], U32, name="v_codes", align_bytes=64)
         v_sc = sb.tile([P, 2, G, P], U8, name="v_sc", tag="v_raw1", align_bytes=64)
@@ -184,7 +192,7 @@ def tile_attend_bias_kernel(tc, qT, k_words, k_scales, vT, vs, kb, offs, out):
                 turned = bank(f"a{g}", f"v_turned{h}{g}")
                 words = sources[g].bitcast(F32)
                 for u in range(2):
-                    nc.tensor.transpose(turned[:, u, :], words[:, u : PASS // 2 : 2], ident[:])
+                    nc.tensor.transpose(turned[:, u, :], words[:, u * P : (u + 1) * P], ident[:])
                 nc.scalar.copy(v_il[:, g].bitcast(F32), turned[:, 0:2, :].rearrange("p u e -> p e u"))
             return v_il
 

@@ -18,6 +18,7 @@ P = 128
 N, T, D, DV, NQ = 1024, 2048, 1024, 256, 128
 PASS = 512
 G = N // PASS
+CHUNK = 256
 LIVE = P - 1
 
 FLOPS = 2 * NQ * N * (D + DV)
@@ -37,6 +38,9 @@ def tile_attend_bias_kernel(tc, qT, k_words, k_scales, vT, vs, kb, offs, out):
         offsets = sb.tile([P, N // 16], U16, name="offsets")
         nc.sync.dma_start(offsets[:], offs)
 
+        def gather(dst, window, start, count):
+            nc.vector.tensor_copy(dst, window.indirect(offsets[:, start // 16 : (start + count) // 16]))
+
         ks_pool = sb.tile([P, T], U8, name="ks_pool", align_bytes=64)
         nc.sync.dma_start(ks_pool[96:P, :].bitcast(I32), k_scales.bitcast(I32).rearrange("o r w -> r o w"))
         nc.vector.memset(ks_pool[0:96, :].bitcast(I32), 0)
@@ -54,29 +58,26 @@ def tile_attend_bias_kernel(tc, qT, k_words, k_scales, vT, vs, kb, offs, out):
         nc.vector.memset(kb_pool[0:LIVE, :], 0.0)
         k_sc = sb.tile([P, 2 * N], U8, name="k_sc", align_bytes=64)
         nc.vector.memset(k_sc[:].bitcast(I32), 0)
-        nc.vector.memset(vs_pool[0:LIVE, 0:768], 0.0)
-        nc.gpsimd.memset(vs_pool[0:LIVE, 764:], 0.0)
+        nc.vector.memset(vs_pool[0:LIVE, 0:256], 0.0)
+        nc.gpsimd.memset(vs_pool[0:LIVE, 252:], 0.0)
         ident = sb.tile([P, P], F32, name="ident")
         make_identity(nc, ident[:])
 
         q_bf = sb.tile([P, 2, NQ, 4], BF16, name="q_bf", align_bytes=64)
         nc.scalar.activation(q_bf[:], q_raw[:].rearrange("p o j w -> p o w j"), ACT.Copy)
 
-        ks0 = sb.tile([P, N], U8, name="ks0", align_bytes=64)
-        nc.vector.tensor_copy(ks0[:], ks_pool[:].indirect(offsets[:]))
+        ks_g = sb.tile([P, N], U8, name="ks_g", align_bytes=64)
+        gather(ks_g[:], ks_pool[:], 0, N)
         for quad in range(4):
             nc.sync.dma_start(
-                k_sc[32 * quad : 32 * quad + 4, 0 : 2 * N].bitcast(I32), ks0[96 + 8 * quad : 104 + 8 * quad, :].bitcast(I32)
+                k_sc[32 * quad : 32 * quad + 4, :].bitcast(I32), ks_g[96 + 8 * quad : 104 + 8 * quad, :].bitcast(I32)
             )
         for h in range(2):
             nc.sync.dma_start(v_raw[h][:], vT[h * P : (h + 1) * P, :])
         kb_g = sb.tile([P, N], F32, name="kb_g")
-        nc.vector.tensor_copy(kb_g[:], kb_pool[:].indirect(offsets[:]))
-        vs_col = [sb.tile([P, 4], F32, name=f"vs_col{g}") for g in range(G)]
+        gather(kb_g[:], kb_pool[:], 0, N)
         vs_g = sb.tile([P, N], F32, name="vs_g")
-        nc.vector.tensor_copy(vs_g[:], vs_pool[:].indirect(offsets[:]))
-        def listed_range(start, count):
-            return offsets[:, start // 16 : (start + count) // 16]
+        gather(vs_g[:], vs_pool[:], 0, N)
 
         kb_col = [sb.tile([P, 4], F32, name=f"kb_col{g}") for g in range(G)]
         for g in range(G):
@@ -91,18 +92,18 @@ def tile_attend_bias_kernel(tc, qT, k_words, k_scales, vT, vs, kb, offs, out):
             vs_dealt[:].rearrange("p (b m u i) -> p b m u i", m=8, u=2, i=2),
             vs_g[:].rearrange("p (b u m i) -> p b m u i", u=2, m=8, i=2),
         )
+        vs_col = [sb.tile([P, 4], F32, name=f"vs_col{g}") for g in range(G)]
         for g in range(G):
             nc.sync.dma_start(vs_col[g][:], vs_dealt[LIVE:P, g * PASS : (g + 1) * PASS])
 
-        chunks = [(c * 256, 256) for c in range(4)]
-
+        chunks = N // CHUNK
         kw_g = [
-            shared.tile([P, n], I32, name=f"kw_g{c}", offset=4 * s0, align_bytes=64)[:] for c, (s0, n) in enumerate(chunks)
+            shared.tile([P, CHUNK], I32, name=f"kw_g{c}", offset=4 * CHUNK * c, align_bytes=64)[:] for c in range(chunks)
         ]
-        k_codes = [sb.tile([P, 2, 2 * n], U8, name=f"k_codes{c}", align_bytes=64) for c, (s0, n) in enumerate(chunks)]
+        k_codes = [sb.tile([P, 2, 2 * CHUNK], U8, name=f"k_codes{c}", align_bytes=64) for c in range(chunks)]
 
         def gather_words(c):
-            nc.vector.tensor_copy(kw_g[c].bitcast(U32), kw_pool[:].bitcast(U32).indirect(listed_range(*chunks[c])))
+            gather(kw_g[c].bitcast(U32), kw_pool[:].bitcast(U32), c * CHUNK, CHUNK)
 
         def part_words(c):
             nc.vector.tensor_copy(
@@ -111,27 +112,38 @@ def tile_attend_bias_kernel(tc, qT, k_words, k_scales, vT, vs, kb, offs, out):
 
         q_codes = sb.tile([P, 2 * NQ], U32, name="q_codes", align_bytes=64)
         q_sc = sb.tile([P, 2 * NQ], U8, name="q_sc", align_bytes=64)
-
         nc.vector.quantize_mx(
             out=q_codes[:].bitcast(FP8X4), scales=q_sc[:], in_=q_bf[:].rearrange("p o w j -> p (o w j)")
         )
         gather_words(0)
-        for c in range(1, len(chunks)):
+        for c in range(1, chunks):
             gather_words(c)
             part_words(c - 1)
-        part_words(len(chunks) - 1)
+        part_words(chunks - 1)
 
-        v_g0 = shared.tile([P, N], BF16, name="v_g0", offset=4 * chunks[1][0], align_bytes=64)
-        nc.vector.tensor_copy(v_g0[:].rearrange("p (u b x) -> p b u x", u=2, x=16), v_raw[0][:].indirect(offsets[:]))
-        s_t = [sb.tile([P, 4, NQ], F32, name=f"s_t{g}", tag=f"s_t{g}", align_bytes=64) for g in range(G)]
-        neg_s1 = sb.tile([P, PASS], F32, name="neg_s1")
-        scores = []
-        neg_m = [sb.tile([P, 1], F32, name=f"neg_m{c}", tag=f"neg_m{c}", align_bytes=64) for c in range(G)]
-        raw_tag = ["b0", "c0", "b1", "d"]
-        for c, (start, count) in enumerate(chunks):
-            raw = bank(raw_tag[c], f"raw{c}")
-            for b in range(count // P):
-                c0 = start + b * P
+        def dealt(tile):
+            return tile.rearrange("p (u b x) -> p b u x", u=2, x=16)
+
+        v_g0 = shared.tile([P, N], BF16, name="v_g0", offset=4 * CHUNK, align_bytes=64)
+        gather(dealt(v_g0[:]), v_raw[0][:], 0, N)
+
+        warm = ps.tile([P, P], F32, tag="e", name="warm")
+        for k in range(5):
+            nc.tensor.matmul_mx(
+                out=warm[:],
+                lhsT=q_codes[:, 0:NQ].bitcast(FP8X4),
+                lhsT_scale=q_sc[:, 0:NQ],
+                rhs=q_codes[:, NQ : 2 * NQ].bitcast(FP8X4),
+                rhs_scale=q_sc[:, NQ : 2 * NQ],
+                start=True,
+                stop=True,
+            )
+
+        s_t = [sb.tile([P, 4, NQ], F32, name=f"s_t{g}", align_bytes=64) for g in range(G)]
+        for c in range(chunks):
+            raw = bank(["b0", "c0", "b1", "d"][c], f"raw{c}")
+            for b in range(CHUNK // P):
+                c0 = c * CHUNK + b * P
                 for o in range(2):
                     nc.tensor.matmul_mx(
                         out=raw[:, b, :],
@@ -142,20 +154,20 @@ def tile_attend_bias_kernel(tc, qT, k_words, k_scales, vT, vs, kb, offs, out):
                         start=(o == 0),
                         stop=(o == 1),
                     )
-            for b in range(count // P):
-                blk = start // P + b
-                nc.scalar.activation(s_t[blk // 4][:, blk % 4, :], raw[:, b, :], ACT.Identity, bias=kb_col[blk // 4][:, blk % 4 : blk % 4 + 1])
-        for c in range(G):
-            turned = bank(f"a{c}", f"scores{c}")
+            for b in range(CHUNK // P):
+                g, blk = divmod(c * CHUNK // P + b, 4)
+                nc.scalar.activation(s_t[g][:, blk, :], raw[:, b, :], ACT.Identity, bias=kb_col[g][:, blk : blk + 1])
+
+        neg_m = [sb.tile([P, 1], F32, name=f"neg_m{g}", tag=f"neg_m{g}", align_bytes=64) for g in range(G)]
+        neg_s1 = sb.tile([P, PASS], F32, name="neg_s1")
+        scores = []
+        for g in range(G):
+            turned = bank(f"a{g}", f"scores{g}")
             for b in range(4):
-                nc.tensor.transpose(turned[:, b, :], s_t[c][:, b, :], ident[:])
+                nc.tensor.transpose(turned[:, b, :], s_t[g][:, b, :], ident[:])
             scores.append(turned[:].rearrange("q b c -> q (b c)"))
-            if c == 0:
-                nc.vector.tensor_reduce(neg_m[0][:], scores[0], mybir.AxisListType.X, ALU.max, negate=True)
-            else:
-                nc.vector.tensor_scalar(
-                    neg_s1[:], scores[1], -1.0, neg_m[0][:], ALU.mult, ALU.min, accum_out=neg_m[1][:]
-                )
+        nc.vector.tensor_reduce(neg_m[0][:], scores[0], mybir.AxisListType.X, ALU.max, negate=True)
+        nc.vector.tensor_scalar(neg_s1[:], scores[1], -1.0, neg_m[0][:], ALU.mult, ALU.min, accum_out=neg_m[1][:])
 
         v_turned0 = bank("a1", "v_turned0")
         for g in range(G):
@@ -171,33 +183,19 @@ def tile_attend_bias_kernel(tc, qT, k_words, k_scales, vT, vs, kb, offs, out):
                     p_sb[:, g, 2 * u : 2 * u + 2, :].rearrange("q i (b m) -> q b m i", m=8),
                     [scores[0], neg_s1[:]][g].rearrange("q (b u m i) -> q u b m i", u=2, m=8, i=2)[:, u],
                     ACT.Exp,
-                    bias=neg_m[-1][:],
+                    bias=neg_m[1][:],
                     scale=[1.0, -1.0][g],
                     accum_out=l_part[:, 2 * g + u : 2 * g + u + 1],
                 )
 
         v_g1 = sb.tile([P, N], BF16, name="v_g1", tag="neg_m0", align_bytes=64)
         for g in range(G):
-            nc.vector.tensor_copy(
-                v_g1[:, g * PASS : (g + 1) * PASS].rearrange("p (u b x) -> p b u x", u=2, x=16),
-                v_raw[1][:].indirect(listed_range(g * PASS, PASS)),
-            )
+            gather(dealt(v_g1[:, g * PASS : (g + 1) * PASS]), v_raw[1][:], g * PASS, PASS)
 
         v_codes = sb.tile([P, 2, G, P], U32, name="v_codes", align_bytes=64)
         v_sc = sb.tile([P, 2, G, P], U8, name="v_sc", tag="v_raw1", align_bytes=64)
-
-        def turn_values(h, slot, sources):
-            v_il = sb.tile([P, G, P, 4], BF16, name=f"v_il{h}", tag=slot, align_bytes=64)
-            for g in range(G):
-                turned = bank(f"a{g}", f"v_turned{h}{g}")
-                words = sources[g].bitcast(F32)
-                for u in range(2):
-                    nc.tensor.transpose(turned[:, u, :], words[:, u * P : (u + 1) * P], ident[:])
-                nc.scalar.copy(v_il[:, g].bitcast(F32), turned[:, 0:2, :].rearrange("p u e -> p e u"))
-            return v_il
-
-        v_il0 = sb.tile([P, G, P, 4], BF16, name="v_il0", tag="neg_m1", align_bytes=64)
-        nc.scalar.copy(v_il0[:].bitcast(F32), v_turned0[:].rearrange("p (g u) e -> p g e u", u=2))
+        v_il = [sb.tile([P, G, P, 4], BF16, name=f"v_il{h}", tag=["neg_m1", "v_il1"][h], align_bytes=64) for h in range(2)]
+        nc.scalar.copy(v_il[0][:].bitcast(F32), v_turned0[:].rearrange("p (g u) e -> p g e u", u=2))
 
         l_sum = sb.tile([P, 1], F32, name="l_sum")
         nc.scalar.activation(l_part[:], l_part[:], ACT.Identity, accum_out=l_sum[:])
@@ -215,28 +213,28 @@ def tile_attend_bias_kernel(tc, qT, k_words, k_scales, vT, vs, kb, offs, out):
                 vs_col[g][:].unsqueeze(1).to_broadcast([P, NQ, 4]),
                 ALU.mult,
             )
-        v_il1 = turn_values(1, "v_il1", [v_g1[:, 0:PASS], v_g1[:, PASS:N]])
+        v_turned1 = bank("a0", "v_turned1")
         for g in range(G):
+            words = v_g1[:, g * PASS : (g + 1) * PASS].bitcast(F32)
+            for u in range(2):
+                nc.tensor.transpose(v_turned1[:, 2 * g + u, :], words[:, u * P : (u + 1) * P], ident[:])
+        nc.scalar.copy(v_il[1][:].bitcast(F32), v_turned1[:].rearrange("p (g u) e -> p g e u", u=2))
+
+        def quantise(codes, scales, values):
             nc.vector.quantize_mx(
-                out=w_codes[:, g, :].bitcast(FP8X4), scales=w_sc[:, g, :], in_=w_il[:, g].rearrange("p q t -> p (q t)")
-            )
-        nc.vector.quantize_mx(
-            out=v_codes[:, 0].rearrange("p g e -> p (g e)").bitcast(FP8X4),
-            scales=v_sc[:, 0].rearrange("p g e -> p (g e)"),
-            in_=v_il0[:].rearrange("p g e t -> p (g e t)"),
-        )
-        for g in range(G):
-            nc.vector.quantize_mx(
-                out=v_codes[:, 1, g].bitcast(FP8X4),
-                scales=v_sc[:, 1, g],
-                in_=v_il1[:, g].rearrange("p e t -> p (e t)"),
+                out=codes.rearrange("p g c -> p (g c)").bitcast(FP8X4),
+                scales=scales.rearrange("p g c -> p (g c)"),
+                in_=values.rearrange("p g c t -> p (g c t)"),
             )
 
-        l_inv = sb.tile([P, 1], F32, name="l_inv", tag="neg_m1", align_bytes=64)
+        quantise(v_codes[:, 0], v_sc[:, 0], v_il[0][:])
+        quantise(w_codes[:], w_sc[:], w_il[:])
+        quantise(v_codes[:, 1], v_sc[:, 1], v_il[1][:])
+        l_inv = sb.tile([P, 1], F32, name="l_inv")
         nc.vector.reciprocal(l_inv[:], l_sum[:])
 
         for h in range(2):
-            y_ps = ps.tile([P, P], F32, tag=["e", "c1"][h], name=f"y_ps{h}")
+            y_ps = ps.tile([P, P], F32, tag=["e", "c0"][h], name=f"y_ps{h}")
             for g in range(G):
                 nc.tensor.matmul_mx(
                     out=y_ps[:],

@@ -30,6 +30,7 @@ def tile_attend_bias_kernel(tc, qT, k_words, k_scales, vT, vs, kb, offs, out):
     with ExitStack() as ctx:
         sb = ctx.enter_context(tc.tile_pool(name="sb", bufs=1))
         shared = ctx.enter_context(tc.tile_pool(name="shared", bufs=1))
+        late = ctx.enter_context(tc.tile_pool(name="late", bufs=1))
         ps = ctx.enter_context(tc.psum_pool(name="ps", bufs=1))
 
         def bank(tag, name):
@@ -47,7 +48,7 @@ def tile_attend_bias_kernel(tc, qT, k_words, k_scales, vT, vs, kb, offs, out):
         kb_pool = sb.tile([P, T], F32, name="kb_pool")
         nc.scalar.dma_start(kb_pool[LIVE:P, :], kb[0:1, :])
         vs_pool = shared.tile([P, T], F32, name="vs_pool", offset=0, align_bytes=64)
-        nc.scalar.dma_start(vs_pool[LIVE:P, :], vs[0:1, :])
+        nc.sync.dma_start(vs_pool[LIVE:P, :], vs[0:1, :])
         v_raw = [sb.tile([P, T], F32, name=f"v_raw{h}", tag=f"v_raw{h}", align_bytes=64) for h in range(2)]
 
         q_raw = sb.tile([P, 2, 4, NQ], F32, name="q_raw", tag="q_raw", align_bytes=64)
@@ -58,8 +59,8 @@ def tile_attend_bias_kernel(tc, qT, k_words, k_scales, vT, vs, kb, offs, out):
         nc.vector.memset(kb_pool[0:LIVE, :], 0.0)
         k_sc = sb.tile([P, 2 * N], U8, name="k_sc", align_bytes=64)
         nc.vector.memset(k_sc[:].bitcast(I32), 0)
-        nc.vector.memset(vs_pool[0:LIVE, 0:256], 0.0)
-        nc.gpsimd.memset(vs_pool[0:LIVE, 252:], 0.0)
+        nc.vector.memset(vs_pool[0:LIVE, 0:512], 0.0)
+        nc.gpsimd.memset(vs_pool[0:LIVE, 508:], 0.0)
         ident = sb.tile([P, P], F32, name="ident")
         make_identity(nc, ident[:])
 
@@ -140,10 +141,11 @@ def tile_attend_bias_kernel(tc, qT, k_words, k_scales, vT, vs, kb, offs, out):
             )
 
         s_t = [sb.tile([P, 4, NQ], F32, name=f"s_t{g}", align_bytes=64) for g in range(G)]
-        for c in range(chunks):
-            raw = bank(["b0", "c0", "b1", "d"][c], f"raw{c}")
-            for b in range(CHUNK // P):
-                c0 = c * CHUNK + b * P
+        for tag, blocks in [("b0", (0, 1)), ("c0", (2, 3)), ("b1", (4, 5)), ("d0", (6,)), ("d1", (7,))]:
+            raw = bank(tag, f"raw_{tag}")
+            for blk in blocks:
+                c, b = divmod(blk, CHUNK // P)
+                c0 = blk * P
                 for o in range(2):
                     nc.tensor.matmul_mx(
                         out=raw[:, b, :],
@@ -154,11 +156,12 @@ def tile_attend_bias_kernel(tc, qT, k_words, k_scales, vT, vs, kb, offs, out):
                         start=(o == 0),
                         stop=(o == 1),
                     )
-            for b in range(CHUNK // P):
-                g, blk = divmod(c * CHUNK // P + b, 4)
-                nc.scalar.activation(s_t[g][:, blk, :], raw[:, b, :], ACT.Identity, bias=kb_col[g][:, blk : blk + 1])
+            for blk in blocks:
+                g, j = divmod(blk, 4)
+                nc.scalar.activation(s_t[g][:, j, :], raw[:, blk % 2, :], ACT.Identity, bias=kb_col[g][:, j : j + 1])
 
-        neg_m = [sb.tile([P, 1], F32, name=f"neg_m{g}", tag=f"neg_m{g}", align_bytes=64) for g in range(G)]
+        neg_m0_slot = late.tile([P, N // 2 + 32], F32, name="neg_m0_slot", offset=0, align_bytes=64)
+        neg_m = [neg_m0_slot[:, 0:1], sb.tile([P, 1], F32, name="neg_m1", tag="neg_m1", align_bytes=64)[:]]
         neg_s1 = sb.tile([P, PASS], F32, name="neg_s1")
         scores = []
         for g in range(G):
@@ -166,14 +169,33 @@ def tile_attend_bias_kernel(tc, qT, k_words, k_scales, vT, vs, kb, offs, out):
             for b in range(4):
                 nc.tensor.transpose(turned[:, b, :], s_t[g][:, b, :], ident[:])
             scores.append(turned[:].rearrange("q b c -> q (b c)"))
-        nc.vector.tensor_reduce(neg_m[0][:], scores[0], mybir.AxisListType.X, ALU.max, negate=True)
-        nc.vector.tensor_scalar(neg_s1[:], scores[1], -1.0, neg_m[0][:], ALU.mult, ALU.min, accum_out=neg_m[1][:])
+        nc.vector.tensor_reduce(neg_m[0], scores[0], mybir.AxisListType.X, ALU.max, negate=True)
+        nc.vector.tensor_scalar(neg_s1[:], scores[1], -1.0, neg_m[0], ALU.mult, ALU.min, accum_out=neg_m[1])
 
-        v_turned0 = bank("a1", "v_turned0")
-        for g in range(G):
+        v_il = [
+            [sb.tile([P, P, 4], BF16, name=f"v_il{h}{g}", tag=f"v_il{h}{g}", align_bytes=64) for g in range(G)]
+            for h in range(2)
+        ]
+        v_il[0][1] = sb.tile([P, P, 4], BF16, name="v_il01_late", tag="neg_m1", align_bytes=64)
+
+        def turn_values(words, tag, name):
+            turned = bank(tag, name)
             for u in range(2):
-                words = v_g0[:, u * PASS + g * 256 : u * PASS + (g + 1) * 256].bitcast(F32)
-                nc.tensor.transpose(v_turned0[:, 2 * g + u, :], words, ident[:])
+                nc.tensor.transpose(turned[:, u, :], words[u], ident[:])
+            return turned
+
+        def copy_values(dst, turned):
+            nc.scalar.copy(dst[:].bitcast(F32), turned[:, 0:2, :].rearrange("p u e -> p e u"))
+
+        v_turned0 = [
+            turn_values(
+                [v_g0[:, u * PASS + g * 256 : u * PASS + (g + 1) * 256].bitcast(F32) for u in range(2)],
+                f"d{g}",
+                f"v_turned0{g}",
+            )
+            for g in range(G)
+        ]
+        copy_values(v_il[0][0], v_turned0[0])
 
         p_sb = sb.tile([P, G, 4, P], F32, name="p_sb")
         l_part = sb.tile([P, 2 * G], F32, name="l_part")
@@ -183,28 +205,30 @@ def tile_attend_bias_kernel(tc, qT, k_words, k_scales, vT, vs, kb, offs, out):
                     p_sb[:, g, 2 * u : 2 * u + 2, :].rearrange("q i (b m) -> q b m i", m=8),
                     [scores[0], neg_s1[:]][g].rearrange("q (b u m i) -> q u b m i", u=2, m=8, i=2)[:, u],
                     ACT.Exp,
-                    bias=neg_m[1][:],
+                    bias=neg_m[1],
                     scale=[1.0, -1.0][g],
                     accum_out=l_part[:, 2 * g + u : 2 * g + u + 1],
                 )
 
-        v_g1 = sb.tile([P, N], BF16, name="v_g1", tag="neg_m0", align_bytes=64)
+        v_g1 = late.tile([P, N], BF16, name="v_g1", offset=0, align_bytes=64)
         for g in range(G):
             gather(dealt(v_g1[:, g * PASS : (g + 1) * PASS]), v_raw[1][:], g * PASS, PASS)
 
         v_codes = sb.tile([P, 2, G, P], U32, name="v_codes", align_bytes=64)
-        v_sc = sb.tile([P, 2, G, P], U8, name="v_sc", tag="v_raw1", align_bytes=64)
-        v_il = [sb.tile([P, G, P, 4], BF16, name=f"v_il{h}", tag=["neg_m1", "v_il1"][h], align_bytes=64) for h in range(2)]
-        nc.scalar.copy(v_il[0][:].bitcast(F32), v_turned0[:].rearrange("p (g u) e -> p g e u", u=2))
-
-        l_sum = sb.tile([P, 1], F32, name="l_sum")
-        nc.scalar.activation(l_part[:], l_part[:], ACT.Identity, accum_out=l_sum[:])
-
+        v_sc = [[sb.tile([P, P], U8, name=f"v_sc{h}{g}", align_bytes=64) for g in range(G)] for h in range(2)]
+        v_sc[0][0] = late.tile([P, P], U8, name="v_sc00_late", offset=2 * N, align_bytes=64)
         w_il = sb.tile([P, G, NQ, 4], BF16, name="w_il", align_bytes=64)
         w_codes = sb.tile([P, G, NQ], U32, name="w_codes", align_bytes=64)
         w_sc = sb.tile([P, G, NQ], U8, name="w_sc", align_bytes=64)
-        for g in range(G):
-            turned = bank(f"b{g}", f"p_turned{g}")
+
+        def quantise(codes, scales, values):
+            nc.vector.quantize_mx(out=codes.bitcast(FP8X4), scales=scales, in_=values.rearrange("p c t -> p (c t)"))
+
+        def quantise_values(h, g):
+            quantise(v_codes[:, h, g], v_sc[h][g][:], v_il[h][g][:])
+
+        def weigh(g):
+            turned = bank(["b0", "c0"][g], f"p_turned{g}")
             for t in range(4):
                 nc.tensor.transpose(turned[:, t, :], p_sb[:, g, t, :], ident[:])
             nc.vector.tensor_tensor(
@@ -213,38 +237,41 @@ def tile_attend_bias_kernel(tc, qT, k_words, k_scales, vT, vs, kb, offs, out):
                 vs_col[g][:].unsqueeze(1).to_broadcast([P, NQ, 4]),
                 ALU.mult,
             )
-        v_turned1 = bank("a0", "v_turned1")
-        for g in range(G):
+
+        def second_half(g):
             words = v_g1[:, g * PASS : (g + 1) * PASS].bitcast(F32)
-            for u in range(2):
-                nc.tensor.transpose(v_turned1[:, 2 * g + u, :], words[:, u * P : (u + 1) * P], ident[:])
-        nc.scalar.copy(v_il[1][:].bitcast(F32), v_turned1[:].rearrange("p (g u) e -> p g e u", u=2))
+            turned = turn_values([words[:, u * P : (u + 1) * P] for u in range(2)], ["a0", "d1"][g], f"v_turned1{g}")
+            copy_values(v_il[1][g], turned)
 
-        def quantise(codes, scales, values):
-            nc.vector.quantize_mx(
-                out=codes.rearrange("p g c -> p (g c)").bitcast(FP8X4),
-                scales=scales.rearrange("p g c -> p (g c)"),
-                in_=values.rearrange("p g c t -> p (g c t)"),
-            )
-
-        quantise(v_codes[:, 0], v_sc[:, 0], v_il[0][:])
-        quantise(w_codes[:], w_sc[:], w_il[:])
-        quantise(v_codes[:, 1], v_sc[:, 1], v_il[1][:])
+        quantise_values(0, 0)
+        copy_values(v_il[0][1], v_turned0[1])
+        weigh(0)
+        second_half(0)
+        quantise_values(0, 1)
+        weigh(1)
+        l_sum = sb.tile([P, 1], F32, name="l_sum")
+        nc.scalar.activation(l_part[:], l_part[:], ACT.Identity, accum_out=l_sum[:])
+        second_half(1)
+        for g in range(G):
+            quantise(w_codes[:, g], w_sc[:, g], w_il[:, g])
+            quantise_values(1, g)
         l_inv = sb.tile([P, 1], F32, name="l_inv")
         nc.vector.reciprocal(l_inv[:], l_sum[:])
 
-        for h in range(2):
-            y_ps = ps.tile([P, P], F32, tag=["e", "c0"][h], name=f"y_ps{h}")
-            for g in range(G):
+        y_ps = [ps.tile([P, P], F32, tag=["e", "a1"][h], name=f"y_ps{h}") for h in range(2)]
+        for g in range(G):
+            for h in range(2):
                 nc.tensor.matmul_mx(
-                    out=y_ps[:],
+                    out=y_ps[h][:],
                     lhsT=w_codes[:, g, :].bitcast(FP8X4),
                     lhsT_scale=w_sc[:, g, :],
                     rhs=v_codes[:, h, g, :].bitcast(FP8X4),
-                    rhs_scale=v_sc[:, h, g, :],
+                    rhs_scale=v_sc[h][g][:],
                     start=(g == 0),
                     stop=(g == G - 1),
                 )
-            y_sb = sb.tile([P, P], F32, name=f"y_sb{h}")
-            nc.scalar.activation(y_sb[:], y_ps[:], ACT.Copy, scale=l_inv[:])
-            nc.sync.dma_start(out[0][:, h * P : (h + 1) * P], y_sb[:])
+        y_sb = [sb.tile([P, P], F32, name=f"y_sb{h}") for h in range(2)]
+        nc.scalar.activation(y_sb[0][:], y_ps[0][:], ACT.Copy, scale=l_inv[:])
+        nc.vector.tensor_scalar(y_sb[1][:], y_ps[1][:], l_inv[:], None, ALU.mult)
+        for h in range(2):
+            nc.sync.dma_start(out[0][:, h * P : (h + 1) * P], y_sb[h][:])

@@ -48,8 +48,11 @@ def tile_attend_bias_kernel(tc, qT, k_words, k_scales, vT, vs, kb, offs, out):
         kb_pool = sb.tile([P, T], F32, name="kb_pool")
         nc.scalar.dma_start(kb_pool[LIVE:P, :], kb[0:1, :])
         vs_pool = shared.tile([P, T], F32, name="vs_pool", offset=0, align_bytes=64)
-        nc.sync.dma_start(vs_pool[LIVE:P, :], vs[0:1, :])
-        v_raw = [sb.tile([P, T], F32, name=f"v_raw{h}", tag=f"v_raw{h}", align_bytes=64) for h in range(2)]
+        nc.scalar.dma_start(vs_pool[LIVE:P, :], vs[0:1, :])
+        v_raw = [
+            late.tile([P, T], F32, name="v_raw0", offset=0, align_bytes=64),
+            sb.tile([P, T], F32, name="v_raw1", align_bytes=64),
+        ]
 
         q_raw = sb.tile([P, 2, 4, NQ], F32, name="q_raw", tag="q_raw", align_bytes=64)
         nc.sync.dma_start(q_raw[:], qT[0].rearrange("(o p j) w -> p o j w", o=2, j=4))
@@ -111,7 +114,7 @@ def tile_attend_bias_kernel(tc, qT, k_words, k_scales, vT, vs, kb, offs, out):
                 k_codes[c][:].bitcast(U16), kw_g[c].bitcast(U16).rearrange("p (n o) -> p o n", o=2)
             )
 
-        q_codes = sb.tile([P, 2 * NQ], U32, name="q_codes", align_bytes=64)
+        q_codes = shared.tile([P, 2 * NQ], U32, name="q_codes", offset=4 * N, align_bytes=64)
         q_sc = sb.tile([P, 2 * NQ], U8, name="q_sc", align_bytes=64)
         nc.vector.quantize_mx(
             out=q_codes[:].bitcast(FP8X4), scales=q_sc[:], in_=q_bf[:].rearrange("p o w j -> p (o w j)")

@@ -49,10 +49,7 @@ def tile_attend_bias_kernel(tc, qT, k_words, k_scales, vT, vs, kb, offs, out):
         nc.scalar.dma_start(kb_pool[LIVE:P, :], kb[0:1, :])
         vs_pool = shared.tile([P, T], F32, name="vs_pool", offset=0, align_bytes=64)
         nc.scalar.dma_start(vs_pool[LIVE:P, :], vs[0:1, :])
-        v_raw = [
-            late.tile([P, T], F32, name="v_raw0", offset=0, align_bytes=64),
-            sb.tile([P, T], F32, name="v_raw1", align_bytes=64),
-        ]
+        v_raw = [sb.tile([P, T], F32, name=f"v_raw{h}", tag=f"v_raw{h}", align_bytes=64) for h in range(2)]
 
         q_raw = sb.tile([P, 2, 4, NQ], F32, name="q_raw", tag="q_raw", align_bytes=64)
         nc.sync.dma_start(q_raw[:], qT[0].rearrange("(o p j) w -> p o j w", o=2, j=4))
@@ -62,8 +59,8 @@ def tile_attend_bias_kernel(tc, qT, k_words, k_scales, vT, vs, kb, offs, out):
         nc.vector.memset(kb_pool[0:LIVE, :], 0.0)
         k_sc = sb.tile([P, 2 * N], U8, name="k_sc", align_bytes=64)
         nc.vector.memset(k_sc[:].bitcast(I32), 0)
-        nc.vector.memset(vs_pool[0:LIVE, 0:512], 0.0)
-        nc.gpsimd.memset(vs_pool[0:LIVE, 508:], 0.0)
+        nc.vector.memset(vs_pool[0:LIVE, 0:256], 0.0)
+        nc.gpsimd.memset(vs_pool[0:LIVE, 252:], 0.0)
         ident = sb.tile([P, P], F32, name="ident")
         make_identity(nc, ident[:])
 
@@ -130,18 +127,6 @@ def tile_attend_bias_kernel(tc, qT, k_words, k_scales, vT, vs, kb, offs, out):
 
         v_g0 = shared.tile([P, N], BF16, name="v_g0", offset=4 * CHUNK, align_bytes=64)
         gather(dealt(v_g0[:]), v_raw[0][:], 0, N)
-
-        warm = ps.tile([P, P], F32, tag="e", name="warm")
-        for k in range(5):
-            nc.tensor.matmul_mx(
-                out=warm[:],
-                lhsT=q_codes[:, 0:NQ].bitcast(FP8X4),
-                lhsT_scale=q_sc[:, 0:NQ],
-                rhs=q_codes[:, NQ : 2 * NQ].bitcast(FP8X4),
-                rhs_scale=q_sc[:, NQ : 2 * NQ],
-                start=True,
-                stop=True,
-            )
 
         s_t = [sb.tile([P, 4, NQ], F32, name=f"s_t{g}", align_bytes=64) for g in range(G)]
         for tag, blocks in [("b0", (0, 1)), ("c0", (2, 3)), ("b1", (4, 5)), ("d0", (6,)), ("d1", (7,))]:

@@ -20,6 +20,8 @@ PASS = 512
 G = N // PASS
 CHUNK = 256
 LIVE = P - 1
+KB_SPLIT = 640
+F32_MAX = 3.4028234e38
 
 FLOPS = 2 * NQ * N * (D + DV)
 BYTES = 4 * D * NQ + 4 * P * T + 32 * T + 4 * DV * T + 2 * 4 * T + 2 * N + 4 * NQ * DV
@@ -45,10 +47,10 @@ def tile_attend_bias_kernel(tc, qT, k_words, k_scales, vT, vs, kb, offs, out):
         ks_pool = sb.tile([P, T], U8, name="ks_pool", align_bytes=64)
         nc.sync.dma_start(ks_pool[96:P, :].bitcast(I32), k_scales.bitcast(I32).rearrange("o r w -> r o w"))
         nc.vector.memset(ks_pool[0:96, :].bitcast(I32), 0)
-        kb_pool = sb.tile([P, T], F32, name="kb_pool")
-        nc.scalar.dma_start(kb_pool[LIVE:P, :], kb[0:1, :])
-        vs_pool = shared.tile([P, T], F32, name="vs_pool", offset=0, align_bytes=64)
+        vs_pool = sb.tile([P, T], F32, name="vs_pool")
         nc.scalar.dma_start(vs_pool[LIVE:P, :], vs[0:1, :])
+        kb_pool = shared.tile([P, T], F32, name="kb_pool", offset=0, align_bytes=64)
+        nc.scalar.dma_start(kb_pool[LIVE:P, :], kb[0:1, :])
         v_raw = [sb.tile([P, T], F32, name=f"v_raw{h}", tag=f"v_raw{h}", align_bytes=64) for h in range(2)]
 
         q_raw = sb.tile([P, 2, 4, NQ], F32, name="q_raw", tag="q_raw", align_bytes=64)
@@ -56,11 +58,11 @@ def tile_attend_bias_kernel(tc, qT, k_words, k_scales, vT, vs, kb, offs, out):
         kw_pool = sb.tile([P, T], I32, name="kw_pool")
         nc.sync.dma_start(kw_pool[:], k_words[0].rearrange("p t b -> p (t b)").bitcast(I32))
 
-        nc.vector.memset(kb_pool[0:LIVE, :], 0.0)
+        nc.vector.memset(vs_pool[0:LIVE, :], 0.0)
         k_sc = sb.tile([P, 2 * N], U8, name="k_sc", align_bytes=64)
         nc.vector.memset(k_sc[:].bitcast(I32), 0)
-        nc.vector.memset(vs_pool[0:LIVE, 0:256], 0.0)
-        nc.gpsimd.memset(vs_pool[0:LIVE, 252:], 0.0)
+        nc.vector.memset(kb_pool[0:LIVE, 0:KB_SPLIT], 0.0)
+        nc.gpsimd.memset(kb_pool[0:LIVE, KB_SPLIT - 4 :], 0.0)
         ident = sb.tile([P, P], F32, name="ident")
         make_identity(nc, ident[:])
 
@@ -75,27 +77,33 @@ def tile_attend_bias_kernel(tc, qT, k_words, k_scales, vT, vs, kb, offs, out):
             )
         for h in range(2):
             nc.sync.dma_start(v_raw[h][:], vT[h * P : (h + 1) * P, :])
+        vs_g1 = sb.tile([P, PASS], F32, name="vs_g1")
+        gather(vs_g1[:], vs_pool[:], PASS, PASS)
         kb_g = sb.tile([P, N], F32, name="kb_g")
         gather(kb_g[:], kb_pool[:], 0, N)
-        vs_g = sb.tile([P, N], F32, name="vs_g")
-        gather(vs_g[:], vs_pool[:], 0, N)
 
-        kb_col = [sb.tile([P, 4], F32, name=f"kb_col{g}") for g in range(G)]
+        kb_col = [
+            sb.tile([P, 4], F32, name="kb_col0"),
+            sb.tile([P, 4], F32, name="kb_col1", tag="kb_col1", align_bytes=64),
+        ]
         for g in range(G):
             turned = bank(f"a{g}", f"kb_turned{g}")
             for b in range(4):
                 c0 = g * PASS + b * P
                 nc.tensor.transpose(turned[:, b, :], kb_g[:, c0 : c0 + P], ident[:])
-            nc.scalar.copy(kb_col[g][:], turned[:, :, LIVE])
+            nc.scalar.activation(kb_col[g][:], turned[:, :, LIVE], ACT.Copy, scale=-1.0)
 
-        vs_dealt = sb.tile([P, N], F32, name="vs_dealt")
-        nc.scalar.copy(
-            vs_dealt[:].rearrange("p (b m u i) -> p b m u i", m=8, u=2, i=2),
-            vs_g[:].rearrange("p (b u m i) -> p b m u i", u=2, m=8, i=2),
-        )
         vs_col = [sb.tile([P, 4], F32, name=f"vs_col{g}") for g in range(G)]
-        for g in range(G):
-            nc.sync.dma_start(vs_col[g][:], vs_dealt[LIVE:P, g * PASS : (g + 1) * PASS])
+
+        def deal_scales(g, gathered, tag):
+            row = sb.tile([P, PASS], F32, name=f"vs_dealt{g}", tag=tag, align_bytes=64)
+            nc.scalar.copy(
+                row[:].rearrange("p (b m u i) -> p b m u i", m=8, u=2, i=2),
+                gathered[:].rearrange("p (b u m i) -> p b m u i", u=2, m=8, i=2),
+            )
+            nc.sync.dma_start(vs_col[g][:], row[LIVE:P, :])
+
+        deal_scales(1, vs_g1, "q_raw")
 
         chunks = N // CHUNK
         kw_g = [
@@ -111,7 +119,7 @@ def tile_attend_bias_kernel(tc, qT, k_words, k_scales, vT, vs, kb, offs, out):
                 k_codes[c][:].bitcast(U16), kw_g[c].bitcast(U16).rearrange("p (n o) -> p o n", o=2)
             )
 
-        q_codes = shared.tile([P, 2 * NQ], U32, name="q_codes", offset=4 * N, align_bytes=64)
+        q_codes = shared.tile([P, 2 * NQ], U32, name="q_codes", offset=6 * N, align_bytes=64)
         q_sc = sb.tile([P, 2 * NQ], U8, name="q_sc", align_bytes=64)
         nc.vector.quantize_mx(
             out=q_codes[:].bitcast(FP8X4), scales=q_sc[:], in_=q_bf[:].rearrange("p o w j -> p (o w j)")
@@ -121,11 +129,13 @@ def tile_attend_bias_kernel(tc, qT, k_words, k_scales, vT, vs, kb, offs, out):
             gather_words(c)
             part_words(c - 1)
         part_words(chunks - 1)
+        vs_g0 = shared.tile([P, PASS], F32, name="vs_g0", offset=4 * CHUNK, align_bytes=64)
+        gather(vs_g0[:], vs_pool[:], 0, PASS)
 
         def dealt(tile):
             return tile.rearrange("p (u b x) -> p b u x", u=2, x=16)
 
-        v_g0 = shared.tile([P, N], BF16, name="v_g0", offset=4 * CHUNK, align_bytes=64)
+        v_g0 = shared.tile([P, N], BF16, name="v_g0", offset=12 * CHUNK, align_bytes=64)
         gather(dealt(v_g0[:]), v_raw[0][:], 0, N)
 
         s_t = [sb.tile([P, 4, NQ], F32, name=f"s_t{g}", align_bytes=64) for g in range(G)]
@@ -146,25 +156,41 @@ def tile_attend_bias_kernel(tc, qT, k_words, k_scales, vT, vs, kb, offs, out):
                     )
             for blk in blocks:
                 g, j = divmod(blk, 4)
-                nc.scalar.activation(s_t[g][:, j, :], raw[:, blk % 2, :], ACT.Identity, bias=kb_col[g][:, j : j + 1])
+                nc.scalar.activation(
+                    s_t[g][:, j, :], raw[:, blk % 2, :], ACT.Identity, bias=kb_col[g][:, j : j + 1], scale=-1.0
+                )
 
-        neg_m0_slot = late.tile([P, N // 2 + 32], F32, name="neg_m0_slot", offset=0, align_bytes=64)
-        neg_m = [neg_m0_slot[:, 0:1], sb.tile([P, 1], F32, name="neg_m1", tag="neg_m1", align_bytes=64)[:]]
-        neg_s1 = sb.tile([P, PASS], F32, name="neg_s1")
-        scores = []
-        for g in range(G):
-            turned = bank(f"a{g}", f"scores{g}")
-            for b in range(4):
-                nc.tensor.transpose(turned[:, b, :], s_t[g][:, b, :], ident[:])
-            scores.append(turned[:].rearrange("q b c -> q (b c)"))
-        nc.vector.tensor_reduce(neg_m[0], scores[0], mybir.AxisListType.X, ALU.max, negate=True)
-        nc.vector.tensor_scalar(neg_s1[:], scores[1], -1.0, neg_m[0], ALU.mult, ALU.min, accum_out=neg_m[1])
+        deal_scales(0, vs_g0, "kb_col1")
 
-        v_il = [
-            [sb.tile([P, P, 4], BF16, name=f"v_il{h}{g}", tag=f"v_il{h}{g}", align_bytes=64) for g in range(G)]
-            for h in range(2)
-        ]
-        v_il[0][1] = sb.tile([P, P, 4], BF16, name="v_il01_late", tag="neg_m1", align_bytes=64)
+        m_slot = late.tile([P, N // 2 + 32], F32, name="m_slot", offset=0, align_bytes=64)
+        m_part = [sb.tile([P, 1], F32, name="m_part0")[:], m_slot[:, 0:1]]
+        neg_m = sb.tile([P, 1], F32, name="neg_m", tag="neg_m", align_bytes=64)
+        neg_s0 = sb.tile([P, PASS], F32, name="neg_s0")
+        floor_s1 = sb.tile([P, PASS], F32, name="floor_s1")
+        halves = []
+        for j, tag in enumerate(["a0", "e"]):
+            turned = bank(tag, f"scores0{j}")
+            for b in range(2):
+                nc.tensor.transpose(turned[:, b, :], s_t[0][:, 2 * j + b, :], ident[:])
+            halves.append(turned[:, 0:2, :].rearrange("q b c -> q (b c)"))
+        turned = bank("a1", "scores1")
+        for b in range(4):
+            nc.tensor.transpose(turned[:, b, :], s_t[1][:, b, :], ident[:])
+        neg_s1 = turned[:].rearrange("q b c -> q (b c)")
+        for j in range(2):
+            nc.vector.tensor_scalar(
+                neg_s0[:, j * 2 * P : (j + 1) * 2 * P], halves[j], 1.0, F32_MAX, ALU.mult, ALU.min, accum_out=m_part[j]
+            )
+        nc.vector.tensor_scalar(floor_s1[:], neg_s1, m_part[0], m_part[1], ALU.min, ALU.min, accum_out=neg_m[:])
+        neg_s = [neg_s0[:], neg_s1]
+
+        first, second = 1, 0
+        v_il = {
+            (0, first): sb.tile([P, P, 4], BF16, name="v_il_early", align_bytes=64),
+            (0, second): sb.tile([P, P, 4], BF16, name="v_il_late", tag="neg_m", align_bytes=64),
+            (1, first): sb.tile([P, P, 4], BF16, name="v_il1a", align_bytes=64),
+            (1, second): sb.tile([P, P, 4], BF16, name="v_il1b", align_bytes=64),
+        }
 
         def turn_values(words, tag, name):
             turned = bank(tag, name)
@@ -175,36 +201,40 @@ def tile_attend_bias_kernel(tc, qT, k_words, k_scales, vT, vs, kb, offs, out):
         def copy_values(dst, turned):
             nc.scalar.copy(dst[:].bitcast(F32), turned[:, 0:2, :].rearrange("p u e -> p e u"))
 
-        v_turned0 = [
-            turn_values(
+        v_turned0 = {
+            g: turn_values(
                 [v_g0[:, u * PASS + g * 256 : u * PASS + (g + 1) * 256].bitcast(F32) for u in range(2)],
-                f"d{g}",
+                tag,
                 f"v_turned0{g}",
             )
-            for g in range(G)
-        ]
-        copy_values(v_il[0][0], v_turned0[0])
+            for g, tag in [(first, "d0"), (second, "d1")]
+        }
+        copy_values(v_il[0, first], v_turned0[first])
 
         p_sb = sb.tile([P, G, 4, P], F32, name="p_sb")
         l_part = sb.tile([P, 2 * G], F32, name="l_part")
-        for g in range(G):
+        for g in (first, second):
             for u in range(2):
                 nc.scalar.activation(
                     p_sb[:, g, 2 * u : 2 * u + 2, :].rearrange("q i (b m) -> q b m i", m=8),
-                    [scores[0], neg_s1[:]][g].rearrange("q (b u m i) -> q u b m i", u=2, m=8, i=2)[:, u],
+                    neg_s[g].rearrange("q (b u m i) -> q u b m i", u=2, m=8, i=2)[:, u],
                     ACT.Exp,
-                    bias=neg_m[1],
-                    scale=[1.0, -1.0][g],
+                    bias=neg_m[:],
+                    scale=-1.0,
                     accum_out=l_part[:, 2 * g + u : 2 * g + u + 1],
                 )
 
         v_g1 = late.tile([P, N], BF16, name="v_g1", offset=0, align_bytes=64)
-        for g in range(G):
+        for g in (first, second):
             gather(dealt(v_g1[:, g * PASS : (g + 1) * PASS]), v_raw[1][:], g * PASS, PASS)
 
         v_codes = sb.tile([P, 2, G, P], U32, name="v_codes", align_bytes=64)
-        v_sc = [[sb.tile([P, P], U8, name=f"v_sc{h}{g}", align_bytes=64) for g in range(G)] for h in range(2)]
-        v_sc[0][0] = late.tile([P, P], U8, name="v_sc00_late", offset=2 * N, align_bytes=64)
+        v_sc = {
+            (0, first): late.tile([P, P], U8, name="v_sc_early", offset=2 * N, align_bytes=64),
+            (0, second): sb.tile([P, P], U8, name="v_sc_late", align_bytes=64),
+            (1, first): sb.tile([P, P], U8, name="v_sc1a", align_bytes=64),
+            (1, second): sb.tile([P, P], U8, name="v_sc1b", align_bytes=64),
+        }
         w_il = sb.tile([P, G, NQ, 4], BF16, name="w_il", align_bytes=64)
         w_codes = sb.tile([P, G, NQ], U32, name="w_codes", align_bytes=64)
         w_sc = sb.tile([P, G, NQ], U8, name="w_sc", align_bytes=64)
@@ -213,10 +243,10 @@ def tile_attend_bias_kernel(tc, qT, k_words, k_scales, vT, vs, kb, offs, out):
             nc.vector.quantize_mx(out=codes.bitcast(FP8X4), scales=scales, in_=values.rearrange("p c t -> p (c t)"))
 
         def quantise_values(h, g):
-            quantise(v_codes[:, h, g], v_sc[h][g][:], v_il[h][g][:])
+            quantise(v_codes[:, h, g], v_sc[h, g][:], v_il[h, g][:])
 
-        def weigh(g):
-            turned = bank(["b0", "c0"][g], f"p_turned{g}")
+        def weigh(g, tag):
+            turned = bank(tag, f"p_turned{g}")
             for t in range(4):
                 nc.tensor.transpose(turned[:, t, :], p_sb[:, g, t, :], ident[:])
             nc.vector.tensor_tensor(
@@ -226,37 +256,37 @@ def tile_attend_bias_kernel(tc, qT, k_words, k_scales, vT, vs, kb, offs, out):
                 ALU.mult,
             )
 
-        def second_half(g):
+        def second_half(g, tag):
             words = v_g1[:, g * PASS : (g + 1) * PASS].bitcast(F32)
-            turned = turn_values([words[:, u * P : (u + 1) * P] for u in range(2)], ["a0", "d1"][g], f"v_turned1{g}")
-            copy_values(v_il[1][g], turned)
+            turned = turn_values([words[:, u * P : (u + 1) * P] for u in range(2)], tag, f"v_turned1{g}")
+            copy_values(v_il[1, g], turned)
 
-        quantise_values(0, 0)
-        copy_values(v_il[0][1], v_turned0[1])
-        weigh(0)
-        second_half(0)
-        quantise_values(0, 1)
-        weigh(1)
+        quantise_values(0, first)
+        copy_values(v_il[0, second], v_turned0[second])
+        weigh(first, "b0")
+        second_half(first, "a1")
+        quantise_values(0, second)
+        weigh(second, "c0")
         l_sum = sb.tile([P, 1], F32, name="l_sum")
         nc.scalar.activation(l_part[:], l_part[:], ACT.Identity, accum_out=l_sum[:])
-        second_half(1)
-        for g in range(G):
+        second_half(second, "d1")
+        for g in (first, second):
             quantise(w_codes[:, g], w_sc[:, g], w_il[:, g])
             quantise_values(1, g)
         l_inv = sb.tile([P, 1], F32, name="l_inv")
         nc.vector.reciprocal(l_inv[:], l_sum[:])
 
-        y_ps = [ps.tile([P, P], F32, tag=["e", "a1"][h], name=f"y_ps{h}") for h in range(2)]
-        for g in range(G):
+        y_ps = [ps.tile([P, P], F32, tag=["e", "b1"][h], name=f"y_ps{h}") for h in range(2)]
+        for g in (first, second):
             for h in range(2):
                 nc.tensor.matmul_mx(
                     out=y_ps[h][:],
                     lhsT=w_codes[:, g, :].bitcast(FP8X4),
                     lhsT_scale=w_sc[:, g, :],
                     rhs=v_codes[:, h, g, :].bitcast(FP8X4),
-                    rhs_scale=v_sc[h][g][:],
-                    start=(g == 0),
-                    stop=(g == G - 1),
+                    rhs_scale=v_sc[h, g][:],
+                    start=(g == first),
+                    stop=(g == second),
                 )
         y_sb = [sb.tile([P, P], F32, name=f"y_sb{h}") for h in range(2)]
         nc.scalar.activation(y_sb[0][:], y_ps[0][:], ACT.Copy, scale=l_inv[:])

@@ -71,7 +71,7 @@ def tile_attend_bias_kernel(tc, qT, k_words, k_scales, vT, vs, kb, offs, out):
 
         ks_g = sb.tile([P, N], U8, name="ks_g", align_bytes=64)
         gather(ks_g[:], ks_pool[:], 0, N)
-        for quad in range(4):
+        for quad in (0, 2, 1, 3):
             nc.sync.dma_start(
                 k_sc[32 * quad : 32 * quad + 4, :].bitcast(I32), ks_g[96 + 8 * quad : 104 + 8 * quad, :].bitcast(I32)
             )
@@ -79,8 +79,9 @@ def tile_attend_bias_kernel(tc, qT, k_words, k_scales, vT, vs, kb, offs, out):
             nc.sync.dma_start(v_raw[h][:], vT[h * P : (h + 1) * P, :])
         vs_g1 = sb.tile([P, PASS], F32, name="vs_g1")
         gather(vs_g1[:], vs_pool[:], PASS, PASS)
-        kb_g = sb.tile([P, N], F32, name="kb_g")
-        gather(kb_g[:], kb_pool[:], 0, N)
+        kb_g = [sb.tile([P, PASS], F32, name=f"kb_g{g}") for g in range(G)]
+        for g in range(G):
+            gather(kb_g[g][:], kb_pool[:], g * PASS, PASS)
 
         kb_col = [
             sb.tile([P, 4], F32, name="kb_col0"),
@@ -89,48 +90,49 @@ def tile_attend_bias_kernel(tc, qT, k_words, k_scales, vT, vs, kb, offs, out):
         for g in range(G):
             turned = bank(f"a{g}", f"kb_turned{g}")
             for b in range(4):
-                c0 = g * PASS + b * P
-                nc.tensor.transpose(turned[:, b, :], kb_g[:, c0 : c0 + P], ident[:])
+                nc.tensor.transpose(turned[:, b, :], kb_g[g][:, b * P : (b + 1) * P], ident[:])
             nc.scalar.activation(kb_col[g][:], turned[:, :, LIVE], ACT.Copy, scale=-1.0)
 
         vs_col = [sb.tile([P, 4], F32, name=f"vs_col{g}") for g in range(G)]
 
-        def deal_scales(g, gathered, tag):
-            row = sb.tile([P, PASS], F32, name=f"vs_dealt{g}", tag=tag, align_bytes=64)
+        def deal_scales(dealt_row, gathered):
             nc.scalar.copy(
-                row[:].rearrange("p (b m u i) -> p b m u i", m=8, u=2, i=2),
-                gathered[:].rearrange("p (b u m i) -> p b m u i", u=2, m=8, i=2),
+                dealt_row.rearrange("p (b m u i) -> p b m u i", m=8, u=2, i=2),
+                gathered.rearrange("p (b u m i) -> p b m u i", u=2, m=8, i=2),
             )
-            nc.sync.dma_start(vs_col[g][:], row[LIVE:P, :])
 
-        deal_scales(1, vs_g1, "q_raw")
+        vs_dealt1 = sb.tile([P, PASS], F32, name="vs_dealt1", tag="q_raw", align_bytes=64)
+        deal_scales(vs_dealt1[:], vs_g1[:])
+        nc.sync.dma_start(vs_col[1][:], vs_dealt1[LIVE:P, :])
 
         chunks = N // CHUNK
         kw_g = [
             shared.tile([P, CHUNK], I32, name=f"kw_g{c}", offset=4 * CHUNK * c, align_bytes=64)[:] for c in range(chunks)
         ]
-        k_codes = [sb.tile([P, 2, 2 * CHUNK], U8, name=f"k_codes{c}", align_bytes=64) for c in range(chunks)]
+        k_codes = [sb.tile([P, 2, 2 * P], U8, name=f"k_codes{blk}", align_bytes=64) for blk in range(N // P)]
 
         def gather_words(c):
             gather(kw_g[c].bitcast(U32), kw_pool[:].bitcast(U32), c * CHUNK, CHUNK)
 
-        def part_words(c):
-            nc.vector.tensor_copy(
-                k_codes[c][:].bitcast(U16), kw_g[c].bitcast(U16).rearrange("p (n o) -> p o n", o=2)
-            )
+        def part_words(blk):
+            c, b = divmod(blk, CHUNK // P)
+            words = kw_g[c][:, b * P : (b + 1) * P]
+            nc.vector.tensor_copy(k_codes[blk][:].bitcast(U16), words.bitcast(U16).rearrange("p (n o) -> p o n", o=2))
 
         q_codes = shared.tile([P, 2 * NQ], U32, name="q_codes", offset=6 * N, align_bytes=64)
         q_sc = sb.tile([P, 2 * NQ], U8, name="q_sc", align_bytes=64)
+        gather_words(0)
         nc.vector.quantize_mx(
             out=q_codes[:].bitcast(FP8X4), scales=q_sc[:], in_=q_bf[:].rearrange("p o w j -> p (o w j)")
         )
-        gather_words(0)
+        part_words(0)
         for c in range(1, chunks):
             gather_words(c)
-            part_words(c - 1)
-        part_words(chunks - 1)
-        vs_g0 = shared.tile([P, PASS], F32, name="vs_g0", offset=4 * CHUNK, align_bytes=64)
-        gather(vs_g0[:], vs_pool[:], 0, PASS)
+            part_words(2 * c - 1)
+            part_words(2 * c)
+        part_words(2 * chunks - 1)
+        vs_g0a = shared.tile([P, CHUNK], F32, name="vs_g0a", offset=8 * CHUNK, align_bytes=64)
+        gather(vs_g0a[:], vs_pool[:], 0, CHUNK)
 
         def dealt(tile):
             return tile.rearrange("p (u b x) -> p b u x", u=2, x=16)
@@ -138,16 +140,15 @@ def tile_attend_bias_kernel(tc, qT, k_words, k_scales, vT, vs, kb, offs, out):
         v_g0 = shared.tile([P, N], BF16, name="v_g0", offset=12 * CHUNK, align_bytes=64)
         gather(dealt(v_g0[:]), v_raw[0][:], 0, N)
 
-        s_t = [sb.tile([P, 4, NQ], F32, name=f"s_t{g}", align_bytes=64) for g in range(G)]
+        s_t = [sb.tile([P, 4, NQ], F32, name=f"s_t{g}", tag=f"s_t{g}", align_bytes=64) for g in range(G)]
         for tag, blocks in [("b0", (0, 1)), ("c0", (2, 3)), ("b1", (4, 5)), ("d0", (6,)), ("d1", (7,))]:
             raw = bank(tag, f"raw_{tag}")
             for blk in blocks:
-                c, b = divmod(blk, CHUNK // P)
                 c0 = blk * P
                 for o in range(2):
                     nc.tensor.matmul_mx(
-                        out=raw[:, b, :],
-                        lhsT=k_codes[c][:, o, 2 * b * P : 2 * (b + 1) * P].bitcast(FP4X4),
+                        out=raw[:, blk % 2, :],
+                        lhsT=k_codes[blk][:, o, :].bitcast(FP4X4),
                         lhsT_scale=k_sc[:, o * N + c0 : o * N + c0 + P],
                         rhs=q_codes[:, o * NQ : (o + 1) * NQ].bitcast(FP8X4),
                         rhs_scale=q_sc[:, o * NQ : (o + 1) * NQ],
@@ -160,7 +161,8 @@ def tile_attend_bias_kernel(tc, qT, k_words, k_scales, vT, vs, kb, offs, out):
                     s_t[g][:, j, :], raw[:, blk % 2, :], ACT.Identity, bias=kb_col[g][:, j : j + 1], scale=-1.0
                 )
 
-        deal_scales(0, vs_g0, "kb_col1")
+        vs_dealt0 = sb.tile([P, PASS], F32, name="vs_dealt0", tag="kb_col1", align_bytes=64)
+        deal_scales(vs_dealt0[:, 0:CHUNK], vs_g0a[:])
 
         m_slot = late.tile([P, N // 2 + 32], F32, name="m_slot", offset=0, align_bytes=64)
         m_part = [sb.tile([P, 1], F32, name="m_part0")[:], m_slot[:, 0:1]]
@@ -181,6 +183,10 @@ def tile_attend_bias_kernel(tc, qT, k_words, k_scales, vT, vs, kb, offs, out):
             nc.vector.tensor_scalar(
                 neg_s0[:, j * 2 * P : (j + 1) * 2 * P], halves[j], 1.0, F32_MAX, ALU.mult, ALU.min, accum_out=m_part[j]
             )
+        vs_g0b = sb.tile([P, CHUNK], F32, name="vs_g0b", tag="s_t0", align_bytes=64)
+        gather(vs_g0b[:], vs_pool[:], CHUNK, CHUNK)
+        deal_scales(vs_dealt0[:, CHUNK:PASS], vs_g0b[:])
+        nc.sync.dma_start(vs_col[0][:], vs_dealt0[LIVE:P, :])
         nc.vector.tensor_scalar(floor_s1[:], neg_s1, m_part[0], m_part[1], ALU.min, ALU.min, accum_out=neg_m[:])
         neg_s = [neg_s0[:], neg_s1]
 

@@ -13,6 +13,7 @@ FP8X4 = mybir.dt.float8_e4m3fn_x4
 FP4X4 = mybir.dt.float4_e2m1fn_x4
 ACT = mybir.ActivationFunctionType
 ALU = mybir.AluOpType
+AXIS = mybir.AxisListType
 
 P = 128
 N, T, D, DV, NQ = 1024, 2048, 1024, 256, 128
@@ -20,8 +21,7 @@ PASS = 512
 G = N // PASS
 CHUNK = 256
 LIVE = P - 1
-KB_SPLIT = 640
-F32_MAX = 3.4028234e38
+KIB = 1024
 
 FLOPS = 2 * NQ * N * (D + DV)
 BYTES = 4 * D * NQ + 4 * P * T + 32 * T + 4 * DV * T + 2 * 4 * T + 2 * N + 4 * NQ * DV
@@ -32,7 +32,6 @@ def tile_attend_bias_kernel(tc, qT, k_words, k_scales, vT, vs, kb, offs, out):
     with ExitStack() as ctx:
         sb = ctx.enter_context(tc.tile_pool(name="sb", bufs=1))
         shared = ctx.enter_context(tc.tile_pool(name="shared", bufs=1))
-        late = ctx.enter_context(tc.tile_pool(name="late", bufs=1))
         ps = ctx.enter_context(tc.psum_pool(name="ps", bufs=1))
 
         def bank(tag, name):
@@ -41,258 +40,233 @@ def tile_attend_bias_kernel(tc, qT, k_words, k_scales, vT, vs, kb, offs, out):
         offsets = sb.tile([P, N // 16], U16, name="offsets")
         nc.sync.dma_start(offsets[:], offs)
 
-        def gather(dst, window, start, count):
-            nc.vector.tensor_copy(dst, window.indirect(offsets[:, start // 16 : (start + count) // 16]))
+        def listed(window, start, count):
+            return window.indirect(offsets[:, start // 16 : (start + count) // 16])
 
         ks_pool = sb.tile([P, T], U8, name="ks_pool", align_bytes=64)
         nc.sync.dma_start(ks_pool[96:P, :].bitcast(I32), k_scales.bitcast(I32).rearrange("o r w -> r o w"))
         nc.vector.memset(ks_pool[0:96, :].bitcast(I32), 0)
-        vs_pool = sb.tile([P, T], F32, name="vs_pool")
-        nc.scalar.dma_start(vs_pool[LIVE:P, :], vs[0:1, :])
-        kb_pool = shared.tile([P, T], F32, name="kb_pool", offset=0, align_bytes=64)
+        kb_pool = sb.tile([P, T], F32, name="kb_pool", tag="kb_pool", align_bytes=64)
         nc.scalar.dma_start(kb_pool[LIVE:P, :], kb[0:1, :])
-        v_raw = [sb.tile([P, T], F32, name=f"v_raw{h}", tag=f"v_raw{h}", align_bytes=64) for h in range(2)]
 
-        q_raw = sb.tile([P, 2, 4, NQ], F32, name="q_raw", tag="q_raw", align_bytes=64)
+        q_raw = shared.tile([P, 2, 4, NQ], F32, name="q_raw", offset=7 * KIB, align_bytes=64)
         nc.sync.dma_start(q_raw[:], qT[0].rearrange("(o p j) w -> p o j w", o=2, j=4))
         kw_pool = sb.tile([P, T], I32, name="kw_pool")
         nc.sync.dma_start(kw_pool[:], k_words[0].rearrange("p t b -> p (t b)").bitcast(I32))
 
-        nc.vector.memset(vs_pool[0:LIVE, :], 0.0)
+        ident_bf = sb.tile([P, P], BF16, name="ident_bf", tag="ident_bf", align_bytes=64)
+        make_identity(nc, ident_bf[:])
+        ident = sb.tile([P, P], F32, name="ident")
+        nc.scalar.activation(ident[:], ident_bf[:], ACT.Copy)
+        nc.vector.memset(kb_pool[0:LIVE, :], 0.0)
         k_sc = sb.tile([P, 2 * N], U8, name="k_sc", align_bytes=64)
         nc.vector.memset(k_sc[:].bitcast(I32), 0)
-        nc.vector.memset(kb_pool[0:LIVE, 0:KB_SPLIT], 0.0)
-        nc.gpsimd.memset(kb_pool[0:LIVE, KB_SPLIT - 4 :], 0.0)
-        ident = sb.tile([P, P], F32, name="ident")
-        make_identity(nc, ident[:])
-
-        q_bf = sb.tile([P, 2, NQ, 4], BF16, name="q_bf", align_bytes=64)
-        nc.scalar.activation(q_bf[:], q_raw[:].rearrange("p o j w -> p o w j"), ACT.Copy)
 
         ks_g = sb.tile([P, N], U8, name="ks_g", align_bytes=64)
-        gather(ks_g[:], ks_pool[:], 0, N)
+        nc.vector.tensor_copy(ks_g[:], listed(ks_pool[:], 0, N))
         for quad in (0, 2, 1, 3):
             nc.sync.dma_start(
                 k_sc[32 * quad : 32 * quad + 4, :].bitcast(I32), ks_g[96 + 8 * quad : 104 + 8 * quad, :].bitcast(I32)
             )
-        for h in range(2):
-            nc.sync.dma_start(v_raw[h][:], vT[h * P : (h + 1) * P, :])
-        vs_g1 = sb.tile([P, PASS], F32, name="vs_g1")
-        gather(vs_g1[:], vs_pool[:], PASS, PASS)
-        kb_g = [sb.tile([P, PASS], F32, name=f"kb_g{g}") for g in range(G)]
-        for g in range(G):
-            gather(kb_g[g][:], kb_pool[:], g * PASS, PASS)
 
-        kb_col = [
-            sb.tile([P, 4], F32, name="kb_col0"),
-            sb.tile([P, 4], F32, name="kb_col1", tag="kb_col1", align_bytes=64),
-        ]
+        q_bf = sb.tile([P, 2, NQ, 4], BF16, name="q_bf", tag="q_bf", align_bytes=64)
+        nc.vector.tensor_copy(
+            q_bf[:].rearrange("p o (c i) j -> p o c j i", i=4), q_raw[:].rearrange("p o j (c i) -> p o c j i", i=4)
+        )
+        vs_pool = shared.tile([P, T], F32, name="vs_pool", offset=0, align_bytes=64)
+        nc.vector.memset(vs_pool[0:LIVE, :], 0.0)
+        nc.sync.dma_start(vs_pool[LIVE:P, :], vs[0:1, :])
+        v_raw0 = shared.tile([P, T], F32, name="v_raw0", offset=10 * KIB, align_bytes=64)
+        nc.sync.dma_start(v_raw0[:], vT[0:P, :])
+
+        kb_g = sb.tile([P, N], F32, name="kb_g", tag="ident_bf", align_bytes=64)
+        for g in range(G):
+            nc.scalar.activation(kb_g[:, g * PASS : (g + 1) * PASS], listed(kb_pool[:], g * PASS, PASS), ACT.Copy)
+        kb_col = [sb.tile([P, 4], F32, name=f"kb_col{g}", tag=f"kb_col{g}", align_bytes=64) for g in range(G)]
         for g in range(G):
             turned = bank(f"a{g}", f"kb_turned{g}")
             for b in range(4):
-                nc.tensor.transpose(turned[:, b, :], kb_g[g][:, b * P : (b + 1) * P], ident[:])
-            nc.scalar.activation(kb_col[g][:], turned[:, :, LIVE], ACT.Copy, scale=-1.0)
-
-        vs_col = [sb.tile([P, 4], F32, name=f"vs_col{g}") for g in range(G)]
-
-        def deal_scales(dealt_row, gathered):
-            nc.scalar.copy(
-                dealt_row.rearrange("p (b m u i) -> p b m u i", m=8, u=2, i=2),
-                gathered.rearrange("p (b u m i) -> p b m u i", u=2, m=8, i=2),
+                nc.tensor.transpose(turned[:, b, :], kb_g[:, g * PASS + b * P : g * PASS + (b + 1) * P], ident[:])
+            nc.scalar.activation(kb_col[g][:], turned[:, :, LIVE], ACT.Copy)
+        neg_kb = [sb.tile([P, 4, P], F32, name=f"neg_kb{g}") for g in range(G)]
+        for g in range(G):
+            spread = bank(f"b{g}", f"kb_spread{g}")
+            for b in range(4):
+                nc.tensor.transpose(spread[:, b, :], kb_col[g][:, b : b + 1].to_broadcast([P, P]), ident[:])
+            nc.scalar.activation(
+                neg_kb[g][:], spread[:].rearrange("q b (m t) -> q t (b m)", t=4), ACT.Copy, scale=-1.0
             )
 
-        vs_dealt1 = sb.tile([P, PASS], F32, name="vs_dealt1", tag="q_raw", align_bytes=64)
-        deal_scales(vs_dealt1[:], vs_g1[:])
-        nc.sync.dma_start(vs_col[1][:], vs_dealt1[LIVE:P, :])
-
-        chunks = N // CHUNK
-        kw_g = [
-            shared.tile([P, CHUNK], I32, name=f"kw_g{c}", offset=4 * CHUNK * c, align_bytes=64)[:] for c in range(chunks)
-        ]
-        k_codes = [sb.tile([P, 2, 2 * P], U8, name=f"k_codes{blk}", align_bytes=64) for blk in range(N // P)]
-
-        def gather_words(c):
-            gather(kw_g[c].bitcast(U32), kw_pool[:].bitcast(U32), c * CHUNK, CHUNK)
-
-        def part_words(blk):
-            c, b = divmod(blk, CHUNK // P)
-            words = kw_g[c][:, b * P : (b + 1) * P]
-            nc.vector.tensor_copy(k_codes[blk][:].bitcast(U16), words.bitcast(U16).rearrange("p (n o) -> p o n", o=2))
-
-        q_codes = shared.tile([P, 2 * NQ], U32, name="q_codes", offset=6 * N, align_bytes=64)
+        q_codes = sb.tile([P, 2 * NQ], U32, name="q_codes", align_bytes=64)
         q_sc = sb.tile([P, 2 * NQ], U8, name="q_sc", align_bytes=64)
-        gather_words(0)
         nc.vector.quantize_mx(
             out=q_codes[:].bitcast(FP8X4), scales=q_sc[:], in_=q_bf[:].rearrange("p o w j -> p (o w j)")
         )
-        part_words(0)
+        v_raw1 = sb.tile([P, T], F32, name="v_raw1", tag="q_bf", align_bytes=64)
+        nc.sync.dma_start(v_raw1[:], vT[P : 2 * P, :])
+
+        chunks = N // CHUNK
+        kw_g = [
+            shared.tile([P, CHUNK], I32, name=f"kw_g{c}", offset=(8 + c % 2) * KIB, align_bytes=64)
+            for c in range(chunks)
+        ]
+        k_codes = [sb.tile([P, 2, 2 * CHUNK], U8, name=f"k_codes{c}", align_bytes=64) for c in range(chunks)]
+
+        def gather_words(c):
+            nc.vector.tensor_copy(kw_g[c][:].bitcast(U32), listed(kw_pool[:].bitcast(U32), c * CHUNK, CHUNK))
+
+        def part_words(c):
+            nc.vector.tensor_copy(
+                k_codes[c][:].bitcast(U16), kw_g[c][:].bitcast(U16).rearrange("p (n o) -> p o n", o=2)
+            )
+
+        gather_words(0)
         for c in range(1, chunks):
             gather_words(c)
-            part_words(2 * c - 1)
-            part_words(2 * c)
-        part_words(2 * chunks - 1)
-        vs_g0a = shared.tile([P, CHUNK], F32, name="vs_g0a", offset=8 * CHUNK, align_bytes=64)
-        gather(vs_g0a[:], vs_pool[:], 0, CHUNK)
+            part_words(c - 1)
+        part_words(chunks - 1)
 
-        def dealt(tile):
-            return tile.rearrange("p (u b x) -> p b u x", u=2, x=16)
-
-        v_g0 = shared.tile([P, N], BF16, name="v_g0", offset=12 * CHUNK, align_bytes=64)
-        gather(dealt(v_g0[:]), v_raw[0][:], 0, N)
-
-        s_t = [sb.tile([P, 4, NQ], F32, name=f"s_t{g}", tag=f"s_t{g}", align_bytes=64) for g in range(G)]
-        for tag, blocks in [("b0", (0, 1)), ("c0", (2, 3)), ("b1", (4, 5)), ("d0", (6,)), ("d1", (7,))]:
-            raw = bank(tag, f"raw_{tag}")
-            for blk in blocks:
-                c0 = blk * P
-                for o in range(2):
-                    nc.tensor.matmul_mx(
-                        out=raw[:, blk % 2, :],
-                        lhsT=k_codes[blk][:, o, :].bitcast(FP4X4),
-                        lhsT_scale=k_sc[:, o * N + c0 : o * N + c0 + P],
-                        rhs=q_codes[:, o * NQ : (o + 1) * NQ].bitcast(FP8X4),
-                        rhs_scale=q_sc[:, o * NQ : (o + 1) * NQ],
-                        start=(o == 0),
-                        stop=(o == 1),
-                    )
-            for blk in blocks:
-                g, j = divmod(blk, 4)
-                nc.scalar.activation(
-                    s_t[g][:, j, :], raw[:, blk % 2, :], ACT.Identity, bias=kb_col[g][:, j : j + 1], scale=-1.0
+        raw01 = ps.tile([P, PASS], F32, tag="a1", name="raw01")
+        raw2 = ps.tile([P, CHUNK], F32, tag="b0", name="raw2")
+        raw3 = ps.tile([P, CHUNK], F32, tag="b1", name="raw3")
+        raw = [raw01[:, 0:CHUNK], raw01[:, CHUNK:PASS], raw2[:], raw3[:]]
+        for c in range(chunks):
+            for o in range(2):
+                nc.tensor.matmul_mx(
+                    out=raw[c],
+                    lhsT=q_codes[:, o * NQ : (o + 1) * NQ].bitcast(FP8X4),
+                    lhsT_scale=q_sc[:, o * NQ : (o + 1) * NQ],
+                    rhs=k_codes[c][:, o, :].bitcast(FP4X4),
+                    rhs_scale=k_sc[:, o * N + c * CHUNK : o * N + (c + 1) * CHUNK],
+                    start=(o == 0),
+                    stop=(o == 1),
                 )
 
-        vs_dealt0 = sb.tile([P, PASS], F32, name="vs_dealt0", tag="kb_col1", align_bytes=64)
-        deal_scales(vs_dealt0[:, 0:CHUNK], vs_g0a[:])
+        vs_g = sb.tile([P, N], F32, name="vs_g", tag="kb_col1", align_bytes=64)
+        nc.scalar.activation(vs_g[:], listed(vs_pool[:], 0, N), ACT.Copy)
+        vs_col = [sb.tile([P, 4], F32, name=f"vs_col{g}") for g in range(G)]
+        for g in range(G):
+            nc.sync.dma_start(vs_col[g][:], vs_g[LIVE:P, g * PASS : (g + 1) * PASS])
 
-        m_slot = late.tile([P, N // 2 + 32], F32, name="m_slot", offset=0, align_bytes=64)
-        m_part = [sb.tile([P, 1], F32, name="m_part0")[:], m_slot[:, 0:1]]
-        neg_m = sb.tile([P, 1], F32, name="neg_m", tag="neg_m", align_bytes=64)
-        neg_s0 = sb.tile([P, PASS], F32, name="neg_s0")
-        floor_s1 = sb.tile([P, PASS], F32, name="floor_s1")
-        halves = []
-        for j, tag in enumerate(["a0", "e"]):
-            turned = bank(tag, f"scores0{j}")
-            for b in range(2):
-                nc.tensor.transpose(turned[:, b, :], s_t[0][:, 2 * j + b, :], ident[:])
-            halves.append(turned[:, 0:2, :].rearrange("q b c -> q (b c)"))
-        turned = bank("a1", "scores1")
-        for b in range(4):
-            nc.tensor.transpose(turned[:, b, :], s_t[1][:, b, :], ident[:])
-        neg_s1 = turned[:].rearrange("q b c -> q (b c)")
-        for j in range(2):
-            nc.vector.tensor_scalar(
-                neg_s0[:, j * 2 * P : (j + 1) * 2 * P], halves[j], 1.0, F32_MAX, ALU.mult, ALU.min, accum_out=m_part[j]
-            )
-        vs_g0b = sb.tile([P, CHUNK], F32, name="vs_g0b", tag="s_t0", align_bytes=64)
-        gather(vs_g0b[:], vs_pool[:], CHUNK, CHUNK)
-        deal_scales(vs_dealt0[:, CHUNK:PASS], vs_g0b[:])
-        nc.sync.dma_start(vs_col[0][:], vs_dealt0[LIVE:P, :])
-        nc.vector.tensor_scalar(floor_s1[:], neg_s1, m_part[0], m_part[1], ALU.min, ALU.min, accum_out=neg_m[:])
-        neg_s = [neg_s0[:], neg_s1]
+        v_g0 = shared.tile([P, N], BF16, name="v_g0", offset=0, align_bytes=64)
+        for g in range(G):
+            nc.scalar.activation(v_g0[:, g * PASS : (g + 1) * PASS], listed(v_raw0[:], g * PASS, PASS), ACT.Copy)
 
-        first, second = 1, 0
-        v_il = {
-            (0, first): sb.tile([P, P, 4], BF16, name="v_il_early", align_bytes=64),
-            (0, second): sb.tile([P, P, 4], BF16, name="v_il_late", tag="neg_m", align_bytes=64),
-            (1, first): sb.tile([P, P, 4], BF16, name="v_il1a", align_bytes=64),
-            (1, second): sb.tile([P, P, 4], BF16, name="v_il1b", align_bytes=64),
-        }
-
-        def turn_values(words, tag, name):
-            turned = bank(tag, name)
+        def turn_values(turned, gathered):
+            words = gathered.bitcast(F32)
             for u in range(2):
-                nc.tensor.transpose(turned[:, u, :], words[u], ident[:])
-            return turned
+                nc.tensor.transpose(turned[:, u, :], words[:, u : PASS // 2 : 2], ident[:])
 
         def copy_values(dst, turned):
-            nc.scalar.copy(dst[:].bitcast(F32), turned[:, 0:2, :].rearrange("p u e -> p e u"))
+            nc.scalar.copy(dst[:].bitcast(F32), turned[:].rearrange("p u e -> p e u"))
 
-        v_turned0 = {
-            g: turn_values(
-                [v_g0[:, u * PASS + g * 256 : u * PASS + (g + 1) * 256].bitcast(F32) for u in range(2)],
-                tag,
-                f"v_turned0{g}",
+        neg_s = [sb.tile([P, 4, P], F32, name=f"neg_s{g}", tag=f"neg_s{g}", align_bytes=64) for g in range(G)]
+        half = P // 2
+
+        def add_bias(g, lo, hi, scores):
+            nc.vector.tensor_tensor(
+                neg_s[g][:, :, lo:hi], neg_kb[g][:, :, lo:hi], scores.rearrange("q (m t) -> q t m", t=4), ALU.subtract
             )
-            for g, tag in [(first, "d0"), (second, "d1")]
-        }
-        copy_values(v_il[0, first], v_turned0[first])
 
-        p_sb = sb.tile([P, G, 4, P], F32, name="p_sb")
+        m01 = sb.tile([P, 1], F32, name="m01", tag="m01", align_bytes=64)
+        m2 = sb.tile([P, 1], F32, name="m2", tag="late", align_bytes=64)
+        neg_m = sb.tile([P, 1], F32, name="neg_m")
+        floor3 = sb.tile([P, 4, half], F32, name="floor3")
+        add_bias(0, 0, P, raw01[:])
+        add_bias(1, 0, half, raw2[:])
+        nc.vector.tensor_reduce(m01[:], neg_s[0][:].rearrange("q t m -> q (t m)"), AXIS.X, ALU.min)
+        add_bias(1, half, P, raw3[:])
+        nc.vector.tensor_reduce(m2[:], neg_s[1][:, :, 0:half], AXIS.XY, ALU.min)
+        nc.vector.tensor_scalar(
+            floor3[:], neg_s[1][:, :, half:P], m01[:], m2[:], ALU.min, ALU.min, accum_out=neg_m[:]
+        )
+
+        v_turned0 = [ps.tile([P, 2, P], F32, tag=["b0", "a1"][g], name=f"v_turned0{g}") for g in range(G)]
+        for g in range(G):
+            turn_values(v_turned0[g][:], v_g0[:, g * PASS : (g + 1) * PASS])
+        v_il = {(0, 0): sb.tile([P, P, 4], BF16, name="v_il00", align_bytes=64)}
+        copy_values(v_il[0, 0], v_turned0[0])
+
+        p_sb = shared.tile([P, G, 4, P], F32, name="p_sb", offset=12 * KIB, align_bytes=64)
         l_part = sb.tile([P, 2 * G], F32, name="l_part")
-        for g in (first, second):
+        for g in range(G):
             for u in range(2):
                 nc.scalar.activation(
-                    p_sb[:, g, 2 * u : 2 * u + 2, :].rearrange("q i (b m) -> q b m i", m=8),
-                    neg_s[g].rearrange("q (b u m i) -> q u b m i", u=2, m=8, i=2)[:, u],
+                    p_sb[:, g, 2 * u : 2 * u + 2, :],
+                    neg_s[g][:, 2 * u : 2 * u + 2, :],
                     ACT.Exp,
                     bias=neg_m[:],
                     scale=-1.0,
                     accum_out=l_part[:, 2 * g + u : 2 * g + u + 1],
                 )
 
-        v_g1 = late.tile([P, N], BF16, name="v_g1", offset=0, align_bytes=64)
-        for g in (first, second):
-            gather(dealt(v_g1[:, g * PASS : (g + 1) * PASS]), v_raw[1][:], g * PASS, PASS)
+        v_g1 = sb.tile([P, N], BF16, name="v_g1", tag="late", align_bytes=64)
+        for g in range(G):
+            nc.vector.tensor_copy(v_g1[:, g * PASS : (g + 1) * PASS], listed(v_raw1[:], g * PASS, PASS))
 
-        v_codes = sb.tile([P, 2, G, P], U32, name="v_codes", align_bytes=64)
-        v_sc = {
-            (0, first): late.tile([P, P], U8, name="v_sc_early", offset=2 * N, align_bytes=64),
-            (0, second): sb.tile([P, P], U8, name="v_sc_late", align_bytes=64),
-            (1, first): sb.tile([P, P], U8, name="v_sc1a", align_bytes=64),
-            (1, second): sb.tile([P, P], U8, name="v_sc1b", align_bytes=64),
+        v_il[0, 1] = sb.tile([P, P, 4], BF16, name="v_il01", tag="neg_s1", align_bytes=64)
+        for g in range(G):
+            v_il[1, g] = sb.tile([P, P, 4], BF16, name=f"v_il1{g}", align_bytes=64)
+        v_codes = {
+            (h, g): sb.tile([P, P], U32, name=f"v_codes{h}{g}", align_bytes=64) for h in range(2) for g in range(G)
         }
-        w_il = sb.tile([P, G, NQ, 4], BF16, name="w_il", align_bytes=64)
-        w_codes = sb.tile([P, G, NQ], U32, name="w_codes", align_bytes=64)
-        w_sc = sb.tile([P, G, NQ], U8, name="w_sc", align_bytes=64)
+        v_sc = {(0, 0): sb.tile([P, P], U8, name="v_sc00", tag="m01", align_bytes=64)}
+        for h, g in [(0, 1), (1, 0), (1, 1)]:
+            v_sc[h, g] = sb.tile([P, P], U8, name=f"v_sc{h}{g}", align_bytes=64)
+        w_il = [sb.tile([P, NQ, 4], BF16, name=f"w_il{g}", align_bytes=64) for g in range(G)]
+        w_codes = [sb.tile([P, NQ], U32, name=f"w_codes{g}", align_bytes=64) for g in range(G)]
+        w_sc = [sb.tile([P, NQ], U8, name=f"w_sc{g}", align_bytes=64) for g in range(G)]
 
         def quantise(codes, scales, values):
-            nc.vector.quantize_mx(out=codes.bitcast(FP8X4), scales=scales, in_=values.rearrange("p c t -> p (c t)"))
+            nc.vector.quantize_mx(
+                out=codes[:].bitcast(FP8X4), scales=scales[:], in_=values[:].rearrange("p c t -> p (c t)")
+            )
 
-        def quantise_values(h, g):
-            quantise(v_codes[:, h, g], v_sc[h, g][:], v_il[h, g][:])
-
-        def weigh(g, tag):
-            turned = bank(tag, f"p_turned{g}")
+        def weigh(g):
+            turned = bank(["a0", "c"][g], f"p_turned{g}")
             for t in range(4):
                 nc.tensor.transpose(turned[:, t, :], p_sb[:, g, t, :], ident[:])
             nc.vector.tensor_tensor(
-                w_il[:, g],
+                w_il[g][:],
                 turned[:].rearrange("p t q -> p q t"),
                 vs_col[g][:].unsqueeze(1).to_broadcast([P, NQ, 4]),
                 ALU.mult,
             )
 
-        def second_half(g, tag):
-            words = v_g1[:, g * PASS : (g + 1) * PASS].bitcast(F32)
-            turned = turn_values([words[:, u * P : (u + 1) * P] for u in range(2)], tag, f"v_turned1{g}")
+        def second_half(g):
+            turned = ps.tile([P, 2, P], F32, tag=["d", "e"][g], name=f"v_turned1{g}")
+            turn_values(turned[:], v_g1[:, g * PASS : (g + 1) * PASS])
             copy_values(v_il[1, g], turned)
 
-        quantise_values(0, first)
-        copy_values(v_il[0, second], v_turned0[second])
-        weigh(first, "b0")
-        second_half(first, "a1")
-        quantise_values(0, second)
-        weigh(second, "c0")
+        def quantise_values(h, g):
+            quantise(v_codes[h, g], v_sc[h, g], v_il[h, g])
+
+        quantise_values(0, 0)
+        copy_values(v_il[0, 1], v_turned0[1])
+        weigh(0)
+        second_half(0)
+        quantise_values(0, 1)
+        weigh(1)
+        second_half(1)
         l_sum = sb.tile([P, 1], F32, name="l_sum")
         nc.scalar.activation(l_part[:], l_part[:], ACT.Identity, accum_out=l_sum[:])
-        second_half(second, "d1")
-        for g in (first, second):
-            quantise(w_codes[:, g], w_sc[:, g], w_il[:, g])
+        for g in range(G):
+            quantise(w_codes[g], w_sc[g], w_il[g])
             quantise_values(1, g)
         l_inv = sb.tile([P, 1], F32, name="l_inv")
         nc.vector.reciprocal(l_inv[:], l_sum[:])
 
-        y_ps = [ps.tile([P, P], F32, tag=["e", "b1"][h], name=f"y_ps{h}") for h in range(2)]
-        for g in (first, second):
+        y_ps = [ps.tile([P, P], F32, tag=["f", "b1"][h], name=f"y_ps{h}") for h in range(2)]
+        for g in range(G):
             for h in range(2):
                 nc.tensor.matmul_mx(
                     out=y_ps[h][:],
-                    lhsT=w_codes[:, g, :].bitcast(FP8X4),
-                    lhsT_scale=w_sc[:, g, :],
-                    rhs=v_codes[:, h, g, :].bitcast(FP8X4),
+                    lhsT=w_codes[g][:].bitcast(FP8X4),
+                    lhsT_scale=w_sc[g][:],
+                    rhs=v_codes[h, g][:].bitcast(FP8X4),
                     rhs_scale=v_sc[h, g][:],
-                    start=(g == first),
-                    stop=(g == second),
+                    start=(g == 0),
+                    stop=(g == G - 1),
                 )
         y_sb = [sb.tile([P, P], F32, name=f"y_sb{h}") for h in range(2)]
         nc.scalar.activation(y_sb[0][:], y_ps[0][:], ACT.Copy, scale=l_inv[:])

@@ -160,7 +160,10 @@ def tile_attend_bias_kernel(tc, qT, k_words, k_scales, vT, vs, kb, offs, out):
         def copy_values(dst, turned):
             nc.scalar.copy(dst[:].bitcast(F32), turned[:].rearrange("p u e -> p e u"))
 
-        neg_s = [sb.tile([P, 4, P], F32, name=f"neg_s{g}", tag=f"neg_s{g}", align_bytes=64) for g in range(G)]
+        neg_s = [
+            sb.tile([P, 4, P], F32, name="neg_s0"),
+            shared.tile([P, 4, P], F32, name="neg_s1", offset=20 * KIB + KIB // 2, align_bytes=64),
+        ]
         half = P // 2
 
         def add_bias(g, lo, hi, scores):
@@ -204,7 +207,7 @@ def tile_attend_bias_kernel(tc, qT, k_words, k_scales, vT, vs, kb, offs, out):
         for g in range(G):
             nc.vector.tensor_copy(v_g1[:, g * PASS : (g + 1) * PASS], listed(v_raw1[:], g * PASS, PASS))
 
-        v_il[0, 1] = sb.tile([P, P, 4], BF16, name="v_il01", tag="neg_s1", align_bytes=64)
+        v_il[0, 1] = shared.tile([P, P, 4], BF16, name="v_il01", offset=22 * KIB, align_bytes=64)
         for g in range(G):
             v_il[1, g] = sb.tile([P, P, 4], BF16, name=f"v_il1{g}", align_bytes=64)
         v_codes = {
@@ -235,24 +238,36 @@ def tile_attend_bias_kernel(tc, qT, k_words, k_scales, vT, vs, kb, offs, out):
 
         def second_half(g):
             turned = ps.tile([P, 2, P], F32, tag=["d", "e"][g], name=f"v_turned1{g}")
-            turn_values(turned[:], v_g1[:, g * PASS : (g + 1) * PASS])
+            for u in range(2):
+                nc.tensor.transpose(turned[:, u, :], v_words1[g][:, u, :], ident[:])
             copy_values(v_il[1, g], turned)
 
         def quantise_values(h, g):
             quantise(v_codes[h, g], v_sc[h, g], v_il[h, g])
 
+        v_words1 = [
+            shared.tile([P, 2, P], F32, name=f"v_words1{g}", offset=(20 + g) * KIB, align_bytes=64) for g in range(G)
+        ]
+
+        def deal_words(g):
+            words = v_g1[:, g * PASS : (g + 1) * PASS].bitcast(F32)
+            nc.scalar.copy(v_words1[g][:], words.rearrange("e (w u) -> e u w", u=2))
+
         quantise_values(0, 0)
+        deal_words(0)
         copy_values(v_il[0, 1], v_turned0[1])
+        deal_words(1)
         weigh(0)
-        second_half(0)
         quantise_values(0, 1)
+        quantise(w_codes[0], w_sc[0], w_il[0])
         weigh(1)
+        second_half(0)
         second_half(1)
         l_sum = sb.tile([P, 1], F32, name="l_sum")
         nc.scalar.activation(l_part[:], l_part[:], ACT.Identity, accum_out=l_sum[:])
-        for g in range(G):
-            quantise(w_codes[g], w_sc[g], w_il[g])
-            quantise_values(1, g)
+        quantise_values(1, 0)
+        quantise(w_codes[1], w_sc[1], w_il[1])
+        quantise_values(1, 1)
         l_inv = sb.tile([P, 1], F32, name="l_inv")
         nc.vector.reciprocal(l_inv[:], l_sum[:])
 

@@ -210,14 +210,17 @@ def tile_attend_bias_kernel(tc, qT, k_words, k_scales, vT, vs, kb, offs, out):
         v_il[0, 1] = shared.tile([P, P, 4], BF16, name="v_il01", offset=22 * KIB, align_bytes=64)
         for g in range(G):
             v_il[1, g] = sb.tile([P, P, 4], BF16, name=f"v_il1{g}", align_bytes=64)
-        v_codes = {
-            (h, g): sb.tile([P, P], U32, name=f"v_codes{h}{g}", align_bytes=64) for h in range(2) for g in range(G)
-        }
+        v_codes = {(0, 1): shared.tile([P, P], U32, name="v_codes01", offset=13 * KIB, align_bytes=64)}
+        for h, g in [(0, 0), (1, 0), (1, 1)]:
+            v_codes[h, g] = sb.tile([P, P], U32, name=f"v_codes{h}{g}", align_bytes=64)
         v_sc = {(0, 0): sb.tile([P, P], U8, name="v_sc00", tag="m01", align_bytes=64)}
         for h, g in [(0, 1), (1, 0), (1, 1)]:
             v_sc[h, g] = sb.tile([P, P], U8, name=f"v_sc{h}{g}", align_bytes=64)
         w_il = [sb.tile([P, NQ, 4], BF16, name=f"w_il{g}", align_bytes=64) for g in range(G)]
-        w_codes = [sb.tile([P, NQ], U32, name=f"w_codes{g}", align_bytes=64) for g in range(G)]
+        w_codes = [
+            shared.tile([P, NQ], U32, name="w_codes0", offset=12 * KIB, align_bytes=64),
+            sb.tile([P, NQ], U32, name="w_codes1", align_bytes=64),
+        ]
         w_sc = [sb.tile([P, NQ], U8, name=f"w_sc{g}", align_bytes=64) for g in range(G)]
 
         def quantise(codes, scales, values):
@@ -255,18 +258,18 @@ def tile_attend_bias_kernel(tc, qT, k_words, k_scales, vT, vs, kb, offs, out):
 
         quantise_values(0, 0)
         deal_words(0)
-        copy_values(v_il[0, 1], v_turned0[1])
         deal_words(1)
+        copy_values(v_il[0, 1], v_turned0[1])
         weigh(0)
-        quantise_values(0, 1)
-        quantise(w_codes[0], w_sc[0], w_il[0])
         weigh(1)
+        quantise(w_codes[0], w_sc[0], w_il[0])
+        quantise_values(0, 1)
         second_half(0)
         second_half(1)
         l_sum = sb.tile([P, 1], F32, name="l_sum")
         nc.scalar.activation(l_part[:], l_part[:], ACT.Identity, accum_out=l_sum[:])
-        quantise_values(1, 0)
         quantise(w_codes[1], w_sc[1], w_il[1])
+        quantise_values(1, 0)
         quantise_values(1, 1)
         l_inv = sb.tile([P, 1], F32, name="l_inv")
         nc.vector.reciprocal(l_inv[:], l_sum[:])

@@ -43,15 +43,15 @@ def tile_attend_bias_kernel(tc, qT, k_words, k_scales, vT, vs, kb, offs, out):
         def listed(window, start, count):
             return window.indirect(offsets[:, start // 16 : (start + count) // 16])
 
-        ks_pool = sb.tile([P, T], U8, name="ks_pool", align_bytes=64)
+        ks_pool = sb.tile([P, T], U8, name="ks_pool", align_bytes=256)
         nc.sync.dma_start(ks_pool[96:P, :].bitcast(I32), k_scales.bitcast(I32).rearrange("o r w -> r o w"))
         nc.vector.memset(ks_pool[0:96, :].bitcast(I32), 0)
-        kb_pool = sb.tile([P, T], F32, name="kb_pool", tag="kb_pool", align_bytes=64)
+        kb_pool = sb.tile([P, T], F32, name="kb_pool", tag="kb_pool", align_bytes=256)
         nc.scalar.dma_start(kb_pool[LIVE:P, :], kb[0:1, :])
 
-        q_raw = shared.tile([P, 2, 4, NQ], F32, name="q_raw", offset=7 * KIB, align_bytes=64)
+        q_raw = shared.tile([P, 2, 4, NQ], F32, name="q_raw", offset=7 * KIB, align_bytes=256)
         nc.sync.dma_start(q_raw[:], qT[0].rearrange("(o p j) w -> p o j w", o=2, j=4))
-        kw_pool = sb.tile([P, T], I32, name="kw_pool")
+        kw_pool = sb.tile([P, T], I32, name="kw_pool", align_bytes=256)
         nc.sync.dma_start(kw_pool[:], k_words[0].rearrange("p t b -> p (t b)").bitcast(I32))
 
         ident_bf = sb.tile([P, P], BF16, name="ident_bf", tag="ident_bf", align_bytes=64)
@@ -69,14 +69,14 @@ def tile_attend_bias_kernel(tc, qT, k_words, k_scales, vT, vs, kb, offs, out):
                 k_sc[32 * quad : 32 * quad + 4, :].bitcast(I32), ks_g[96 + 8 * quad : 104 + 8 * quad, :].bitcast(I32)
             )
 
-        q_bf = sb.tile([P, 2, NQ, 4], BF16, name="q_bf", tag="q_bf", align_bytes=64)
+        q_bf = sb.tile([P, 2, NQ, 4], BF16, name="q_bf", tag="q_bf", align_bytes=256)
         nc.vector.tensor_copy(
             q_bf[:].rearrange("p o (c i) j -> p o c j i", i=4), q_raw[:].rearrange("p o j (c i) -> p o c j i", i=4)
         )
-        vs_pool = shared.tile([P, T], F32, name="vs_pool", offset=0, align_bytes=64)
+        vs_pool = shared.tile([P, T], F32, name="vs_pool", offset=0, align_bytes=256)
         nc.vector.memset(vs_pool[0:LIVE, :], 0.0)
         nc.sync.dma_start(vs_pool[LIVE:P, :], vs[0:1, :])
-        v_raw0 = shared.tile([P, T], F32, name="v_raw0", offset=10 * KIB, align_bytes=64)
+        v_raw0 = shared.tile([P, T], F32, name="v_raw0", offset=10 * KIB, align_bytes=256)
         nc.sync.dma_start(v_raw0[:], vT[0:P, :])
 
         kb_g = sb.tile([P, N], F32, name="kb_g", tag="ident_bf", align_bytes=64)
@@ -102,12 +102,12 @@ def tile_attend_bias_kernel(tc, qT, k_words, k_scales, vT, vs, kb, offs, out):
         nc.vector.quantize_mx(
             out=q_codes[:].bitcast(FP8X4), scales=q_sc[:], in_=q_bf[:].rearrange("p o w j -> p (o w j)")
         )
-        v_raw1 = sb.tile([P, T], F32, name="v_raw1", tag="q_bf", align_bytes=64)
+        v_raw1 = sb.tile([P, T], F32, name="v_raw1", tag="q_bf", align_bytes=256)
         nc.sync.dma_start(v_raw1[:], vT[P : 2 * P, :])
 
         chunks = N // CHUNK
         kw_g = [
-            shared.tile([P, CHUNK], I32, name=f"kw_g{c}", offset=(8 + c % 2) * KIB, align_bytes=64)
+            shared.tile([P, CHUNK], I32, name=f"kw_g{c}", offset=(8 + c % 2) * KIB, align_bytes=256)
             for c in range(chunks)
         ]
         k_codes = [sb.tile([P, 2, 2 * CHUNK], U8, name=f"k_codes{c}", align_bytes=64) for c in range(chunks)]
@@ -148,7 +148,7 @@ def tile_attend_bias_kernel(tc, qT, k_words, k_scales, vT, vs, kb, offs, out):
         for g in range(G):
             nc.sync.dma_start(vs_col[g][:], vs_g[LIVE:P, g * PASS : (g + 1) * PASS])
 
-        v_g0 = shared.tile([P, N], BF16, name="v_g0", offset=0, align_bytes=64)
+        v_g0 = shared.tile([P, N], BF16, name="v_g0", offset=0, align_bytes=256)
         for g in range(G):
             nc.scalar.activation(v_g0[:, g * PASS : (g + 1) * PASS], listed(v_raw0[:], g * PASS, PASS), ACT.Copy)
 
@@ -162,7 +162,7 @@ def tile_attend_bias_kernel(tc, qT, k_words, k_scales, vT, vs, kb, offs, out):
 
         neg_s = [
             sb.tile([P, 4, P], F32, name="neg_s0"),
-            shared.tile([P, 4, P], F32, name="neg_s1", offset=20 * KIB + KIB // 2, align_bytes=64),
+            shared.tile([P, 4, P], F32, name="neg_s1", offset=20 * KIB + KIB // 2, align_bytes=256),
         ]
         half = P // 2
 
@@ -190,7 +190,7 @@ def tile_attend_bias_kernel(tc, qT, k_words, k_scales, vT, vs, kb, offs, out):
         v_il = {(0, 0): sb.tile([P, P, 4], BF16, name="v_il00", align_bytes=64)}
         copy_values(v_il[0, 0], v_turned0[0])
 
-        p_sb = shared.tile([P, G, 4, P], F32, name="p_sb", offset=12 * KIB, align_bytes=64)
+        p_sb = shared.tile([P, G, 4, P], F32, name="p_sb", offset=12 * KIB, align_bytes=256)
         l_part = sb.tile([P, 2 * G], F32, name="l_part")
         for g in range(G):
             for u in range(2):
@@ -207,10 +207,10 @@ def tile_attend_bias_kernel(tc, qT, k_words, k_scales, vT, vs, kb, offs, out):
         for g in range(G):
             nc.vector.tensor_copy(v_g1[:, g * PASS : (g + 1) * PASS], listed(v_raw1[:], g * PASS, PASS))
 
-        v_il[0, 1] = shared.tile([P, P, 4], BF16, name="v_il01", offset=22 * KIB, align_bytes=64)
+        v_il[0, 1] = shared.tile([P, P, 4], BF16, name="v_il01", offset=22 * KIB, align_bytes=256)
         for g in range(G):
             v_il[1, g] = sb.tile([P, P, 4], BF16, name=f"v_il1{g}", align_bytes=64)
-        v_codes = {(0, 1): shared.tile([P, P], U32, name="v_codes01", offset=13 * KIB, align_bytes=64)}
+        v_codes = {(0, 1): shared.tile([P, P], U32, name="v_codes01", offset=13 * KIB, align_bytes=256)}
         for h, g in [(0, 0), (1, 0), (1, 1)]:
             v_codes[h, g] = sb.tile([P, P], U32, name=f"v_codes{h}{g}", align_bytes=64)
         v_sc = {(0, 0): sb.tile([P, P], U8, name="v_sc00", tag="m01", align_bytes=64)}
@@ -218,7 +218,7 @@ def tile_attend_bias_kernel(tc, qT, k_words, k_scales, vT, vs, kb, offs, out):
             v_sc[h, g] = sb.tile([P, P], U8, name=f"v_sc{h}{g}", align_bytes=64)
         w_il = [sb.tile([P, NQ, 4], BF16, name=f"w_il{g}", align_bytes=64) for g in range(G)]
         w_codes = [
-            shared.tile([P, NQ], U32, name="w_codes0", offset=12 * KIB, align_bytes=64),
+            shared.tile([P, NQ], U32, name="w_codes0", offset=12 * KIB, align_bytes=256),
             sb.tile([P, NQ], U32, name="w_codes1", align_bytes=64),
         ]
         w_sc = [sb.tile([P, NQ], U8, name=f"w_sc{g}", align_bytes=64) for g in range(G)]
@@ -249,7 +249,7 @@ def tile_attend_bias_kernel(tc, qT, k_words, k_scales, vT, vs, kb, offs, out):
             quantise(v_codes[h, g], v_sc[h, g], v_il[h, g])
 
         v_words1 = [
-            shared.tile([P, 2, P], F32, name=f"v_words1{g}", offset=(20 + g) * KIB, align_bytes=64) for g in range(G)
+            shared.tile([P, 2, P], F32, name=f"v_words1{g}", offset=(20 + g) * KIB, align_bytes=256) for g in range(G)
         ]
 
         def deal_words(g):

@@ -82,17 +82,17 @@ def tile_attend_bias_kernel(tc, qT, k_words, k_scales, vT, vs, kb, offs, out):
         kb_g = sb.tile([P, N], F32, name="kb_g", tag="ident_bf", align_bytes=64)
         for g in range(G):
             nc.scalar.activation(kb_g[:, g * PASS : (g + 1) * PASS], listed(kb_pool[:], g * PASS, PASS), ACT.Copy)
-        kb_col = [sb.tile([P, 4], F32, name=f"kb_col{g}", tag=f"kb_col{g}", align_bytes=64) for g in range(G)]
+        kb_col = [sb.tile([P, 4, P], F32, name=f"kb_col{g}", tag=f"kb_col{g}", align_bytes=64) for g in range(G)]
         for g in range(G):
             turned = bank(f"a{g}", f"kb_turned{g}")
             for b in range(4):
                 nc.tensor.transpose(turned[:, b, :], kb_g[:, g * PASS + b * P : g * PASS + (b + 1) * P], ident[:])
-            nc.scalar.activation(kb_col[g][:], turned[:, :, LIVE], ACT.Copy)
+            nc.scalar.activation(kb_col[g][:], turned[:, :, LIVE:P].to_broadcast([P, 4, P]), ACT.Copy)
         neg_kb = [sb.tile([P, 4, P], F32, name=f"neg_kb{g}") for g in range(G)]
         for g in range(G):
             spread = bank(f"b{g}", f"kb_spread{g}")
             for b in range(4):
-                nc.tensor.transpose(spread[:, b, :], kb_col[g][:, b : b + 1].to_broadcast([P, P]), ident[:])
+                nc.tensor.transpose(spread[:, b, :], kb_col[g][:, b, :], ident[:])
             nc.scalar.activation(
                 neg_kb[g][:], spread[:].rearrange("q b (m t) -> q t (b m)", t=4), ACT.Copy, scale=-1.0
             )

from contextlib import ExitStack

import concourse.mybir as mybir
from concourse.masks import make_identity

F32 = mybir.dt.float32
BF16 = mybir.dt.bfloat16
I32 = mybir.dt.int32
U32 = mybir.dt.uint32
U16 = mybir.dt.uint16
U8 = mybir.dt.uint8
FP8X4 = mybir.dt.float8_e4m3fn_x4
FP4X4 = mybir.dt.float4_e2m1fn_x4
ACT = mybir.ActivationFunctionType
ALU = mybir.AluOpType
AXIS = mybir.AxisListType

P = 128
N, T, D, DV, NQ = 1024, 2048, 1024, 256, 128
PASS = 512
G = N // PASS
CHUNK = 256
LIVE = P - 1
KIB = 1024

FLOPS = 2 * NQ * N * (D + DV)
BYTES = 4 * D * NQ + 4 * P * T + 32 * T + 4 * DV * T + 2 * 4 * T + 2 * N + 4 * NQ * DV


def tile_attend_bias_kernel(tc, qT, k_words, k_scales, vT, vs, kb, offs, out):
    nc = tc.nc
    with ExitStack() as ctx:
        sb = ctx.enter_context(tc.tile_pool(name="sb", bufs=1))
        shared = ctx.enter_context(tc.tile_pool(name="shared", bufs=1))
        ps = ctx.enter_context(tc.psum_pool(name="ps", bufs=1))

        def bank(tag, name):
            return ps.tile([P, 4, P], F32, tag=tag, name=name)

        offsets = sb.tile([P, N // 16], U16, name="offsets")
        nc.sync.dma_start(offsets[:], offs)

        def listed(window, start, count):
            return window.indirect(offsets[:, start // 16 : (start + count) // 16])

        ks_pool = sb.tile([P, T], U8, name="ks_pool", align_bytes=256)
        nc.sync.dma_start(ks_pool[96:P, :].bitcast(I32), k_scales.bitcast(I32).rearrange("o r w -> r o w"))
        nc.vector.memset(ks_pool[0:96, :].bitcast(I32), 0)
        kb_pool = sb.tile([P, T], F32, name="kb_pool", tag="kb_pool", align_bytes=256)
        nc.scalar.dma_start(kb_pool[LIVE:P, :], kb[0:1, :])

        q_raw = shared.tile([P, 2, 4, NQ], F32, name="q_raw", offset=7 * KIB, align_bytes=256)
        nc.sync.dma_start(q_raw[:], qT[0].rearrange("(o p j) w -> p o j w", o=2, j=4))
        kw_pool = sb.tile([P, T], I32, name="kw_pool", align_bytes=256)
        nc.sync.dma_start(kw_pool[:], k_words[0].rearrange("p t b -> p (t b)").bitcast(I32))

        ident_bf = sb.tile([P, P], BF16, name="ident_bf", tag="ident_bf", align_bytes=64)
        make_identity(nc, ident_bf[:])
        ident = sb.tile([P, P], F32, name="ident")
        nc.scalar.activation(ident[:], ident_bf[:], ACT.Copy)
        nc.vector.memset(kb_pool[0:LIVE, :], 0.0)
        k_sc = sb.tile([P, 2 * N], U8, name="k_sc", align_bytes=64)
        nc.vector.memset(k_sc[:].bitcast(I32), 0)

        ks_g = sb.tile([P, N], U8, name="ks_g", align_bytes=64)
        nc.vector.tensor_copy(ks_g[:], listed(ks_pool[:], 0, N))
        for quad in (0, 2, 1, 3):
            nc.sync.dma_start(
                k_sc[32 * quad : 32 * quad + 4, :].bitcast(I32), ks_g[96 + 8 * quad : 104 + 8 * quad, :].bitcast(I32)
            )

        q_bf = sb.tile([P, 2, NQ, 4], BF16, name="q_bf", tag="q_bf", align_bytes=256)
        nc.vector.tensor_copy(
            q_bf[:].rearrange("p o (c i) j -> p o c j i", i=4), q_raw[:].rearrange("p o j (c i) -> p o c j i", i=4)
        )
        vs_pool = shared.tile([P, T], F32, name="vs_pool", offset=0, align_bytes=256)
        nc.vector.memset(vs_pool[0:LIVE, :], 0.0)
        nc.sync.dma_start(vs_pool[LIVE:P, :], vs[0:1, :])
        v_raw0 = shared.tile([P, T], F32, name="v_raw0", offset=10 * KIB, align_bytes=256)
        nc.sync.dma_start(v_raw0[:], vT[0:P, :])

        kb_g = sb.tile([P, N], F32, name="kb_g", tag="ident_bf", align_bytes=64)
        for g in range(G):
            nc.scalar.activation(kb_g[:, g * PASS : (g + 1) * PASS], listed(kb_pool[:], g * PASS, PASS), ACT.Copy)
        kb_col = [sb.tile([P, 4, P], F32, name=f"kb_col{g}", tag=f"kb_col{g}", align_bytes=64) for g in range(G)]
        for g in range(G):
            turned = bank(f"a{g}", f"kb_turned{g}")
            for b in range(4):
                nc.tensor.transpose(turned[:, b, :], kb_g[:, g * PASS + b * P : g * PASS + (b + 1) * P], ident[:])
            nc.scalar.activation(kb_col[g][:], turned[:, :, LIVE:P].to_broadcast([P, 4, P]), ACT.Copy)
        neg_kb = [sb.tile([P, 4, P], F32, name=f"neg_kb{g}") for g in range(G)]
        for g in range(G):
            spread = bank(f"b{g}", f"kb_spread{g}")
            for b in range(4):
                nc.tensor.transpose(spread[:, b, :], kb_col[g][:, b, :], ident[:])
            nc.scalar.activation(
                neg_kb[g][:], spread[:].rearrange("q b (m t) -> q t (b m)", t=4), ACT.Copy, scale=-1.0
            )

        q_codes = sb.tile([P, 2 * NQ], U32, name="q_codes", align_bytes=64)
        q_sc = sb.tile([P, 2 * NQ], U8, name="q_sc", align_bytes=64)
        nc.vector.quantize_mx(
            out=q_codes[:].bitcast(FP8X4), scales=q_sc[:], in_=q_bf[:].rearrange("p o w j -> p (o w j)")
        )
        v_raw1 = sb.tile([P, T], F32, name="v_raw1", tag="q_bf", align_bytes=256)
        nc.sync.dma_start(v_raw1[:], vT[P : 2 * P, :])

        chunks = N // CHUNK
        kw_g = [
            shared.tile([P, CHUNK], I32, name=f"kw_g{c}", offset=(8 + c % 2) * KIB, align_bytes=256)
            for c in range(chunks)
        ]
        k_codes = [sb.tile([P, 2, 2 * CHUNK], U8, name=f"k_codes{c}", align_bytes=64) for c in range(chunks)]

        def gather_words(c):
            nc.vector.tensor_copy(kw_g[c][:].bitcast(U32), listed(kw_pool[:].bitcast(U32), c * CHUNK, CHUNK))

        def part_words(c):
            nc.vector.tensor_copy(
                k_codes[c][:].bitcast(U16), kw_g[c][:].bitcast(U16).rearrange("p (n o) -> p o n", o=2)
            )

        gather_words(0)
        for c in range(1, chunks):
            gather_words(c)
            part_words(c - 1)
        part_words(chunks - 1)

        raw01 = ps.tile([P, PASS], F32, tag="a1", name="raw01")
        raw2 = ps.tile([P, CHUNK], F32, tag="b0", name="raw2")
        raw3 = ps.tile([P, CHUNK], F32, tag="b1", name="raw3")
        raw = [raw01[:, 0:CHUNK], raw01[:, CHUNK:PASS], raw2[:], raw3[:]]
        for c in range(chunks):
            for o in range(2):
                nc.tensor.matmul_mx(
                    out=raw[c],
                    lhsT=q_codes[:, o * NQ : (o + 1) * NQ].bitcast(FP8X4),
                    lhsT_scale=q_sc[:, o * NQ : (o + 1) * NQ],
                    rhs=k_codes[c][:, o, :].bitcast(FP4X4),
                    rhs_scale=k_sc[:, o * N + c * CHUNK : o * N + (c + 1) * CHUNK],
                    start=(o == 0),
                    stop=(o == 1),
                )

        vs_g = sb.tile([P, N], F32, name="vs_g", tag="kb_col1", align_bytes=64)
        nc.scalar.activation(vs_g[:], listed(vs_pool[:], 0, N), ACT.Copy)
        vs_col = [sb.tile([P, 4], F32, name=f"vs_col{g}") for g in range(G)]
        for g in range(G):
            nc.sync.dma_start(vs_col[g][:], vs_g[LIVE:P, g * PASS : (g + 1) * PASS])

        v_g0 = shared.tile([P, N], BF16, name="v_g0", offset=0, align_bytes=256)
        for g in range(G):
            nc.scalar.activation(v_g0[:, g * PASS : (g + 1) * PASS], listed(v_raw0[:], g * PASS, PASS), ACT.Copy)

        def turn_values(turned, gathered):
            words = gathered.bitcast(F32)
            for u in range(2):
                nc.tensor.transpose(turned[:, u, :], words[:, u : PASS // 2 : 2], ident[:])

        def copy_values(dst, turned):
            nc.scalar.copy(dst[:].bitcast(F32), turned[:].rearrange("p u e -> p e u"))

        neg_s = [
            sb.tile([P, 4, P], F32, name="neg_s0"),
            shared.tile([P, 4, P], F32, name="neg_s1", offset=20 * KIB + KIB // 2, align_bytes=256),
        ]
        half = P // 2

        def add_bias(g, lo, hi, scores):
            nc.vector.tensor_tensor(
                neg_s[g][:, :, lo:hi], neg_kb[g][:, :, lo:hi], scores.rearrange("q (m t) -> q t m", t=4), ALU.subtract
            )

        m01 = sb.tile([P, 1], F32, name="m01", tag="m01", align_bytes=64)
        m2 = sb.tile([P, 1], F32, name="m2", tag="late", align_bytes=64)
        neg_m = sb.tile([P, 1], F32, name="neg_m")
        floor3 = sb.tile([P, 4, half], F32, name="floor3")
        add_bias(0, 0, P, raw01[:])
        add_bias(1, 0, half, raw2[:])
        nc.vector.tensor_reduce(m01[:], neg_s[0][:].rearrange("q t m -> q (t m)"), AXIS.X, ALU.min)
        add_bias(1, half, P, raw3[:])
        nc.vector.tensor_reduce(m2[:], neg_s[1][:, :, 0:half], AXIS.XY, ALU.min)
        nc.vector.tensor_scalar(
            floor3[:], neg_s[1][:, :, half:P], m01[:], m2[:], ALU.min, ALU.min, accum_out=neg_m[:]
        )

        v_turned0 = [ps.tile([P, 2, P], F32, tag=["b0", "a1"][g], name=f"v_turned0{g}") for g in range(G)]
        for g in range(G):
            turn_values(v_turned0[g][:], v_g0[:, g * PASS : (g + 1) * PASS])
        v_il = {(0, 0): sb.tile([P, P, 4], BF16, name="v_il00", align_bytes=64)}
        copy_values(v_il[0, 0], v_turned0[0])

        p_sb = shared.tile([P, G, 4, P], F32, name="p_sb", offset=12 * KIB, align_bytes=256)
        l_part = sb.tile([P, 2 * G], F32, name="l_part")
        for g in range(G):
            for u in range(2):
                nc.scalar.activation(
                    p_sb[:, g, 2 * u : 2 * u + 2, :],
                    neg_s[g][:, 2 * u : 2 * u + 2, :],
                    ACT.Exp,
                    bias=neg_m[:],
                    scale=-1.0,
                    accum_out=l_part[:, 2 * g + u : 2 * g + u + 1],
                )

        v_g1 = sb.tile([P, N], BF16, name="v_g1", tag="late", align_bytes=64)
        for g in range(G):
            nc.vector.tensor_copy(v_g1[:, g * PASS : (g + 1) * PASS], listed(v_raw1[:], g * PASS, PASS))

        v_il[0, 1] = shared.tile([P, P, 4], BF16, name="v_il01", offset=22 * KIB, align_bytes=256)
        for g in range(G):
            v_il[1, g] = sb.tile([P, P, 4], BF16, name=f"v_il1{g}", align_bytes=64)
        v_codes = {(0, 1): shared.tile([P, P], U32, name="v_codes01", offset=13 * KIB, align_bytes=256)}
        for h, g in [(0, 0), (1, 0), (1, 1)]:
            v_codes[h, g] = sb.tile([P, P], U32, name=f"v_codes{h}{g}", align_bytes=64)
        v_sc = {(0, 0): sb.tile([P, P], U8, name="v_sc00", tag="m01", align_bytes=64)}
        for h, g in [(0, 1), (1, 0), (1, 1)]:
            v_sc[h, g] = sb.tile([P, P], U8, name=f"v_sc{h}{g}", align_bytes=64)
        w_il = [sb.tile([P, NQ, 4], BF16, name=f"w_il{g}", align_bytes=64) for g in range(G)]
        w_codes = [
            shared.tile([P, NQ], U32, name="w_codes0", offset=12 * KIB, align_bytes=256),
            sb.tile([P, NQ], U32, name="w_codes1", align_bytes=64),
        ]
        w_sc = [sb.tile([P, NQ], U8, name=f"w_sc{g}", align_bytes=64) for g in range(G)]

        def quantise(codes, scales, values):
            nc.vector.quantize_mx(
                out=codes[:].bitcast(FP8X4), scales=scales[:], in_=values[:].rearrange("p c t -> p (c t)")
            )

        def weigh(g):
            turned = bank(["a0", "c"][g], f"p_turned{g}")
            for t in range(4):
                nc.tensor.transpose(turned[:, t, :], p_sb[:, g, t, :], ident[:])
            nc.vector.tensor_tensor(
                w_il[g][:],
                turned[:].rearrange("p t q -> p q t"),
                vs_col[g][:].unsqueeze(1).to_broadcast([P, NQ, 4]),
                ALU.mult,
            )

        def second_half(g):
            turned = ps.tile([P, 2, P], F32, tag=["d", "e"][g], name=f"v_turned1{g}")
            for u in range(2):
                nc.tensor.transpose(turned[:, u, :], v_words1[g][:, u, :], ident[:])
            copy_values(v_il[1, g], turned)

        def quantise_values(h, g):
            quantise(v_codes[h, g], v_sc[h, g], v_il[h, g])

        v_words1 = [
            shared.tile([P, 2, P], F32, name=f"v_words1{g}", offset=(20 + g) * KIB, align_bytes=256) for g in range(G)
        ]

        def deal_words(g):
            words = v_g1[:, g * PASS : (g + 1) * PASS].bitcast(F32)
            nc.scalar.copy(v_words1[g][:], words.rearrange("e (w u) -> e u w", u=2))

        quantise_values(0, 0)
        deal_words(0)
        deal_words(1)
        copy_values(v_il[0, 1], v_turned0[1])
        weigh(0)
        weigh(1)
        quantise(w_codes[0], w_sc[0], w_il[0])
        quantise_values(0, 1)
        second_half(0)
        second_half(1)
        l_sum = sb.tile([P, 1], F32, name="l_sum")
        nc.scalar.activation(l_part[:], l_part[:], ACT.Identity, accum_out=l_sum[:])
        quantise(w_codes[1], w_sc[1], w_il[1])
        quantise_values(1, 0)
        quantise_values(1, 1)
        l_inv = sb.tile([P, 1], F32, name="l_inv")
        nc.vector.reciprocal(l_inv[:], l_sum[:])

        y_ps = [ps.tile([P, P], F32, tag=["f", "b1"][h], name=f"y_ps{h}") for h in range(2)]
        for g in range(G):
            for h in range(2):
                nc.tensor.matmul_mx(
                    out=y_ps[h][:],
                    lhsT=w_codes[g][:].bitcast(FP8X4),
                    lhsT_scale=w_sc[g][:],
                    rhs=v_codes[h, g][:].bitcast(FP8X4),
                    rhs_scale=v_sc[h, g][:],
                    start=(g == 0),
                    stop=(g == G - 1),
                )
        y_sb = [sb.tile([P, P], F32, name=f"y_sb{h}") for h in range(2)]
        nc.scalar.activation(y_sb[0][:], y_ps[0][:], ACT.Copy, scale=l_inv[:])
        nc.vector.tensor_scalar(y_sb[1][:], y_ps[1][:], l_inv[:], None, ALU.mult)
        for h in range(2):
            nc.sync.dma_start(out[0][:, h * P : (h + 1) * P], y_sb[h][:])
